import numpy as np
import ml_dtypes


def mxq(x, axis, fmt="e4m3"):
    dtype, down = {"e4m3": (ml_dtypes.float8_e4m3fn, 7), "e5m2": (ml_dtypes.float8_e5m2, 14)}[fmt]
    v = np.moveaxis(np.asarray(x, np.float32).astype(ml_dtypes.bfloat16).astype(np.float64), axis, -1)
    blocks = v.reshape(v.shape[:-1] + (-1, 32))
    amax = np.abs(blocks).max(-1, keepdims=True)
    byte = np.maximum(np.where(amax > 0, np.frexp(amax)[1] - 1 + 127, 0) - down, 1)
    scale = np.exp2(byte - 127.0)
    codes = (blocks / scale).astype(np.float32).astype(dtype).astype(np.float64)
    return np.moveaxis((codes * scale).reshape(v.shape), -1, axis)


WIDE = False


def mx_kscale(k):
    if not WIDE:
        return np.ones(k)
    levels = np.array([10, -10, 5, -5, 0])
    if k % 512:
        return np.exp2(np.random.permutation(np.resize(levels, k // 32))).repeat(32)
    a = np.empty((k // 512, 16))
    for p in range(k // 512):
        a[p, :8] = np.random.permutation(np.resize(levels, 8))
        for g in range(8):
            far = levels[np.abs(levels - a[p, g]) >= 10]
            a[p, g + 8] = far[np.random.randint(len(far))]
    return np.exp2(a.ravel()).repeat(32)


def f64(x):
    return np.asarray(x).astype(np.float64)


def striped(idx):
    return np.tile(idx.reshape(-1, 16).T, (8, 1)).astype(np.uint16)


def unstriped(offs):
    return offs[:16].T.reshape(-1).astype(np.int64)


E2M1 = np.array([0.0, 0.5, 1.0, 1.5, 2.0, 3.0, 4.0, 6.0, -0.0, -0.5, -1.0, -1.5, -2.0, -3.0, -4.0, -6.0])


def pack_weight(w, fmt):
    k, n = w.shape
    w = f64(np.asarray(w, np.float32).astype(ml_dtypes.bfloat16)).reshape(k // 32, 32, n)
    amax = np.abs(w).max(1)
    if fmt == "e4m3":
        byte = np.frexp(amax)[1] - 1 + 127 - 7
    else:
        mant, ex = np.frexp(amax / 6.0)
        byte = np.where(mant > 0.5, ex, ex - 1) + 127
    byte = np.clip(np.where(amax > 0, byte, 1), 1, 254)
    scaled = (w * np.exp2(127.0 - byte)[:, None, :]).reshape(k, n).astype(np.float32)
    by_word = np.ascontiguousarray(scaled.reshape(k // 512, 128, 4, n).transpose(0, 1, 3, 2))
    if fmt == "e4m3":
        words = by_word.astype(ml_dtypes.float8_e4m3fn).view(np.uint8)
    else:
        c = by_word.astype(ml_dtypes.float4_e2m1fn).view(np.uint8) & 0xF
        words = (c[..., 0::2] | (c[..., 1::2] << 4)).reshape(k // 512, 128, 2 * n)
    return np.ascontiguousarray(words), np.ascontiguousarray(byte.astype(np.uint8).reshape(k // 512, 16, n))


def unpack_weight(words, scales, fmt):
    g, _, n = scales.shape
    words = np.ascontiguousarray(words).reshape(g, 128, n, -1)
    if fmt == "e4m3":
        vals = words.view(ml_dtypes.float8_e4m3fn).astype(np.float64)
    else:
        nib = np.empty((g, 128, n, 4), np.uint8)
        nib[..., 0::2] = words & 0xF
        nib[..., 1::2] = words >> 4
        vals = E2M1[nib]
    vals = vals * np.repeat(np.exp2(scales.astype(np.float64) - 127.0), 8, axis=1)[..., None]
    return vals.transpose(0, 1, 3, 2).reshape(g * 512, n)


def gelu(v):
    return 0.5 * v * (1.0 + np.tanh(np.sqrt(2.0 / np.pi) * (v + 0.044715 * v**3)))


K, H, T, S, T2, T3, S2, P = 1024, 512, 2048, 512, 1024, 2048, 1024, 512

def setup_inputs():
    n = np.random.standard_normal
    s = mx_kscale(K)[:, None]
    u = mx_kscale(H)[:, None]
    tab_words, tab_scales = pack_weight(n((K, T)) * s, "e4m3")
    tab2_words, tab2_scales = pack_weight(0.5 * n((H, T3)) / np.sqrt(H) / u, "e4m3")
    w4_words, w4_scales = pack_weight(1.5 * n((K, H)) / np.sqrt(K) / s * u.T, "e2m1")
    return {
        "tab_words": tab_words, "tab_scales": tab_scales,
        "offs": striped(np.random.permutation(T)[:S]),
        "w4_words": w4_words, "w4_scales": w4_scales,
        "wg": (1.5 * n((K, H)) / np.sqrt(K) / s).astype(np.float32),
        "page0": (n((H, T2)) * u).astype(np.float32),
        "wgs": np.exp(0.3 * n((128, S))).astype(np.float32),
        "offs3": striped(np.random.permutation(T2)[:S]),
        "tab2_words": tab2_words, "tab2_scales": tab2_scales,
        "offs2": striped(np.random.permutation(T3)[:S2]),
        "offs4": striped(np.random.permutation(T2)[:P]),
        "bid": np.exp(0.3 * n(S2)).astype(np.float32),
        "reserve": np.random.uniform(0.2, 0.6, (S2, P)).astype(np.float32),
    }

def reference(tab_words, tab_scales, offs, w4_words, w4_scales, wg, page0, wgs, offs3,
              tab2_words, tab2_scales, offs2, offs4, bid, reserve):
    v = unpack_weight(tab_words, tab_scales, "e4m3")[:, unstriped(offs)]
    v2 = unpack_weight(tab2_words, tab2_scales, "e4m3")[:, unstriped(offs2)]
    w4 = unpack_weight(w4_words, w4_scales, "e2m1")
    a = w4.T @ v
    b = mxq(f64(wg), 0, "e4m3").T @ v
    h = a * (1.0 / (1.0 + np.exp(-b)))
    page = f64(page0).copy()
    page[:, unstriped(offs3)] = np.tile(f64(wgs), (H // 128, 1)) * h
    e = v2.T @ mxq(page, 0, "e4m3")
    x = e[:, unstriped(offs4)]
    return np.exp(x) * f64(bid)[:, None] - f64(reserve)

@@ -1,0 +1,196 @@
+from contextlib import ExitStack
+
+import concourse.mybir as mybir
+
+K, H, T, S, T2, T3, S2, PICKS = 1024, 512, 2048, 512, 1024, 2048, 1024, 512
+FLOPS = 2 * (2 * K * H * S + H * S2 * T2)
+
+F32 = mybir.dt.float32
+BF16 = mybir.dt.bfloat16
+I32 = mybir.dt.int32
+U32 = mybir.dt.uint32
+U16 = mybir.dt.uint16
+U8 = mybir.dt.uint8
+FP8X4 = mybir.dt.float8_e4m3fn_x4
+FP4X4 = mybir.dt.float4_e2m1fn_x4
+ACT = mybir.ActivationFunctionType
+ALU = mybir.AluOpType
+
+P = 128
+PACK = 4
+PASSES = K // (P * PACK)
+BANK = 512
+QUADS = 4
+
+
+def load_scale_rows(queue, plane, scales):
+    passes = scales.shape[0]
+    for q in range(QUADS):
+        queue.dma_start(
+            out=plane[32 * q : 32 * q + 4, :].bitcast(I32).rearrange("r (a n) -> r a n", a=passes),
+            in_=scales[:, 4 * q : 4 * q + 4, :].bitcast(I32).rearrange("a r n -> r a n"),
+        )
+
+
+def tile_list_auction_slot_scores_kernel(
+    tc, tab_words, tab_scales, offs, w4_words, w4_scales, wg, page0, wgs, offs3,
+    tab2_words, tab2_scales, offs2, offs4, bid, reserve, out,
+):
+    nc = tc.nc
+    with ExitStack() as ctx:
+        keep = ctx.enter_context(tc.tile_pool(name="keep", bufs=1))
+        ring = ctx.enter_context(tc.tile_pool(name="ring", bufs=3))
+        psum = ctx.enter_context(tc.psum_pool(name="psum", bufs=8))
+
+        idx = keep.tile([P, S // 16], U16, name="idx")
+        idx2 = keep.tile([P, S2 // 16], U16, name="idx2")
+        idx3 = keep.tile([P, S // 16], U16, name="idx3")
+        idx4 = keep.tile([P, PICKS // 16], U16, name="idx4")
+
+        tab_plane = keep.tile([P, PASSES * T], U8, name="tab_plane", align_bytes=64)
+        w4_plane = keep.tile([P, PASSES * H], U8, name="w4_plane", align_bytes=64)
+        tab2_plane = keep.tile([P, T3], U8, name="tab2_plane", align_bytes=64)
+        nc.vector.memset(tab_plane[:].bitcast(I32), 0)
+        nc.vector.memset(w4_plane[:].bitcast(I32), 0)
+        nc.vector.memset(tab2_plane[:].bitcast(I32), 0)
+
+        wg_raw = [keep.tile([P, PACK, H], F32, name="wg_raw%d" % a) for a in range(PASSES)]
+        tab = [keep.tile([P, T], U32, name="tab%d" % a) for a in range(PASSES)]
+        w4_raw = keep.tile([P, PASSES * 2 * H], U8, name="w4_raw", align_bytes=64)
+        page = [keep.tile([P, T2], F32, name="page%d" % t) for t in range(PACK)]
+        wgs_sb = keep.tile([P, PACK * S], F32, name="wgs_sb")
+        tab2 = keep.tile([P, T3], U32, name="tab2")
+        bid_sb = keep.tile([P, S2 // P], F32, name="bid_sb")
+        reserve_sb = [keep.tile([P, 4, PICKS], F32, name="reserve%d" % u) for u in range(2)]
+
+        for a in range(PASSES):
+            nc.sync.dma_start(out=wg_raw[a][:], in_=wg[512 * a : 512 * (a + 1), :].rearrange("(p j) c -> p j c", j=PACK))
+        nc.sync.dma_start(idx[:], offs)
+        nc.scalar.dma_start(
+            out=w4_raw[:].bitcast(I32).rearrange("p (a n) -> p a n", a=PASSES),
+            in_=w4_words.bitcast(I32).rearrange("a p n -> p a n"),
+        )
+        load_scale_rows(nc.scalar, tab_plane, tab_scales)
+        for a in range(PASSES):
+            nc.sync.dma_start(out=tab[a][:].bitcast(I32), in_=tab_words[a].rearrange("p t i -> p (t i)").bitcast(I32))
+        load_scale_rows(nc.scalar, w4_plane, w4_scales)
+        page_rows = page0.rearrange("(p t) c -> t p c", t=PACK)
+        nc.sync.dma_start(out=page[0][:], in_=page_rows[0])
+        for q in range(QUADS):
+            nc.sync.dma_start(out=wgs_sb[32 * q : 32 * (q + 1), :], in_=wgs.rearrange("(p t) j -> p (t j)", t=PACK))
+        nc.sync.dma_start(idx3[:], offs3)
+        nc.sync.dma_start(idx2[:], offs2)
+        load_scale_rows(nc.sync, tab2_plane, tab2_scales)
+        for t in range(1, PACK):
+            nc.sync.dma_start(out=page[t][:], in_=page_rows[t])
+        nc.sync.dma_start(out=tab2[:].bitcast(I32), in_=tab2_words[0].rearrange("p t i -> p (t i)").bitcast(I32))
+        nc.sync.dma_start(idx4[:], offs4)
+        with nc.allow_non_contiguous_dma(reason="one bid a partition"):
+            nc.sync.dma_start(out=bid_sb[:], in_=bid.rearrange("(i p) -> p i", p=P))
+        for u in range(2):
+            nc.sync.dma_start(
+                out=reserve_sb[u][:],
+                in_=reserve[512 * u : 512 * (u + 1), :].rearrange("(i p) m -> p i m", p=P),
+            )
+
+        w4_codes = keep.tile([P, PASSES * 2 * H], U8, name="w4_codes", align_bytes=64)
+        nc.vector.tensor_copy(
+            out=w4_codes[:].bitcast(U16).rearrange("p (a t m) -> p a m t", a=PASSES, t=PACK),
+            in_=w4_raw[:].bitcast(U16).rearrange("p (a m t) -> p a m t", a=PASSES, t=PACK),
+        )
+
+        v_scale = [keep.tile([P, S], U8, name="v_scale%d" % a, align_bytes=64) for a in range(PASSES)]
+        for a in range(PASSES):
+            nc.vector.tensor_copy(v_scale[a][:], tab_plane[:, a * T : (a + 1) * T].indirect(idx[:]))
+
+        w4_scale = keep.tile([P, PASSES * H], U8, name="w4_scale", align_bytes=64)
+        nc.vector.tensor_copy(
+            out=w4_scale[:].rearrange("p (a t m) -> p a m t", a=PASSES, t=PACK),
+            in_=w4_plane[:].rearrange("p (a m t) -> p a m t", a=PASSES, t=PACK),
+        )
+
+        wg_codes = [keep.tile([P, H], U32, name="wg_codes%d" % a, align_bytes=64) for a in range(PASSES)]
+        wg_scale = [keep.tile([P, H], U8, name="wg_scale%d" % a, align_bytes=64) for a in range(PASSES)]
+        for a in range(PASSES):
+            wg_bf = keep.tile([P, H * PACK], BF16, name="wg_bf%d" % a, align_bytes=64)
+            nc.scalar.copy(
+                out=wg_bf[:].rearrange("p (t m j) -> p m j t", t=PACK, j=PACK),
+                in_=wg_raw[a][:].rearrange("p j (m t) -> p m j t", t=PACK),
+            )
+            nc.vector.quantize_mx(out=wg_codes[a][:].bitcast(FP8X4), scales=wg_scale[a][:], in_=wg_bf[:])
+
+        feat = [psum.tile([P, BANK], F32, name="bank") for t in range(PACK)]
+        gate = [psum.tile([P, BANK], F32, name="bank") for t in range(PACK)]
+        for a in range(PASSES):
+            v_codes = keep.tile([P, S], U32, name="v_codes%d" % a, align_bytes=64)
+            nc.vector.tensor_copy(v_codes[:], tab[a][:].indirect(idx[:]))
+            for t in range(PACK):
+                nc.tensor.matmul_mx(
+                    out=gate[t][:],
+                    lhsT=wg_codes[a][:, P * t : P * (t + 1)].bitcast(FP8X4),
+                    lhsT_scale=wg_scale[a][:, P * t : P * (t + 1)],
+                    rhs=v_codes[:].bitcast(FP8X4), rhs_scale=v_scale[a][:],
+                    start=(a == 0), stop=(a == PASSES - 1),
+                )
+                c0 = a * H + P * t
+                nc.tensor.matmul_mx(
+                    out=feat[t][:],
+                    lhsT=w4_codes[:, 2 * c0 : 2 * (c0 + P)].bitcast(FP4X4),
+                    lhsT_scale=w4_scale[:, c0 : c0 + P],
+                    rhs=v_codes[:].bitcast(FP8X4), rhs_scale=v_scale[a][:],
+                    start=(a == 0), stop=(a == PASSES - 1),
+                )
+
+        v2_scale = keep.tile([P, S2], U8, name="v2_scale", align_bytes=64)
+        nc.vector.tensor_copy(v2_scale[:], tab2_plane[:].indirect(idx2[:]))
+
+        halves = T2 // BANK
+        page_bf = [keep.tile([P, BANK, PACK], BF16, name="page_bf%d" % c, align_bytes=64) for c in range(halves)]
+        sigs = []
+        for t in range(PACK):
+            sig = keep.tile([P, S], F32, name="sig%d" % t)
+            nc.scalar.activation(out=sig[:], in_=gate[t][:], func=ACT.Sigmoid)
+            sigs.append(sig)
+        for t in range(PACK):
+            h = ring.tile([P, S], F32, name="h")
+            nc.vector.tensor_tensor(h[:], feat[t][:], sigs[t][:], ALU.mult)
+            nc.vector.tensor_tensor(page[t][:].indirect(idx3[:]), h[:], wgs_sb[:, t * S : (t + 1) * S], ALU.mult)
+            for c in range(halves):
+                nc.scalar.copy(out=page_bf[c][:, :, t], in_=page[t][:, c * BANK : (c + 1) * BANK])
+
+        chunk = 256
+        v2_codes = [keep.tile([P, chunk], U32, name="v2_codes%d" % g, align_bytes=64) for g in range(S2 // chunk)]
+        for g in range(S2 // chunk):
+            nc.vector.tensor_copy(v2_codes[g][:], tab2[:].indirect(idx2[:, g * chunk // 16 : (g + 1) * chunk // 16]))
+
+        page_codes = [keep.tile([P, BANK], U32, name="page_codes%d" % c, align_bytes=64) for c in range(halves)]
+        page_scale = [keep.tile([P, BANK], U8, name="page_scale%d" % c, align_bytes=64) for c in range(halves)]
+        for c in range(halves):
+            nc.vector.quantize_mx(
+                out=page_codes[c][:].bitcast(FP8X4), scales=page_scale[c][:],
+                in_=page_bf[c][:].rearrange("p c t -> p (c t)"),
+            )
+
+        for i in range(S2 // P):
+            g, o = divmod(i * P, chunk)
+            e = ring.tile([P, T2], F32, name="e")
+            for c in range(halves):
+                acc = psum.tile([P, BANK], F32, name="bank")
+                nc.tensor.matmul_mx(
+                    out=acc[:],
+                    lhsT=v2_codes[g][:, o : o + P].bitcast(FP8X4),
+                    lhsT_scale=v2_scale[:, i * P : (i + 1) * P],
+                    rhs=page_codes[c][:].bitcast(FP8X4), rhs_scale=page_scale[c][:],
+                    start=True, stop=True,
+                )
+                nc.scalar.copy(out=e[:, c * BANK : (c + 1) * BANK], in_=acc[:])
+            x = ring.tile([P, PICKS], F32, name="x")
+            nc.vector.tensor_copy(x[:], e[:].indirect(idx4[:]))
+            ex = ring.tile([P, PICKS], F32, name="ex")
+            nc.scalar.activation(out=ex[:], in_=x[:], func=ACT.Exp)
+            res = ring.tile([P, PICKS], F32, name="res")
+            nc.vector.scalar_tensor_tensor(
+                out=res[:], in0=ex[:], scalar=bid_sb[:, i : i + 1], in1=reserve_sb[i // 4][:, i % 4, :],
+                op0=ALU.mult, op1=ALU.subtract,
+            )
+            nc.sync.dma_start(out=out[i * P : (i + 1) * P, :], in_=res[:])

@@ -24,10 +24,9 @@ QUADS = 4
 
 
 def load_scale_rows(queue, plane, scales):
-    passes = scales.shape[0]
     for q in range(QUADS):
         queue.dma_start(
-            out=plane[32 * q : 32 * q + 4, :].bitcast(I32).rearrange("r (a n) -> r a n", a=passes),
+            out=plane[32 * q : 32 * q + 4, :].bitcast(I32),
             in_=scales[:, 4 * q : 4 * q + 4, :].bitcast(I32).rearrange("a r n -> r a n"),
         )
 
@@ -40,50 +39,71 @@ def tile_list_auction_slot_scores_kernel(
     with ExitStack() as ctx:
         keep = ctx.enter_context(tc.tile_pool(name="keep", bufs=1))
         ring = ctx.enter_context(tc.tile_pool(name="ring", bufs=3))
-        psum = ctx.enter_context(tc.psum_pool(name="psum", bufs=8))
+        psum = ctx.enter_context(tc.psum_pool(name="psum", bufs=1))
 
         idx = keep.tile([P, S // 16], U16, name="idx")
         idx2 = keep.tile([P, S2 // 16], U16, name="idx2")
         idx3 = keep.tile([P, S // 16], U16, name="idx3")
         idx4 = keep.tile([P, PICKS // 16], U16, name="idx4")
 
-        tab_plane = keep.tile([P, PASSES * T], U8, name="tab_plane", align_bytes=64)
-        w4_plane = keep.tile([P, PASSES * H], U8, name="w4_plane", align_bytes=64)
+        def slot(shape, dtype, name, tag):
+            return keep.tile(shape, dtype, name=name, tag=tag, align_bytes=64)
+
+        tab_plane = slot([P, PASSES * T], U8, "tab_plane", "s_ts")
+        w4_plane = slot([P, PASSES * H], U8, "w4_plane", "s_w4s")
         tab2_plane = keep.tile([P, T3], U8, name="tab2_plane", align_bytes=64)
-        nc.vector.memset(tab_plane[:].bitcast(I32), 0)
+        warm = keep.tile([P, 2], F32, name="warm")
+        nc.gpsimd.memset(tab_plane[:].bitcast(I32), 0)
+        nc.vector.memset(warm[:], 0.0)
         nc.vector.memset(w4_plane[:].bitcast(I32), 0)
         nc.vector.memset(tab2_plane[:].bitcast(I32), 0)
+        nc.scalar.activation(out=warm[:, 1:2], in_=warm[:, 0:1], func=ACT.Sigmoid)
 
-        wg_raw = [keep.tile([P, PACK, H], F32, name="wg_raw%d" % a) for a in range(PASSES)]
-        tab = [keep.tile([P, T], U32, name="tab%d" % a) for a in range(PASSES)]
+        def load_wg(a):
+            nc.sync.dma_start(out=wg_raw[a][:], in_=wg[512 * a : 512 * (a + 1), :].rearrange("(p j) c -> p j c", j=PACK))
+
+        def load_words(tile, words):
+            nc.sync.dma_start(out=tile[:].bitcast(I32), in_=words.rearrange("p t i -> p (t i)").bitcast(I32))
+
+        def load_page(t):
+            nc.sync.dma_start(out=page[t][:], in_=page_rows[t])
+
+        def load_wgs(u):
+            for q in range(QUADS):
+                nc.sync.dma_start(out=wgs_sb[u][32 * q : 32 * (q + 1), :], in_=wgs_rows[:, 2 * S * u : 2 * S * (u + 1)])
+
         w4_raw = keep.tile([P, PASSES * 2 * H], U8, name="w4_raw", align_bytes=64)
+        wg_raw = [keep.tile([P, PACK, H], F32, name="wg_raw%d" % a) for a in range(PASSES)]
+        tab = [slot([P, T], U32, "tab%d" % a, "s_tab%d" % a) for a in range(PASSES)]
+        page_rows = page0.rearrange("(p t) c -> t p c", t=PACK)
         page = [keep.tile([P, T2], F32, name="page%d" % t) for t in range(PACK)]
-        wgs_sb = keep.tile([P, PACK * S], F32, name="wgs_sb")
+        wgs_rows = wgs.rearrange("(p t) j -> p (t j)", t=PACK)
+        wgs_sb = [slot([P, 2 * S], F32, "wgs_sb%d" % u, "s_wgs%d" % u) for u in range(2)]
         tab2 = keep.tile([P, T3], U32, name="tab2")
         bid_sb = keep.tile([P, S2 // P], F32, name="bid_sb")
         reserve_sb = [keep.tile([P, 4, PICKS], F32, name="reserve%d" % u) for u in range(2)]
 
-        for a in range(PASSES):
-            nc.sync.dma_start(out=wg_raw[a][:], in_=wg[512 * a : 512 * (a + 1), :].rearrange("(p j) c -> p j c", j=PACK))
         nc.sync.dma_start(idx[:], offs)
-        nc.scalar.dma_start(
+        nc.sync.dma_start(
             out=w4_raw[:].bitcast(I32).rearrange("p (a n) -> p a n", a=PASSES),
             in_=w4_words.bitcast(I32).rearrange("a p n -> p a n"),
         )
-        load_scale_rows(nc.scalar, tab_plane, tab_scales)
+        load_wg(0)
+        load_scale_rows(nc.sync, tab_plane, tab_scales)
+        load_wg(1)
+        load_scale_rows(nc.sync, w4_plane, w4_scales)
         for a in range(PASSES):
-            nc.sync.dma_start(out=tab[a][:].bitcast(I32), in_=tab_words[a].rearrange("p t i -> p (t i)").bitcast(I32))
-        load_scale_rows(nc.scalar, w4_plane, w4_scales)
-        page_rows = page0.rearrange("(p t) c -> t p c", t=PACK)
-        nc.sync.dma_start(out=page[0][:], in_=page_rows[0])
-        for q in range(QUADS):
-            nc.sync.dma_start(out=wgs_sb[32 * q : 32 * (q + 1), :], in_=wgs.rearrange("(p t) j -> p (t j)", t=PACK))
-        nc.sync.dma_start(idx3[:], offs3)
+            load_words(tab[a], tab_words[a])
         nc.sync.dma_start(idx2[:], offs2)
         load_scale_rows(nc.sync, tab2_plane, tab2_scales)
-        for t in range(1, PACK):
-            nc.sync.dma_start(out=page[t][:], in_=page_rows[t])
-        nc.sync.dma_start(out=tab2[:].bitcast(I32), in_=tab2_words[0].rearrange("p t i -> p (t i)").bitcast(I32))
+        load_page(0)
+        load_wgs(0)
+        nc.sync.dma_start(idx3[:], offs3)
+        load_page(1)
+        load_wgs(1)
+        load_page(2)
+        load_page(3)
+        load_words(tab2, tab2_words[0])
         nc.sync.dma_start(idx4[:], offs4)
         with nc.allow_non_contiguous_dma(reason="one bid a partition"):
             nc.sync.dma_start(out=bid_sb[:], in_=bid.rearrange("(i p) -> p i", p=P))
@@ -98,70 +118,93 @@ def tile_list_auction_slot_scores_kernel(
             out=w4_codes[:].bitcast(U16).rearrange("p (a t m) -> p a m t", a=PASSES, t=PACK),
             in_=w4_raw[:].bitcast(U16).rearrange("p (a m t) -> p a m t", a=PASSES, t=PACK),
         )
-
         v_scale = [keep.tile([P, S], U8, name="v_scale%d" % a, align_bytes=64) for a in range(PASSES)]
         for a in range(PASSES):
             nc.vector.tensor_copy(v_scale[a][:], tab_plane[:, a * T : (a + 1) * T].indirect(idx[:]))
 
-        w4_scale = keep.tile([P, PASSES * H], U8, name="w4_scale", align_bytes=64)
+        wg_codes, wg_scale, v_codes = [], [], []
+
+        def quantise_wg(a, tag):
+            wg_bf = slot([P, H * PACK], BF16, "wg_bf%d" % a, "s_bf%d" % a)
+            nc.scalar.copy(
+                out=wg_bf[:].rearrange("p (t m j) -> p m t j", t=PACK, j=PACK),
+                in_=wg_raw[a][:].rearrange("p j (m t) -> p m t j", t=PACK),
+            )
+            wg_codes.append(slot([P, H], U32, "wg_codes%d" % a, tag))
+            wg_scale.append(keep.tile([P, H], U8, name="wg_scale%d" % a, align_bytes=64))
+            nc.vector.quantize_mx(out=wg_codes[a][:].bitcast(FP8X4), scales=wg_scale[a][:], in_=wg_bf[:])
+
+        def gather_v(a, tag):
+            v_codes.append(slot([P, S], U32, "v_codes%d" % a, tag))
+            nc.vector.tensor_copy(v_codes[a][:], tab[a][:].indirect(idx[:]))
+
+        quantise_wg(0, "s_ts")
+        w4_scale = slot([P, PASSES * H], U8, "w4_scale", "s_bf0")
         nc.vector.tensor_copy(
             out=w4_scale[:].rearrange("p (a t m) -> p a m t", a=PASSES, t=PACK),
             in_=w4_plane[:].rearrange("p (a m t) -> p a m t", a=PASSES, t=PACK),
         )
+        gather_v(0, "s_w4s")
+        quantise_wg(1, "s_tab0")
+        gather_v(1, "s_bf1")
 
-        wg_codes = [keep.tile([P, H], U32, name="wg_codes%d" % a, align_bytes=64) for a in range(PASSES)]
-        wg_scale = [keep.tile([P, H], U8, name="wg_scale%d" % a, align_bytes=64) for a in range(PASSES)]
-        for a in range(PASSES):
-            wg_bf = keep.tile([P, H * PACK], BF16, name="wg_bf%d" % a, align_bytes=64)
-            nc.scalar.copy(
-                out=wg_bf[:].rearrange("p (t m j) -> p m j t", t=PACK, j=PACK),
-                in_=wg_raw[a][:].rearrange("p j (m t) -> p m j t", t=PACK),
+        gate, feat, sigs = [], [], []
+
+        def gate_pass(t, a):
+            nc.tensor.matmul_mx(
+                out=gate[t][:],
+                lhsT=wg_codes[a][:, P * t : P * (t + 1)].bitcast(FP8X4),
+                lhsT_scale=wg_scale[a][:, P * t : P * (t + 1)],
+                rhs=v_codes[a][:].bitcast(FP8X4), rhs_scale=v_scale[a][:],
+                start=(a == 0), stop=(a == PASSES - 1),
             )
-            nc.vector.quantize_mx(out=wg_codes[a][:].bitcast(FP8X4), scales=wg_scale[a][:], in_=wg_bf[:])
 
-        feat = [psum.tile([P, BANK], F32, name="bank") for t in range(PACK)]
-        gate = [psum.tile([P, BANK], F32, name="bank") for t in range(PACK)]
-        for a in range(PASSES):
-            v_codes = keep.tile([P, S], U32, name="v_codes%d" % a, align_bytes=64)
-            nc.vector.tensor_copy(v_codes[:], tab[a][:].indirect(idx[:]))
-            for t in range(PACK):
-                nc.tensor.matmul_mx(
-                    out=gate[t][:],
-                    lhsT=wg_codes[a][:, P * t : P * (t + 1)].bitcast(FP8X4),
-                    lhsT_scale=wg_scale[a][:, P * t : P * (t + 1)],
-                    rhs=v_codes[:].bitcast(FP8X4), rhs_scale=v_scale[a][:],
-                    start=(a == 0), stop=(a == PASSES - 1),
-                )
-                c0 = a * H + P * t
-                nc.tensor.matmul_mx(
-                    out=feat[t][:],
-                    lhsT=w4_codes[:, 2 * c0 : 2 * (c0 + P)].bitcast(FP4X4),
-                    lhsT_scale=w4_scale[:, c0 : c0 + P],
-                    rhs=v_codes[:].bitcast(FP8X4), rhs_scale=v_scale[a][:],
-                    start=(a == 0), stop=(a == PASSES - 1),
-                )
+        def feat_pass(t, a):
+            c0 = a * H + P * t
+            nc.tensor.matmul_mx(
+                out=feat[t][:],
+                lhsT=w4_codes[:, 2 * c0 : 2 * (c0 + P)].bitcast(FP4X4),
+                lhsT_scale=w4_scale[:, c0 : c0 + P],
+                rhs=v_codes[a][:].bitcast(FP8X4), rhs_scale=v_scale[a][:],
+                start=(a == 0), stop=(a == PASSES - 1),
+            )
 
-        v2_scale = keep.tile([P, S2], U8, name="v2_scale", align_bytes=64)
-        nc.vector.tensor_copy(v2_scale[:], tab2_plane[:].indirect(idx2[:]))
+        def gate_slice(t):
+            gate.append(psum.tile([P, BANK], F32, name="gate", bufs=2))
+            for a in range(PASSES):
+                gate_pass(t, a)
+            sigs.append(keep.tile([P, S], F32, name="sig%d" % t))
+            nc.scalar.activation(out=sigs[t][:], in_=gate[t][:], func=ACT.Sigmoid)
+
+        def feat_slice(t):
+            feat.append(psum.tile([P, BANK], F32, name="feat"))
+            for a in range(PASSES):
+                feat_pass(t, a)
+
+        gate_slice(0)
+        feat_slice(0)
+        for t in range(1, PACK):
+            gate_slice(t)
+
+        v2_scale = [slot([P, S2 // 2], U8, "v2_scale0", "s_tab1")]
+        nc.vector.tensor_copy(v2_scale[0][:], tab2_plane[:].indirect(idx2[:, 0:32]))
 
         halves = T2 // BANK
-        page_bf = [keep.tile([P, BANK, PACK], BF16, name="page_bf%d" % c, align_bytes=64) for c in range(halves)]
-        sigs = []
+        page_bf = [slot([P, BANK, PACK], BF16, "page_bf%d" % c, "g_pb%d" % c) for c in range(halves)]
+        warm2 = keep.tile([P, 1], F32, name="warm2")
+        nc.scalar.activation(out=warm2[:], in_=sigs[PACK - 1][:, 0:1], func=ACT.Exp)
         for t in range(PACK):
-            sig = keep.tile([P, S], F32, name="sig%d" % t)
-            nc.scalar.activation(out=sig[:], in_=gate[t][:], func=ACT.Sigmoid)
-            sigs.append(sig)
-        for t in range(PACK):
+            if t > 0:
+                feat_slice(t)
             h = ring.tile([P, S], F32, name="h")
             nc.vector.tensor_tensor(h[:], feat[t][:], sigs[t][:], ALU.mult)
-            nc.vector.tensor_tensor(page[t][:].indirect(idx3[:]), h[:], wgs_sb[:, t * S : (t + 1) * S], ALU.mult)
+            nc.vector.tensor_tensor(page[t][:].indirect(idx3[:]), h[:], wgs_sb[t // 2][:, (t % 2) * S : (t % 2 + 1) * S], ALU.mult)
             for c in range(halves):
                 nc.scalar.copy(out=page_bf[c][:, :, t], in_=page[t][:, c * BANK : (c + 1) * BANK])
 
-        chunk = 256
-        v2_codes = [keep.tile([P, chunk], U32, name="v2_codes%d" % g, align_bytes=64) for g in range(S2 // chunk)]
-        for g in range(S2 // chunk):
-            nc.vector.tensor_copy(v2_codes[g][:], tab2[:].indirect(idx2[:, g * chunk // 16 : (g + 1) * chunk // 16]))
+        chunk = 512
+        v2_codes = [slot([P, chunk], U32, "v2_codes0", "s_wgs1")]
+        nc.vector.tensor_copy(v2_codes[0][:], tab2[:].indirect(idx2[:, 0:32]))
 
         page_codes = [keep.tile([P, BANK], U32, name="page_codes%d" % c, align_bytes=64) for c in range(halves)]
         page_scale = [keep.tile([P, BANK], U8, name="page_scale%d" % c, align_bytes=64) for c in range(halves)]
@@ -170,27 +213,44 @@ def tile_list_auction_slot_scores_kernel(
                 out=page_codes[c][:].bitcast(FP8X4), scales=page_scale[c][:],
                 in_=page_bf[c][:].rearrange("p c t -> p (c t)"),
             )
+        v2_scale.append(slot([P, chunk], U8, "v2_scale1", "g_pb0"))
+        nc.vector.tensor_copy(v2_scale[1][:], tab2_plane[:].indirect(idx2[:, 32:64]))
+        v2_codes.append(slot([P, chunk], U32, "v2_codes1", "g_pb1"))
+        nc.vector.tensor_copy(v2_codes[1][:], tab2[:].indirect(idx2[:, 32:64]))
 
-        for i in range(S2 // P):
+        picked = {}
+
+        def front(i):
             g, o = divmod(i * P, chunk)
             e = ring.tile([P, T2], F32, name="e")
             for c in range(halves):
-                acc = psum.tile([P, BANK], F32, name="bank")
+                acc = psum.tile([P, BANK], F32, name="bank", bufs=5)
                 nc.tensor.matmul_mx(
                     out=acc[:],
                     lhsT=v2_codes[g][:, o : o + P].bitcast(FP8X4),
-                    lhsT_scale=v2_scale[:, i * P : (i + 1) * P],
+                    lhsT_scale=v2_scale[i // 4][:, (i % 4) * P : (i % 4 + 1) * P],
                     rhs=page_codes[c][:].bitcast(FP8X4), rhs_scale=page_scale[c][:],
                     start=True, stop=True,
                 )
                 nc.scalar.copy(out=e[:, c * BANK : (c + 1) * BANK], in_=acc[:])
-            x = ring.tile([P, PICKS], F32, name="x")
+            x = ring.tile([P, PICKS], F32, name="x", bufs=4)
             nc.vector.tensor_copy(x[:], e[:].indirect(idx4[:]))
+            picked[i] = x
+
+        def back(i):
             ex = ring.tile([P, PICKS], F32, name="ex")
-            nc.scalar.activation(out=ex[:], in_=x[:], func=ACT.Exp)
+            nc.scalar.activation(out=ex[:], in_=picked[i][:], func=ACT.Exp)
             res = ring.tile([P, PICKS], F32, name="res")
             nc.vector.scalar_tensor_tensor(
                 out=res[:], in0=ex[:], scalar=bid_sb[:, i : i + 1], in1=reserve_sb[i // 4][:, i % 4, :],
                 op0=ALU.mult, op1=ALU.subtract,
             )
             nc.sync.dma_start(out=out[i * P : (i + 1) * P, :], in_=res[:])
+
+        tiles = S2 // P
+        lag = 2
+        for i in range(tiles + lag):
+            if i < tiles:
+                front(i)
+            if i >= lag:
+                back(i - lag)

@@ -20,13 +20,18 @@ P = 128
 PACK = 4
 PASSES = K // (P * PACK)
 BANK = 512
+BANKS = 8
 QUADS = 4
+V2_ROW = 8
+TILES = S2 // P
+HALVES = T2 // BANK
+PIECES = ((0, 512), (512, 768), (768, 1024))
 
 
-def load_scale_rows(queue, plane, scales):
+def load_scale_rows(queue, plane, scales, row):
     for q in range(QUADS):
         queue.dma_start(
-            out=plane[32 * q : 32 * q + 4, :].bitcast(I32),
+            out=plane[32 * q + row : 32 * q + row + 4, :].bitcast(I32),
             in_=scales[:, 4 * q : 4 * q + 4, :].bitcast(I32).rearrange("a r n -> r a n"),
         )
 
@@ -49,15 +54,20 @@ def tile_list_auction_slot_scores_kernel(
         def slot(shape, dtype, name, tag):
             return keep.tile(shape, dtype, name=name, tag=tag, align_bytes=64)
 
+        def bank(k):
+            return psum.tile([P, BANK], F32, name="bank%d" % k, tag="bank%d" % k)
+
         tab_plane = slot([P, PASSES * T], U8, "tab_plane", "s_ts")
         w4_plane = slot([P, PASSES * H], U8, "w4_plane", "s_w4s")
-        tab2_plane = keep.tile([P, T3], U8, name="tab2_plane", align_bytes=64)
-        warm = keep.tile([P, 2], F32, name="warm")
-        nc.gpsimd.memset(tab_plane[:].bitcast(I32), 0)
-        nc.vector.memset(warm[:], 0.0)
+        tab2_plane = slot([P, T3], U8, "tab2_plane", "s_t2s")
+        zero = slot([P, 1], F32, "zero", "s_zero")
+        warm_sigmoid = keep.tile([P, 1], F32, name="warm_sigmoid")
+        nc.vector.memset(zero[:], 0.0)
+        nc.vector.memset(tab_plane[:, 0:T].bitcast(I32), 0)
+        nc.gpsimd.memset(tab_plane[:, T : 2 * T].bitcast(I32), 0)
         nc.vector.memset(w4_plane[:].bitcast(I32), 0)
-        nc.vector.memset(tab2_plane[:].bitcast(I32), 0)
-        nc.scalar.activation(out=warm[:, 1:2], in_=warm[:, 0:1], func=ACT.Sigmoid)
+        nc.gpsimd.memset(tab2_plane[:].bitcast(I32), 0)
+        nc.scalar.activation(out=warm_sigmoid[:], in_=zero[:], func=ACT.Sigmoid)
 
         def load_wg(a):
             nc.sync.dma_start(out=wg_raw[a][:], in_=wg[512 * a : 512 * (a + 1), :].rearrange("(p j) c -> p j c", j=PACK))
@@ -68,19 +78,21 @@ def tile_list_auction_slot_scores_kernel(
         def load_page(t):
             nc.sync.dma_start(out=page[t][:], in_=page_rows[t])
 
-        def load_wgs(u):
-            for q in range(QUADS):
-                nc.sync.dma_start(out=wgs_sb[u][32 * q : 32 * (q + 1), :], in_=wgs_rows[:, 2 * S * u : 2 * S * (u + 1)])
+        def load_wgs(tile, first, last):
+            for q in (0, 2, 1, 3):
+                nc.sync.dma_start(out=tile[32 * q : 32 * (q + 1), :], in_=wgs_rows[:, S * first : S * last])
 
-        w4_raw = keep.tile([P, PASSES * 2 * H], U8, name="w4_raw", align_bytes=64)
+        w4_raw = slot([P, PASSES * 2 * H], U8, "w4_raw", "s_w4r")
         wg_raw = [keep.tile([P, PACK, H], F32, name="wg_raw%d" % a) for a in range(PASSES)]
         tab = [slot([P, T], U32, "tab%d" % a, "s_tab%d" % a) for a in range(PASSES)]
         page_rows = page0.rearrange("(p t) c -> t p c", t=PACK)
         page = [keep.tile([P, T2], F32, name="page%d" % t) for t in range(PACK)]
         wgs_rows = wgs.rearrange("(p t) j -> p (t j)", t=PACK)
-        wgs_sb = [slot([P, 2 * S], F32, "wgs_sb%d" % u, "s_wgs%d" % u) for u in range(2)]
-        tab2 = keep.tile([P, T3], U32, name="tab2")
-        bid_sb = keep.tile([P, S2 // P], F32, name="bid_sb")
+        wgs_first = slot([P, S], F32, "wgs_first", "s_wgs0")
+        wgs_rest = slot([P, (PACK - 1) * S], F32, "wgs_rest", "s_wgs")
+        wgs_of = [wgs_first[:]] + [wgs_rest[:, S * u : S * (u + 1)] for u in range(PACK - 1)]
+        tab2 = slot([P, T3], U32, "tab2", "s_tab2")
+        bid_sb = keep.tile([P, TILES], F32, name="bid_sb")
         reserve_sb = [keep.tile([P, 4, PICKS], F32, name="reserve%d" % u) for u in range(2)]
 
         nc.sync.dma_start(idx[:], offs)
@@ -89,24 +101,24 @@ def tile_list_auction_slot_scores_kernel(
             in_=w4_words.bitcast(I32).rearrange("a p n -> p a n"),
         )
         load_wg(0)
-        load_scale_rows(nc.sync, tab_plane, tab_scales)
+        load_scale_rows(nc.sync, tab_plane, tab_scales, 0)
         load_wg(1)
-        load_scale_rows(nc.sync, w4_plane, w4_scales)
+        load_scale_rows(nc.sync, w4_plane, w4_scales, 0)
         for a in range(PASSES):
             load_words(tab[a], tab_words[a])
         nc.sync.dma_start(idx2[:], offs2)
-        load_scale_rows(nc.sync, tab2_plane, tab2_scales)
-        load_page(0)
-        load_wgs(0)
+        load_scale_rows(nc.sync, tab2_plane, tab2_scales, V2_ROW)
         nc.sync.dma_start(idx3[:], offs3)
-        load_page(1)
-        load_wgs(1)
-        load_page(2)
-        load_page(3)
-        load_words(tab2, tab2_words[0])
-        nc.sync.dma_start(idx4[:], offs4)
+        load_page(0)
+        load_wgs(wgs_first, 0, 1)
         with nc.allow_non_contiguous_dma(reason="one bid a partition"):
             nc.sync.dma_start(out=bid_sb[:], in_=bid.rearrange("(i p) -> p i", p=P))
+        load_page(1)
+        load_wgs(wgs_rest, 1, PACK)
+        load_words(tab2, tab2_words[0])
+        load_page(2)
+        load_page(3)
+        nc.sync.dma_start(idx4[:], offs4)
         for u in range(2):
             nc.sync.dma_start(
                 out=reserve_sb[u][:],
@@ -115,8 +127,8 @@ def tile_list_auction_slot_scores_kernel(
 
         w4_codes = keep.tile([P, PASSES * 2 * H], U8, name="w4_codes", align_bytes=64)
         nc.vector.tensor_copy(
-            out=w4_codes[:].bitcast(U16).rearrange("p (a t m) -> p a m t", a=PASSES, t=PACK),
-            in_=w4_raw[:].bitcast(U16).rearrange("p (a m t) -> p a m t", a=PASSES, t=PACK),
+            out=w4_codes[:].bitcast(U16).rearrange("p (a t m) -> p a t m", a=PASSES, t=PACK),
+            in_=w4_raw[:].bitcast(U16).rearrange("p (a m t) -> p a t m", a=PASSES, t=PACK),
         )
         v_scale = [keep.tile([P, S], U8, name="v_scale%d" % a, align_bytes=64) for a in range(PASSES)]
         for a in range(PASSES):
@@ -141,116 +153,130 @@ def tile_list_auction_slot_scores_kernel(
         quantise_wg(0, "s_ts")
         w4_scale = slot([P, PASSES * H], U8, "w4_scale", "s_bf0")
         nc.vector.tensor_copy(
-            out=w4_scale[:].rearrange("p (a t m) -> p a m t", a=PASSES, t=PACK),
-            in_=w4_plane[:].rearrange("p (a m t) -> p a m t", a=PASSES, t=PACK),
+            out=w4_scale[:].rearrange("p (a t m) -> p a t m", a=PASSES, t=PACK),
+            in_=w4_plane[:].rearrange("p (a m t) -> p a t m", a=PASSES, t=PACK),
         )
         gather_v(0, "s_w4s")
         quantise_wg(1, "s_tab0")
         gather_v(1, "s_bf1")
 
-        gate, feat, sigs = [], [], []
-
-        def gate_pass(t, a):
-            nc.tensor.matmul_mx(
-                out=gate[t][:],
-                lhsT=wg_codes[a][:, P * t : P * (t + 1)].bitcast(FP8X4),
-                lhsT_scale=wg_scale[a][:, P * t : P * (t + 1)],
-                rhs=v_codes[a][:].bitcast(FP8X4), rhs_scale=v_scale[a][:],
-                start=(a == 0), stop=(a == PASSES - 1),
-            )
-
-        def feat_pass(t, a):
-            c0 = a * H + P * t
-            nc.tensor.matmul_mx(
-                out=feat[t][:],
-                lhsT=w4_codes[:, 2 * c0 : 2 * (c0 + P)].bitcast(FP4X4),
-                lhsT_scale=w4_scale[:, c0 : c0 + P],
-                rhs=v_codes[a][:].bitcast(FP8X4), rhs_scale=v_scale[a][:],
-                start=(a == 0), stop=(a == PASSES - 1),
-            )
+        feat, sigs = [], []
 
         def gate_slice(t):
-            gate.append(psum.tile([P, BANK], F32, name="gate", bufs=2))
+            gate = bank(2 * (t % 2))
+            cols = slice(P * t, P * (t + 1))
             for a in range(PASSES):
-                gate_pass(t, a)
-            sigs.append(keep.tile([P, S], F32, name="sig%d" % t))
-            nc.scalar.activation(out=sigs[t][:], in_=gate[t][:], func=ACT.Sigmoid)
+                nc.tensor.matmul_mx(
+                    out=gate[:],
+                    lhsT=wg_codes[a][:, cols].bitcast(FP8X4), lhsT_scale=wg_scale[a][:, cols],
+                    rhs=v_codes[a][:].bitcast(FP8X4), rhs_scale=v_scale[a][:],
+                    start=(a == 0), stop=(a == PASSES - 1),
+                )
+            sigs.append(slot([P, S], F32, "sig%d" % t, "s_sig%d" % t))
+            nc.scalar.activation(out=sigs[t][:], in_=gate[:], func=ACT.Sigmoid, bias=zero[:])
 
         def feat_slice(t):
-            feat.append(psum.tile([P, BANK], F32, name="feat"))
+            feat.append(bank((1, 3, 0, 2)[t]))
             for a in range(PASSES):
-                feat_pass(t, a)
+                c0 = a * H + P * t
+                nc.tensor.matmul_mx(
+                    out=feat[t][:],
+                    lhsT=w4_codes[:, 2 * c0 : 2 * (c0 + P)].bitcast(FP4X4),
+                    lhsT_scale=w4_scale[:, c0 : c0 + P],
+                    rhs=v_codes[a][:].bitcast(FP8X4), rhs_scale=v_scale[a][:],
+                    start=(a == 0), stop=(a == PASSES - 1),
+                )
 
-        gate_slice(0)
-        feat_slice(0)
-        for t in range(1, PACK):
+        for t in range(2):
             gate_slice(t)
+            feat_slice(t)
+        for t in range(2, PACK):
+            gate_slice(t)
+        for t in range(2, PACK):
+            feat_slice(t)
 
-        v2_scale = [slot([P, S2 // 2], U8, "v2_scale0", "s_tab1")]
-        nc.vector.tensor_copy(v2_scale[0][:], tab2_plane[:].indirect(idx2[:, 0:32]))
+        half = S2 // 2
+        v2_scale = [slot([P, half], U8, "v2_scale0", "s_tab1")]
+        nc.vector.tensor_copy(v2_scale[0][:], tab2_plane[:].indirect(idx2[:, 0 : half // 16]))
 
-        halves = T2 // BANK
-        page_bf = [slot([P, BANK, PACK], BF16, "page_bf%d" % c, "g_pb%d" % c) for c in range(halves)]
-        warm2 = keep.tile([P, 1], F32, name="warm2")
-        nc.scalar.activation(out=warm2[:], in_=sigs[PACK - 1][:, 0:1], func=ACT.Exp)
+        ln_bid = slot([P, TILES], F32, "ln_bid", "s_zero")
+        nc.scalar.activation(out=ln_bid[:], in_=bid_sb[:], func=ACT.Ln)
+        warm_exp = slot([P, 1], F32, "warm_exp", "s_pb0")
+        nc.scalar.activation(out=warm_exp[:], in_=ln_bid[:, 0:1], func=ACT.Exp)
+
+        page_bf = [slot([P, hi - lo, PACK], BF16, "page_bf%d" % c, "s_pb%d" % c) for c, (lo, hi) in enumerate(PIECES)]
+        hs = []
+
+        def product(t):
+            hs.append(slot([P, S], F32, "h%d" % t, ("s_h0", "s_h0", "s_wgs0", "s_sig1")[t]))
+            nc.vector.tensor_tensor(hs[t][:], feat[t][:], sigs[t][:], ALU.mult)
+
         for t in range(PACK):
-            if t > 0:
-                feat_slice(t)
-            h = ring.tile([P, S], F32, name="h")
-            nc.vector.tensor_tensor(h[:], feat[t][:], sigs[t][:], ALU.mult)
-            nc.vector.tensor_tensor(page[t][:].indirect(idx3[:]), h[:], wgs_sb[t // 2][:, (t % 2) * S : (t % 2 + 1) * S], ALU.mult)
-            for c in range(halves):
-                nc.scalar.copy(out=page_bf[c][:, :, t], in_=page[t][:, c * BANK : (c + 1) * BANK])
+            for ahead in ((0,), (1, 2, 3), (), ())[t]:
+                product(ahead)
+            nc.vector.tensor_tensor(page[t][:].indirect(idx3[:]), hs[t][:], wgs_of[t], ALU.mult)
+            for c, (lo, hi) in enumerate(PIECES):
+                nc.scalar.copy(out=page_bf[c][:, :, t], in_=page[t][:, lo:hi])
 
-        chunk = 512
-        v2_codes = [slot([P, chunk], U32, "v2_codes0", "s_wgs1")]
-        nc.vector.tensor_copy(v2_codes[0][:], tab2[:].indirect(idx2[:, 0:32]))
+        v2_codes = [slot([P, half], U32, "v2_codes0", "s_wgs")]
+        nc.vector.tensor_copy(v2_codes[0][:], tab2[:].indirect(idx2[:, 0 : half // 16]))
 
-        page_codes = [keep.tile([P, BANK], U32, name="page_codes%d" % c, align_bytes=64) for c in range(halves)]
-        page_scale = [keep.tile([P, BANK], U8, name="page_scale%d" % c, align_bytes=64) for c in range(halves)]
-        for c in range(halves):
+        page_codes = [keep.tile([P, BANK], U32, name="page_codes0", align_bytes=64)]
+        page_scale = [keep.tile([P, BANK], U8, name="page_scale%d" % c, align_bytes=64) for c in range(HALVES)]
+        for c, (lo, hi) in enumerate(PIECES):
+            cols = slice(lo % BANK, lo % BANK + hi - lo)
             nc.vector.quantize_mx(
-                out=page_codes[c][:].bitcast(FP8X4), scales=page_scale[c][:],
+                out=page_codes[lo // BANK][:, cols].bitcast(FP8X4), scales=page_scale[lo // BANK][:, cols],
                 in_=page_bf[c][:].rearrange("p c t -> p (c t)"),
             )
-        v2_scale.append(slot([P, chunk], U8, "v2_scale1", "g_pb0"))
-        nc.vector.tensor_copy(v2_scale[1][:], tab2_plane[:].indirect(idx2[:, 32:64]))
-        v2_codes.append(slot([P, chunk], U32, "v2_codes1", "g_pb1"))
-        nc.vector.tensor_copy(v2_codes[1][:], tab2[:].indirect(idx2[:, 32:64]))
+            if c == 0:
+                v2_scale.append(slot([P, half], U8, "v2_scale1", "s_pb0"))
+                nc.vector.tensor_copy(v2_scale[1][:], tab2_plane[:].indirect(idx2[:, half // 16 : S2 // 16]))
+                page_codes.append(slot([P, BANK], U32, "page_codes1", "s_t2s"))
+        v2_codes.append(slot([P, half], U32, "v2_codes1", "s_pb%d" % (len(PIECES) - 1)))
+        nc.vector.tensor_copy(v2_codes[1][:], tab2[:].indirect(idx2[:, half // 16 : S2 // 16]))
 
-        picked = {}
+        picked, banks_used = {}, []
+
+        def parts(i):
+            return [(0, PICKS // 2), (PICKS // 2, PICKS)] if i == TILES - 1 else [(0, PICKS)]
 
         def front(i):
-            g, o = divmod(i * P, chunk)
-            e = ring.tile([P, T2], F32, name="e")
-            for c in range(halves):
-                acc = psum.tile([P, BANK], F32, name="bank", bufs=5)
+            e = ring.tile([P, T2], F32, name="e", bufs=4)
+            spans = PIECES if i == 0 else ((0, BANK), (BANK, T2))
+            for lo, hi in spans:
+                c, cols = lo // BANK, slice(lo % BANK, lo % BANK + hi - lo)
+                acc = bank((4, 5, 6, 7, 1, 3, 0, 2)[len(banks_used) % BANKS])
+                banks_used.append(acc)
                 nc.tensor.matmul_mx(
-                    out=acc[:],
-                    lhsT=v2_codes[g][:, o : o + P].bitcast(FP8X4),
-                    lhsT_scale=v2_scale[i // 4][:, (i % 4) * P : (i % 4 + 1) * P],
-                    rhs=page_codes[c][:].bitcast(FP8X4), rhs_scale=page_scale[c][:],
+                    out=acc[:, 0 : hi - lo],
+                    lhsT=v2_codes[i // 4][:, (i % 4) * P : (i % 4 + 1) * P].bitcast(FP8X4),
+                    lhsT_scale=v2_scale[i // 4][V2_ROW:P, (i % 4) * P : (i % 4 + 1) * P],
+                    rhs=page_codes[c][:, cols].bitcast(FP8X4), rhs_scale=page_scale[c][:, cols],
                     start=True, stop=True,
                 )
-                nc.scalar.copy(out=e[:, c * BANK : (c + 1) * BANK], in_=acc[:])
-            x = ring.tile([P, PICKS], F32, name="x", bufs=4)
-            nc.vector.tensor_copy(x[:], e[:].indirect(idx4[:]))
-            picked[i] = x
+                if i in (2, 4, 5, 6) and c == 1:
+                    nc.vector.tensor_copy(out=e[:, lo:hi], in_=acc[:, 0 : hi - lo])
+                else:
+                    nc.scalar.copy(out=e[:, lo:hi], in_=acc[:, 0 : hi - lo])
+            picked[i] = []
+            for lo, hi in parts(i):
+                x = ring.tile([P, hi - lo], F32, name="x", bufs=TILES + 1)
+                nc.vector.tensor_copy(x[:], e[:].indirect(idx4[:, lo // 16 : hi // 16]))
+                picked[i].append(x)
 
         def back(i):
-            ex = ring.tile([P, PICKS], F32, name="ex")
-            nc.scalar.activation(out=ex[:], in_=picked[i][:], func=ACT.Exp)
-            res = ring.tile([P, PICKS], F32, name="res")
-            nc.vector.scalar_tensor_tensor(
-                out=res[:], in0=ex[:], scalar=bid_sb[:, i : i + 1], in1=reserve_sb[i // 4][:, i % 4, :],
-                op0=ALU.mult, op1=ALU.subtract,
-            )
-            nc.sync.dma_start(out=out[i * P : (i + 1) * P, :], in_=res[:])
+            finish = nc.vector if i == TILES - 1 else nc.gpsimd
+            for x, (lo, hi) in zip(picked[i], parts(i)):
+                ex = ring.tile([P, hi - lo], F32, name="ex", bufs=TILES + 1)
+                nc.scalar.activation(out=ex[:], in_=x[:], func=ACT.Exp, bias=ln_bid[:, i : i + 1])
+                res = ring.tile([P, hi - lo], F32, name="res", bufs=TILES + 1)
+                finish.tensor_tensor(res[:], ex[:], reserve_sb[i // 4][:, i % 4, lo:hi], ALU.subtract)
+                nc.sync.dma_start(out=out[i * P : (i + 1) * P, lo:hi], in_=res[:])
 
-        tiles = S2 // P
         lag = 2
-        for i in range(tiles + lag):
-            if i < tiles:
+        for i in range(TILES + lag):
+            if i < TILES:
                 front(i)
             if i >= lag:
                 back(i - lag)

@@ -25,7 +25,7 @@ QUADS = 4
 V2_ROW = 8
 TILES = S2 // P
 HALVES = T2 // BANK
-PIECES = ((0, 512), (512, 768), (768, 1024))
+PIECES = ((0, 256), (256, 512), (512, 1024))
 
 
 def load_scale_rows(queue, plane, scales, row):
@@ -44,6 +44,7 @@ def tile_list_auction_slot_scores_kernel(
     with ExitStack() as ctx:
         keep = ctx.enter_context(tc.tile_pool(name="keep", bufs=1))
         ring = ctx.enter_context(tc.tile_pool(name="ring", bufs=3))
+        links = ctx.enter_context(tc.tile_pool(name="links", bufs=1))
         psum = ctx.enter_context(tc.psum_pool(name="psum", bufs=1))
 
         idx = keep.tile([P, S // 16], U16, name="idx")
@@ -201,10 +202,13 @@ def tile_list_auction_slot_scores_kernel(
 
         ln_bid = slot([P, TILES], F32, "ln_bid", "s_zero")
         nc.scalar.activation(out=ln_bid[:], in_=bid_sb[:], func=ACT.Ln)
-        warm_exp = slot([P, 1], F32, "warm_exp", "s_pb0")
-        nc.scalar.activation(out=warm_exp[:], in_=ln_bid[:, 0:1], func=ACT.Exp)
+        def on_piece(shape, dtype, name, c):
+            return links.tile(shape, dtype, name=name, align_bytes=64, offset=2 * PACK * PIECES[c][0])
 
-        page_bf = [slot([P, hi - lo, PACK], BF16, "page_bf%d" % c, "s_pb%d" % c) for c, (lo, hi) in enumerate(PIECES)]
+        warm_exp = on_piece([P, 2 * T2], F32, "warm_exp", 0)
+        nc.scalar.activation(out=warm_exp[:, 0:1], in_=ln_bid[:, 0:1], func=ACT.Exp)
+
+        page_bf = [on_piece([P, hi - lo, PACK], BF16, "page_bf%d" % c, c) for c, (lo, hi) in enumerate(PIECES)]
         hs = []
 
         def product(t):
@@ -218,47 +222,52 @@ def tile_list_auction_slot_scores_kernel(
             for c, (lo, hi) in enumerate(PIECES):
                 nc.scalar.copy(out=page_bf[c][:, :, t], in_=page[t][:, lo:hi])
 
-        v2_codes = [slot([P, half], U32, "v2_codes0", "s_wgs")]
-        nc.vector.tensor_copy(v2_codes[0][:], tab2[:].indirect(idx2[:, 0 : half // 16]))
-
-        page_codes = [keep.tile([P, BANK], U32, name="page_codes0", align_bytes=64)]
+        v2_codes = []
+        page_codes = [keep.tile([P, BANK], U32, name="page_codes0", align_bytes=64), slot([P, BANK], U32, "page_codes1", "s_tab2")]
         page_scale = [keep.tile([P, BANK], U8, name="page_scale%d" % c, align_bytes=64) for c in range(HALVES)]
-        for c, (lo, hi) in enumerate(PIECES):
+
+        def gather_v2(u, codes):
+            v2_codes.append(codes)
+            nc.vector.tensor_copy(v2_codes[u][:], tab2[:].indirect(idx2[:, u * half // 16 : (u + 1) * half // 16]))
+
+        def quantise_page(c):
+            lo, hi = PIECES[c]
             cols = slice(lo % BANK, lo % BANK + hi - lo)
             nc.vector.quantize_mx(
                 out=page_codes[lo // BANK][:, cols].bitcast(FP8X4), scales=page_scale[lo // BANK][:, cols],
                 in_=page_bf[c][:].rearrange("p c t -> p (c t)"),
             )
-            if c == 0:
-                v2_scale.append(slot([P, half], U8, "v2_scale1", "s_pb0"))
-                nc.vector.tensor_copy(v2_scale[1][:], tab2_plane[:].indirect(idx2[:, half // 16 : S2 // 16]))
-                page_codes.append(slot([P, BANK], U32, "page_codes1", "s_t2s"))
-        v2_codes.append(slot([P, half], U32, "v2_codes1", "s_pb%d" % (len(PIECES) - 1)))
-        nc.vector.tensor_copy(v2_codes[1][:], tab2[:].indirect(idx2[:, half // 16 : S2 // 16]))
 
-        picked, banks_used = {}, []
+        gather_v2(0, slot([P, half], U32, "v2_codes0", "s_wgs"))
+        quantise_page(0)
+        quantise_page(1)
+        gather_v2(1, on_piece([P, half], U32, "v2_codes1", 1))
+        quantise_page(2)
+        v2_scale.append(on_piece([P, half], U8, "v2_scale1", 2))
+        nc.vector.tensor_copy(v2_scale[1][:], tab2_plane[:].indirect(idx2[:, half // 16 : S2 // 16]))
+
+        picked, scores = {}, {}
 
         def parts(i):
             return [(0, PICKS // 2), (PICKS // 2, PICKS)] if i == TILES - 1 else [(0, PICKS)]
 
-        def front(i):
-            e = ring.tile([P, T2], F32, name="e", bufs=4)
-            spans = PIECES if i == 0 else ((0, BANK), (BANK, T2))
-            for lo, hi in spans:
-                c, cols = lo // BANK, slice(lo % BANK, lo % BANK + hi - lo)
-                acc = bank((4, 5, 6, 7, 1, 3, 0, 2)[len(banks_used) % BANKS])
-                banks_used.append(acc)
+        def score(i, c):
+            if c == 0:
+                scores[i] = slot([P, T2], F32, "e%d" % i, "s_e%d" % (i % 4))
+            acc = bank(4 * c + i % 4)
+            entries = slice((i % 4) * P, (i % 4 + 1) * P)
+            for lo, hi in PIECES[:2] if (i, c) == (0, 0) else ((0, BANK),):
                 nc.tensor.matmul_mx(
-                    out=acc[:, 0 : hi - lo],
-                    lhsT=v2_codes[i // 4][:, (i % 4) * P : (i % 4 + 1) * P].bitcast(FP8X4),
-                    lhsT_scale=v2_scale[i // 4][V2_ROW:P, (i % 4) * P : (i % 4 + 1) * P],
-                    rhs=page_codes[c][:, cols].bitcast(FP8X4), rhs_scale=page_scale[c][:, cols],
+                    out=acc[:, lo:hi],
+                    lhsT=v2_codes[i // 4][:, entries].bitcast(FP8X4), lhsT_scale=v2_scale[i // 4][V2_ROW:P, entries],
+                    rhs=page_codes[c][:, lo:hi].bitcast(FP8X4), rhs_scale=page_scale[c][:, lo:hi],
                     start=True, stop=True,
                 )
-                if i in (2, 4, 5, 6) and c == 1:
-                    nc.vector.tensor_copy(out=e[:, lo:hi], in_=acc[:, 0 : hi - lo])
-                else:
-                    nc.scalar.copy(out=e[:, lo:hi], in_=acc[:, 0 : hi - lo])
+            empty = nc.vector.tensor_copy if (i, c) in ((3, 1), (5, 1)) else nc.scalar.copy
+            empty(out=scores[i][:, c * BANK : (c + 1) * BANK], in_=acc[:])
+
+        def pick(i):
+            e = scores[i]
             picked[i] = []
             for lo, hi in parts(i):
                 x = ring.tile([P, hi - lo], F32, name="x", bufs=TILES + 1)
@@ -266,7 +275,7 @@ def tile_list_auction_slot_scores_kernel(
                 picked[i].append(x)
 
         def back(i):
-            finish = nc.vector if i == TILES - 1 else nc.gpsimd
+            finish = nc.vector if i >= TILES - 2 else nc.gpsimd
             for x, (lo, hi) in zip(picked[i], parts(i)):
                 ex = ring.tile([P, hi - lo], F32, name="ex", bufs=TILES + 1)
                 nc.scalar.activation(out=ex[:], in_=x[:], func=ACT.Exp, bias=ln_bid[:, i : i + 1])
@@ -274,9 +283,17 @@ def tile_list_auction_slot_scores_kernel(
                 finish.tensor_tensor(res[:], ex[:], reserve_sb[i // 4][:, i % 4, lo:hi], ALU.subtract)
                 nc.sync.dma_start(out=out[i * P : (i + 1) * P, lo:hi], in_=res[:])
 
-        lag = 2
-        for i in range(TILES + lag):
-            if i < TILES:
-                front(i)
-            if i >= lag:
-                back(i - lag)
+        ahead = 3
+        for c in range(HALVES):
+            for i in range(2):
+                score(i, c)
+        for c in range(HALVES):
+            score(2, c)
+        pick(0)
+        for i in range(TILES):
+            if i + 1 < TILES:
+                pick(i + 1)
+            back(i)
+            if i + ahead < TILES:
+                for c in range(HALVES):
+                    score(i + ahead, c)

@@ -21,7 +21,6 @@ PACK = 4
 PASSES = K // (P * PACK)
 BANK = 512
 BANKS = 8
-QUADS = 4
 V2_ROW = 8
 TILES = S2 // P
 HALVES = T2 // BANK
@@ -29,10 +28,10 @@ PIECES = ((0, 256), (256, 512), (512, 1024))
 
 
 def load_scale_rows(queue, plane, scales, row):
-    for q in range(QUADS):
+    for r in range(4):
         queue.dma_start(
-            out=plane[32 * q + row : 32 * q + row + 4, :].bitcast(I32),
-            in_=scales[:, 4 * q : 4 * q + 4, :].bitcast(I32).rearrange("a r n -> r a n"),
+            out=plane[row + r : P : 32, :].bitcast(I32),
+            in_=scales.bitcast(I32).rearrange("a (q r) n -> r q a n", r=4)[r],
         )
 
 
@@ -63,11 +62,11 @@ def tile_list_auction_slot_scores_kernel(
         tab2_plane = slot([P, T3], U8, "tab2_plane", "s_t2s")
         zero = slot([P, 1], F32, "zero", "s_zero")
         warm_sigmoid = keep.tile([P, 1], F32, name="warm_sigmoid")
+        for plane in (w4_plane, tab2_plane, tab_plane):
+            nc.vector.memset(plane[:].bitcast(I32), 0)
         nc.vector.memset(zero[:], 0.0)
-        nc.vector.memset(tab_plane[:, 0:T].bitcast(I32), 0)
-        nc.gpsimd.memset(tab_plane[:, T : 2 * T].bitcast(I32), 0)
-        nc.vector.memset(w4_plane[:].bitcast(I32), 0)
-        nc.gpsimd.memset(tab2_plane[:].bitcast(I32), 0)
+        load_scale_rows(nc.gpsimd, w4_plane, w4_scales, 0)
+        load_scale_rows(nc.gpsimd, tab2_plane, tab2_scales, V2_ROW)
         nc.scalar.activation(out=warm_sigmoid[:], in_=zero[:], func=ACT.Sigmoid)
 
         def load_wg(a):
@@ -90,8 +89,9 @@ def tile_list_auction_slot_scores_kernel(
         page = [keep.tile([P, T2], F32, name="page%d" % t) for t in range(PACK)]
         wgs_rows = wgs.rearrange("(p t) j -> p (t j)", t=PACK)
         wgs_first = slot([P, S], F32, "wgs_first", "s_wgs0")
-        wgs_rest = slot([P, (PACK - 1) * S], F32, "wgs_rest", "s_wgs")
-        wgs_of = [wgs_first[:]] + [wgs_rest[:, S * u : S * (u + 1)] for u in range(PACK - 1)]
+        wgs_second = slot([P, S], F32, "wgs_second", "s_wgs1")
+        wgs_rest = slot([P, 2 * S], F32, "wgs_rest", "s_wgs")
+        wgs_of = [wgs_first[:], wgs_second[:], wgs_rest[:, 0:S], wgs_rest[:, S : 2 * S]]
         tab2 = slot([P, T3], U32, "tab2", "s_tab2")
         bid_sb = keep.tile([P, TILES], F32, name="bid_sb")
         reserve_sb = [keep.tile([P, 4, PICKS], F32, name="reserve%d" % u) for u in range(2)]
@@ -104,20 +104,19 @@ def tile_list_auction_slot_scores_kernel(
         load_wg(0)
         load_scale_rows(nc.sync, tab_plane, tab_scales, 0)
         load_wg(1)
-        load_scale_rows(nc.sync, w4_plane, w4_scales, 0)
         for a in range(PASSES):
             load_words(tab[a], tab_words[a])
         nc.sync.dma_start(idx2[:], offs2)
-        load_scale_rows(nc.sync, tab2_plane, tab2_scales, V2_ROW)
-        nc.sync.dma_start(idx3[:], offs3)
         load_page(0)
         load_wgs(wgs_first, 0, 1)
+        nc.sync.dma_start(idx3[:], offs3)
         with nc.allow_non_contiguous_dma(reason="one bid a partition"):
             nc.sync.dma_start(out=bid_sb[:], in_=bid.rearrange("(i p) -> p i", p=P))
         load_page(1)
-        load_wgs(wgs_rest, 1, PACK)
-        load_words(tab2, tab2_words[0])
+        load_wgs(wgs_second, 1, 2)
         load_page(2)
+        load_wgs(wgs_rest, 2, PACK)
+        load_words(tab2, tab2_words[0])
         load_page(3)
         nc.sync.dma_start(idx4[:], offs4)
         for u in range(2):
@@ -152,52 +151,49 @@ def tile_list_auction_slot_scores_kernel(
             nc.vector.tensor_copy(v_codes[a][:], tab[a][:].indirect(idx[:]))
 
         quantise_wg(0, "s_ts")
-        w4_scale = slot([P, PASSES * H], U8, "w4_scale", "s_bf0")
+        gather_v(0, "s_bf0")
+        quantise_wg(1, "s_tab0")
+        gather_v(1, "s_bf1")
+        w4_scale = slot([P, PASSES * H], U8, "w4_scale", "s_tab1")
         nc.vector.tensor_copy(
             out=w4_scale[:].rearrange("p (a t m) -> p a t m", a=PASSES, t=PACK),
             in_=w4_plane[:].rearrange("p (a m t) -> p a t m", a=PASSES, t=PACK),
         )
-        gather_v(0, "s_w4s")
-        quantise_wg(1, "s_tab0")
-        gather_v(1, "s_bf1")
 
-        feat, sigs = [], []
+        gate = [bank(t) for t in range(PACK)]
+        feat = [bank(PACK + t) for t in range(PACK)]
+        sigs = []
 
-        def gate_slice(t):
-            gate = bank(2 * (t % 2))
+        def gate_pass(t, a):
             cols = slice(P * t, P * (t + 1))
-            for a in range(PASSES):
-                nc.tensor.matmul_mx(
-                    out=gate[:],
-                    lhsT=wg_codes[a][:, cols].bitcast(FP8X4), lhsT_scale=wg_scale[a][:, cols],
-                    rhs=v_codes[a][:].bitcast(FP8X4), rhs_scale=v_scale[a][:],
-                    start=(a == 0), stop=(a == PASSES - 1),
-                )
+            nc.tensor.matmul_mx(
+                out=gate[t][:],
+                lhsT=wg_codes[a][:, cols].bitcast(FP8X4), lhsT_scale=wg_scale[a][:, cols],
+                rhs=v_codes[a][:].bitcast(FP8X4), rhs_scale=v_scale[a][:],
+                start=(a == 0), stop=(a == PASSES - 1),
+            )
+
+        def feat_pass(t, a):
+            c0 = a * H + P * t
+            nc.tensor.matmul_mx(
+                out=feat[t][:],
+                lhsT=w4_codes[:, 2 * c0 : 2 * (c0 + P)].bitcast(FP4X4),
+                lhsT_scale=w4_scale[:, c0 : c0 + P],
+                rhs=v_codes[a][:].bitcast(FP8X4), rhs_scale=v_scale[a][:],
+                start=(a == 0), stop=(a == PASSES - 1),
+            )
+
+        for t in range(PACK):
+            gate_pass(t, 0)
+        for t in range(PACK):
+            gate_pass(t, 1)
             sigs.append(slot([P, S], F32, "sig%d" % t, "s_sig%d" % t))
-            nc.scalar.activation(out=sigs[t][:], in_=gate[:], func=ACT.Sigmoid, bias=zero[:])
-
-        def feat_slice(t):
-            feat.append(bank((1, 3, 0, 2)[t]))
+            nc.scalar.activation(out=sigs[t][:], in_=gate[t][:], func=ACT.Sigmoid, bias=zero[:])
             for a in range(PASSES):
-                c0 = a * H + P * t
-                nc.tensor.matmul_mx(
-                    out=feat[t][:],
-                    lhsT=w4_codes[:, 2 * c0 : 2 * (c0 + P)].bitcast(FP4X4),
-                    lhsT_scale=w4_scale[:, c0 : c0 + P],
-                    rhs=v_codes[a][:].bitcast(FP8X4), rhs_scale=v_scale[a][:],
-                    start=(a == 0), stop=(a == PASSES - 1),
-                )
-
-        for t in range(2):
-            gate_slice(t)
-            feat_slice(t)
-        for t in range(2, PACK):
-            gate_slice(t)
-        for t in range(2, PACK):
-            feat_slice(t)
+                feat_pass(t, a)
 
         half = S2 // 2
-        v2_scale = [slot([P, half], U8, "v2_scale0", "s_tab1")]
+        v2_scale = [slot([P, half], U8, "v2_scale0", "s_w4s")]
         nc.vector.tensor_copy(v2_scale[0][:], tab2_plane[:].indirect(idx2[:, 0 : half // 16]))
 
         ln_bid = slot([P, TILES], F32, "ln_bid", "s_zero")
@@ -212,11 +208,11 @@ def tile_list_auction_slot_scores_kernel(
         hs = []
 
         def product(t):
-            hs.append(slot([P, S], F32, "h%d" % t, ("s_h0", "s_h0", "s_wgs0", "s_sig1")[t]))
+            hs.append(slot([P, S], F32, "h%d" % t, ("s_h0", "s_h1", "s_h0", "s_wgs0")[t]))
             nc.vector.tensor_tensor(hs[t][:], feat[t][:], sigs[t][:], ALU.mult)
 
         for t in range(PACK):
-            for ahead in ((0,), (1, 2, 3), (), ())[t]:
+            for ahead in ((0, 1), (2, 3), (), ())[t]:
                 product(ahead)
             nc.vector.tensor_tensor(page[t][:].indirect(idx3[:]), hs[t][:], wgs_of[t], ALU.mult)
             for c, (lo, hi) in enumerate(PIECES):

@@ -1,6 +1,7 @@
 from contextlib import ExitStack
 
 import concourse.mybir as mybir
+from concourse.masks import make_identity
 
 K, H, T, S, T2, T3, S2, PICKS = 1024, 512, 2048, 512, 1024, 2048, 1024, 512
 FLOPS = 2 * (2 * K * H * S + H * S2 * T2)
@@ -21,7 +22,6 @@ PACK = 4
 PASSES = K // (P * PACK)
 BANK = 512
 BANKS = 8
-V2_ROW = 8
 TILES = S2 // P
 HALVES = T2 // BANK
 PIECES = ((0, 256), (256, 512), (512, 1024))
@@ -60,14 +60,19 @@ def tile_list_auction_slot_scores_kernel(
         tab_plane = slot([P, PASSES * T], U8, "tab_plane", "s_ts")
         w4_plane = slot([P, PASSES * H], U8, "w4_plane", "s_w4s")
         tab2_plane = slot([P, T3], U8, "tab2_plane", "s_t2s")
-        zero = slot([P, 1], F32, "zero", "s_zero")
-        warm_sigmoid = keep.tile([P, 1], F32, name="warm_sigmoid")
-        for plane in (w4_plane, tab2_plane, tab_plane):
+        v2_scale = keep.tile([P, S2], U8, name="v2_scale", align_bytes=64)
+        one = keep.tile([P, 1], F32, name="one")
+        bid_rows = keep.tile([P, P], F32, name="bid_rows")
+        identity = keep.tile([P, P], F32, name="identity")
+        for plane in (tab2_plane, tab_plane):
             nc.vector.memset(plane[:].bitcast(I32), 0)
-        nc.vector.memset(zero[:], 0.0)
-        load_scale_rows(nc.gpsimd, w4_plane, w4_scales, 0)
-        load_scale_rows(nc.gpsimd, tab2_plane, tab2_scales, V2_ROW)
-        nc.scalar.activation(out=warm_sigmoid[:], in_=zero[:], func=ACT.Sigmoid)
+        nc.gpsimd.memset(one[:], 1.0)
+        for plane in (w4_plane, v2_scale):
+            nc.gpsimd.memset(plane[:].bitcast(I32), 0)
+        nc.gpsimd.memset(bid_rows[:], 0.0)
+        make_identity(nc, identity[:])
+        warm_ln = keep.tile([P, 1], F32, name="warm_ln")
+        nc.scalar.activation(out=warm_ln[:], in_=one[:], func=ACT.Ln)
 
         def load_wg(a):
             nc.sync.dma_start(out=wg_raw[a][:], in_=wg[512 * a : 512 * (a + 1), :].rearrange("(p j) c -> p j c", j=PACK))
@@ -83,7 +88,7 @@ def tile_list_auction_slot_scores_kernel(
                 nc.sync.dma_start(out=tile[32 * q : 32 * (q + 1), :], in_=wgs_rows[:, S * first : S * last])
 
         w4_raw = slot([P, PASSES * 2 * H], U8, "w4_raw", "s_w4r")
-        wg_raw = [keep.tile([P, PACK, H], F32, name="wg_raw%d" % a) for a in range(PASSES)]
+        wg_raw = [slot([P, PACK, H], F32, "wg_raw%d" % a, "s_raw%d" % a) for a in range(PASSES)]
         tab = [slot([P, T], U32, "tab%d" % a, "s_tab%d" % a) for a in range(PASSES)]
         page_rows = page0.rearrange("(p t) c -> t p c", t=PACK)
         page = [keep.tile([P, T2], F32, name="page%d" % t) for t in range(PACK)]
@@ -93,25 +98,25 @@ def tile_list_auction_slot_scores_kernel(
         wgs_rest = slot([P, 2 * S], F32, "wgs_rest", "s_wgs")
         wgs_of = [wgs_first[:], wgs_second[:], wgs_rest[:, 0:S], wgs_rest[:, S : 2 * S]]
         tab2 = slot([P, T3], U32, "tab2", "s_tab2")
-        bid_sb = keep.tile([P, TILES], F32, name="bid_sb")
         reserve_sb = [keep.tile([P, 4, PICKS], F32, name="reserve%d" % u) for u in range(2)]
 
         nc.sync.dma_start(idx[:], offs)
+        nc.sync.dma_start(idx2[:], offs2)
         nc.sync.dma_start(
             out=w4_raw[:].bitcast(I32).rearrange("p (a n) -> p a n", a=PASSES),
             in_=w4_words.bitcast(I32).rearrange("a p n -> p a n"),
         )
+        nc.sync.dma_start(out=tab2_plane[0:P:8, :].bitcast(I32), in_=tab2_scales[0].bitcast(I32))
         load_wg(0)
         load_scale_rows(nc.sync, tab_plane, tab_scales, 0)
         load_wg(1)
+        nc.sync.dma_start(out=bid_rows[0:TILES, :], in_=bid.rearrange("(i p) -> i p", p=P))
         for a in range(PASSES):
             load_words(tab[a], tab_words[a])
-        nc.sync.dma_start(idx2[:], offs2)
+        load_scale_rows(nc.sync, w4_plane, w4_scales, 0)
         load_page(0)
         load_wgs(wgs_first, 0, 1)
         nc.sync.dma_start(idx3[:], offs3)
-        with nc.allow_non_contiguous_dma(reason="one bid a partition"):
-            nc.sync.dma_start(out=bid_sb[:], in_=bid.rearrange("(i p) -> p i", p=P))
         load_page(1)
         load_wgs(wgs_second, 1, 2)
         load_page(2)
@@ -130,7 +135,11 @@ def tile_list_auction_slot_scores_kernel(
             out=w4_codes[:].bitcast(U16).rearrange("p (a t m) -> p a t m", a=PASSES, t=PACK),
             in_=w4_raw[:].bitcast(U16).rearrange("p (a m t) -> p a t m", a=PASSES, t=PACK),
         )
-        v_scale = [keep.tile([P, S], U8, name="v_scale%d" % a, align_bytes=64) for a in range(PASSES)]
+        v2_rows = slot([P, S2], U8, "v2_rows", "s_w4r")
+        nc.vector.tensor_copy(v2_rows[:], tab2_plane[:].indirect(idx2[:]))
+        for r in range(4):
+            nc.sync.dma_start(out=v2_scale[r:P:32, :].bitcast(I32), in_=v2_rows[8 * r : P : 32, :].bitcast(I32))
+        v_scale = [slot([P, S], U8, "v_scale%d" % a, ("s_t2s", "s_vs1")[a]) for a in range(PASSES)]
         for a in range(PASSES):
             nc.vector.tensor_copy(v_scale[a][:], tab_plane[:, a * T : (a + 1) * T].indirect(idx[:]))
 
@@ -160,6 +169,13 @@ def tile_list_auction_slot_scores_kernel(
             in_=w4_plane[:].rearrange("p (a m t) -> p a t m", a=PASSES, t=PACK),
         )
 
+        bid_turned = bank(BANKS - 1)
+        nc.tensor.transpose(bid_turned[:, 0:P], bid_rows[:], identity[:])
+        ln_bid = slot([P, TILES], F32, "ln_bid", "s_raw1")
+        nc.scalar.activation(out=ln_bid[:], in_=bid_turned[:, 0:TILES], func=ACT.Ln)
+        warm_sigmoid = keep.tile([P, 1], F32, name="warm_sigmoid")
+        nc.scalar.activation(out=warm_sigmoid[:], in_=ln_bid[:, 0:1], func=ACT.Sigmoid)
+
         gate = [bank(t) for t in range(PACK)]
         feat = [bank(PACK + t) for t in range(PACK)]
         sigs = []
@@ -188,21 +204,17 @@ def tile_list_auction_slot_scores_kernel(
         for t in range(PACK):
             gate_pass(t, 1)
             sigs.append(slot([P, S], F32, "sig%d" % t, "s_sig%d" % t))
-            nc.scalar.activation(out=sigs[t][:], in_=gate[t][:], func=ACT.Sigmoid, bias=zero[:])
+            nc.scalar.activation(out=sigs[t][:], in_=gate[t][:], func=ACT.Sigmoid)
             for a in range(PASSES):
                 feat_pass(t, a)
 
         half = S2 // 2
-        v2_scale = [slot([P, half], U8, "v2_scale0", "s_w4s")]
-        nc.vector.tensor_copy(v2_scale[0][:], tab2_plane[:].indirect(idx2[:, 0 : half // 16]))
 
-        ln_bid = slot([P, TILES], F32, "ln_bid", "s_zero")
-        nc.scalar.activation(out=ln_bid[:], in_=bid_sb[:], func=ACT.Ln)
         def on_piece(shape, dtype, name, c):
             return links.tile(shape, dtype, name=name, align_bytes=64, offset=2 * PACK * PIECES[c][0])
 
         warm_exp = on_piece([P, 2 * T2], F32, "warm_exp", 0)
-        nc.scalar.activation(out=warm_exp[:, 0:1], in_=ln_bid[:, 0:1], func=ACT.Exp)
+        nc.scalar.activation(out=warm_exp[:, 0:1], in_=sigs[PACK - 1][:, 0:1], func=ACT.Exp)
 
         page_bf = [on_piece([P, hi - lo, PACK], BF16, "page_bf%d" % c, c) for c, (lo, hi) in enumerate(PIECES)]
         hs = []
@@ -239,8 +251,6 @@ def tile_list_auction_slot_scores_kernel(
         quantise_page(1)
         gather_v2(1, on_piece([P, half], U32, "v2_codes1", 1))
         quantise_page(2)
-        v2_scale.append(on_piece([P, half], U8, "v2_scale1", 2))
-        nc.vector.tensor_copy(v2_scale[1][:], tab2_plane[:].indirect(idx2[:, half // 16 : S2 // 16]))
 
         picked, scores = {}, {}
 
@@ -249,17 +259,17 @@ def tile_list_auction_slot_scores_kernel(
 
         def score(i, c):
             if c == 0:
-                scores[i] = slot([P, T2], F32, "e%d" % i, "s_e%d" % (i % 4))
+                scores[i] = on_piece([P, T2], F32, "e2", 2) if i == 2 else slot([P, T2], F32, "e%d" % i, "s_e%d" % (i % 4))
             acc = bank(4 * c + i % 4)
             entries = slice((i % 4) * P, (i % 4 + 1) * P)
             for lo, hi in PIECES[:2] if (i, c) == (0, 0) else ((0, BANK),):
                 nc.tensor.matmul_mx(
                     out=acc[:, lo:hi],
-                    lhsT=v2_codes[i // 4][:, entries].bitcast(FP8X4), lhsT_scale=v2_scale[i // 4][V2_ROW:P, entries],
+                    lhsT=v2_codes[i // 4][:, entries].bitcast(FP8X4), lhsT_scale=v2_scale[:, i * P : (i + 1) * P],
                     rhs=page_codes[c][:, lo:hi].bitcast(FP8X4), rhs_scale=page_scale[c][:, lo:hi],
                     start=True, stop=True,
                 )
-            empty = nc.vector.tensor_copy if (i, c) in ((3, 1), (5, 1)) else nc.scalar.copy
+            empty = nc.vector.tensor_copy if (i, c) in ((2, 0), (0, 1), (5, 1)) else nc.scalar.copy
             empty(out=scores[i][:, c * BANK : (c + 1) * BANK], in_=acc[:])
 
         def pick(i):
@@ -281,15 +291,15 @@ def tile_list_auction_slot_scores_kernel(
 
         ahead = 3
         for c in range(HALVES):
-            for i in range(2):
+            for i in range(ahead):
                 score(i, c)
-        for c in range(HALVES):
-            score(2, c)
+        score(ahead, 0)
         pick(0)
         for i in range(TILES):
             if i + 1 < TILES:
                 pick(i + 1)
             back(i)
             if i + ahead < TILES:
-                for c in range(HALVES):
-                    score(i + ahead, c)
+                score(i + ahead, 1)
+            if i + ahead + 1 < TILES:
+                score(i + ahead + 1, 0)

@@ -269,7 +269,7 @@ def tile_list_auction_slot_scores_kernel(
                     rhs=page_codes[c][:, lo:hi].bitcast(FP8X4), rhs_scale=page_scale[c][:, lo:hi],
                     start=True, stop=True,
                 )
-            empty = nc.vector.tensor_copy if (i, c) in ((2, 0), (0, 1), (5, 1)) else nc.scalar.copy
+            empty = nc.vector.tensor_copy if (i, c) in ((2, 0), (1, 1), (5, 1)) else nc.scalar.copy
             empty(out=scores[i][:, c * BANK : (c + 1) * BANK], in_=acc[:])
 
         def pick(i):
@@ -285,21 +285,26 @@ def tile_list_auction_slot_scores_kernel(
             for x, (lo, hi) in zip(picked[i], parts(i)):
                 ex = ring.tile([P, hi - lo], F32, name="ex", bufs=TILES + 1)
                 nc.scalar.activation(out=ex[:], in_=x[:], func=ACT.Exp, bias=ln_bid[:, i : i + 1])
-                res = ring.tile([P, hi - lo], F32, name="res", bufs=TILES + 1)
+                if i == TILES - 2:
+                    res = slot([P, hi - lo], F32, "res_late", "s_e3")
+                else:
+                    res = ring.tile([P, hi - lo], F32, name="res", bufs=TILES)
                 finish.tensor_tensor(res[:], ex[:], reserve_sb[i // 4][:, i % 4, lo:hi], ALU.subtract)
                 nc.sync.dma_start(out=out[i * P : (i + 1) * P, lo:hi], in_=res[:])
 
-        ahead = 3
         for c in range(HALVES):
-            for i in range(ahead):
+            for i in range(3):
                 score(i, c)
-        score(ahead, 0)
+        for c in range(HALVES):
+            score(3, c)
         pick(0)
+        rest = [(i, c) for i in range(4, TILES) for c in range(HALVES)]
+        taken = 0
         for i in range(TILES):
             if i + 1 < TILES:
                 pick(i + 1)
             back(i)
-            if i + ahead < TILES:
-                score(i + ahead, 1)
-            if i + ahead + 1 < TILES:
-                score(i + ahead + 1, 0)
+            count = {3: 2, 4: 3}.get(i, 1)
+            for tile, c in rest[taken : taken + count]:
+                score(tile, c)
+            taken = taken + count

@@ -24,6 +24,7 @@ BANK = 512
 BANKS = 8
 TILES = S2 // P
 HALVES = T2 // BANK
+CUTS = ((0, S // 2), (S // 2, S))
 PIECES = ((0, 256), (256, 512), (512, 1024))
 
 
@@ -67,10 +68,10 @@ def tile_list_auction_slot_scores_kernel(
         for plane in (tab2_plane, tab_plane):
             nc.vector.memset(plane[:].bitcast(I32), 0)
         nc.gpsimd.memset(one[:], 1.0)
-        for plane in (w4_plane, v2_scale):
-            nc.gpsimd.memset(plane[:].bitcast(I32), 0)
         nc.gpsimd.memset(bid_rows[:], 0.0)
+        nc.gpsimd.memset(w4_plane[:].bitcast(I32), 0)
         make_identity(nc, identity[:])
+        nc.gpsimd.memset(v2_scale[:].bitcast(I32), 0)
         warm_ln = keep.tile([P, 1], F32, name="warm_ln")
         nc.scalar.activation(out=warm_ln[:], in_=one[:], func=ACT.Ln)
 
@@ -100,20 +101,20 @@ def tile_list_auction_slot_scores_kernel(
         tab2 = slot([P, T3], U32, "tab2", "s_tab2")
         reserve_sb = [keep.tile([P, 4, PICKS], F32, name="reserve%d" % u) for u in range(2)]
 
-        nc.sync.dma_start(idx[:], offs)
         nc.sync.dma_start(idx2[:], offs2)
+        nc.sync.dma_start(idx[:], offs)
         nc.sync.dma_start(
             out=w4_raw[:].bitcast(I32).rearrange("p (a n) -> p a n", a=PASSES),
             in_=w4_words.bitcast(I32).rearrange("a p n -> p a n"),
         )
         nc.sync.dma_start(out=tab2_plane[0:P:8, :].bitcast(I32), in_=tab2_scales[0].bitcast(I32))
+        nc.sync.dma_start(out=bid_rows[0:TILES, :], in_=bid.rearrange("(i p) -> i p", p=P))
         load_wg(0)
         load_scale_rows(nc.sync, tab_plane, tab_scales, 0)
-        load_wg(1)
-        nc.sync.dma_start(out=bid_rows[0:TILES, :], in_=bid.rearrange("(i p) -> i p", p=P))
-        for a in range(PASSES):
-            load_words(tab[a], tab_words[a])
+        load_words(tab[0], tab_words[0])
         load_scale_rows(nc.sync, w4_plane, w4_scales, 0)
+        load_wg(1)
+        load_words(tab[1], tab_words[1])
         load_page(0)
         load_wgs(wgs_first, 0, 1)
         nc.sync.dma_start(idx3[:], offs3)
@@ -130,103 +131,155 @@ def tile_list_auction_slot_scores_kernel(
                 in_=reserve[512 * u : 512 * (u + 1), :].rearrange("(i p) m -> p i m", p=P),
             )
 
-        w4_codes = keep.tile([P, PASSES * 2 * H], U8, name="w4_codes", align_bytes=64)
-        nc.vector.tensor_copy(
-            out=w4_codes[:].bitcast(U16).rearrange("p (a t m) -> p a t m", a=PASSES, t=PACK),
-            in_=w4_raw[:].bitcast(U16).rearrange("p (a m t) -> p a t m", a=PASSES, t=PACK),
-        )
-        v2_rows = slot([P, S2], U8, "v2_rows", "s_w4r")
+        def fresh(shape, dtype, name):
+            return keep.tile(shape, dtype, name=name, align_bytes=64)
+
+        v2_rows = fresh([P, S2], U8, "v2_rows")
         nc.vector.tensor_copy(v2_rows[:], tab2_plane[:].indirect(idx2[:]))
         for r in range(4):
             nc.sync.dma_start(out=v2_scale[r:P:32, :].bitcast(I32), in_=v2_rows[8 * r : P : 32, :].bitcast(I32))
-        v_scale = [slot([P, S], U8, "v_scale%d" % a, ("s_t2s", "s_vs1")[a]) for a in range(PASSES)]
+        v_scale = [fresh([P, S], U8, "v_scale%d" % a) for a in range(PASSES)]
         for a in range(PASSES):
             nc.vector.tensor_copy(v_scale[a][:], tab_plane[:, a * T : (a + 1) * T].indirect(idx[:]))
 
-        wg_codes, wg_scale, v_codes = [], [], []
+        wg_codes, wg_scale = {}, {}
+        v_codes = []
 
-        def quantise_wg(a, tag):
-            wg_bf = slot([P, H * PACK], BF16, "wg_bf%d" % a, "s_bf%d" % a)
-            nc.scalar.copy(
-                out=wg_bf[:].rearrange("p (t m j) -> p m t j", t=PACK, j=PACK),
-                in_=wg_raw[a][:].rearrange("p j (m t) -> p m t j", t=PACK),
+        def round_wg(copy, a, first, last, tag):
+            wg_bf = slot([P, (last - first) * P * PACK], BF16, "wg_bf%d_%d" % (a, first), tag)
+            copy(
+                out=wg_bf[:].rearrange("p (t m j) -> p m t j", m=P, j=PACK),
+                in_=wg_raw[a][:].rearrange("p j (m t) -> p m t j", t=PACK)[:, :, first:last, :],
             )
-            wg_codes.append(slot([P, H], U32, "wg_codes%d" % a, tag))
-            wg_scale.append(keep.tile([P, H], U8, name="wg_scale%d" % a, align_bytes=64))
-            nc.vector.quantize_mx(out=wg_codes[a][:].bitcast(FP8X4), scales=wg_scale[a][:], in_=wg_bf[:])
+            return wg_bf
+
+        def quantise_wg(wg_bf, a, first, last, tag):
+            codes = slot([P, P * (last - first)], U32, "wg_codes%d_%d" % (a, first), tag)
+            scale = fresh([P, P * (last - first)], U8, "wg_scale%d_%d" % (a, first))
+            nc.vector.quantize_mx(out=codes[:].bitcast(FP8X4), scales=scale[:], in_=wg_bf[:])
+            for t in range(first, last):
+                cols = slice(P * (t - first), P * (t - first + 1))
+                wg_codes[a, t] = codes[:, cols]
+                wg_scale[a, t] = scale[:, cols]
 
         def gather_v(a, tag):
             v_codes.append(slot([P, S], U32, "v_codes%d" % a, tag))
-            nc.vector.tensor_copy(v_codes[a][:], tab[a][:].indirect(idx[:]))
-
-        quantise_wg(0, "s_ts")
-        gather_v(0, "s_bf0")
-        quantise_wg(1, "s_tab0")
-        gather_v(1, "s_bf1")
-        w4_scale = slot([P, PASSES * H], U8, "w4_scale", "s_tab1")
-        nc.vector.tensor_copy(
-            out=w4_scale[:].rearrange("p (a t m) -> p a t m", a=PASSES, t=PACK),
-            in_=w4_plane[:].rearrange("p (a m t) -> p a t m", a=PASSES, t=PACK),
-        )
+            for lo, hi in ((0, S),) if a == 0 else CUTS:
+                nc.vector.tensor_copy(v_codes[a][:, lo:hi], tab[a][:].indirect(idx[:, lo // 16 : hi // 16]))
 
         bid_turned = bank(BANKS - 1)
         nc.tensor.transpose(bid_turned[:, 0:P], bid_rows[:], identity[:])
-        ln_bid = slot([P, TILES], F32, "ln_bid", "s_raw1")
+        ln_bid = fresh([P, TILES], F32, "ln_bid")
         nc.scalar.activation(out=ln_bid[:], in_=bid_turned[:, 0:TILES], func=ACT.Ln)
         warm_sigmoid = keep.tile([P, 1], F32, name="warm_sigmoid")
         nc.scalar.activation(out=warm_sigmoid[:], in_=ln_bid[:, 0:1], func=ACT.Sigmoid)
 
-        gate = [bank(t) for t in range(PACK)]
-        feat = [bank(PACK + t) for t in range(PACK)]
-        sigs = []
+        whole = round_wg(nc.scalar.copy, 0, 0, PACK, "s_bf0")
+        gather_v(0, "s_ts")
+        quantise_wg(whole, 0, 0, PACK, "s_tab0")
+        w4_codes = fresh([P, PASSES * 2 * H], U8, "w4_codes")
+        nc.vector.tensor_copy(
+            out=w4_codes[:].bitcast(U16).rearrange("p (a t m i) -> p a m t i", a=PASSES, t=PACK, i=8),
+            in_=w4_raw[:].bitcast(U16).rearrange("p (a m i t) -> p a m t i", a=PASSES, t=PACK, i=8),
+        )
+        w4_scale = slot([P, PASSES * H], U8, "w4_scale", "s_bf0")
+        nc.vector.tensor_copy(
+            out=w4_scale[:].rearrange("p (a t m i) -> p a m t i", a=PASSES, t=PACK, i=16),
+            in_=w4_plane[:].rearrange("p (a m i t) -> p a m t i", a=PASSES, t=PACK, i=16),
+        )
 
-        def gate_pass(t, a):
-            cols = slice(P * t, P * (t + 1))
+        low = round_wg(nc.scalar.copy, 1, 0, 2, "s_bf2")
+        high = round_wg(nc.scalar.copy, 1, 2, PACK, "s_bf1")
+        quantise_wg(low, 1, 0, 2, "s_w4s")
+        gather_v(1, "s_bf2")
+        quantise_wg(high, 1, 2, PACK, "s_tab1")
+
+        def gate_pass(acc, t, a, lo=0, hi=S):
             nc.tensor.matmul_mx(
-                out=gate[t][:],
-                lhsT=wg_codes[a][:, cols].bitcast(FP8X4), lhsT_scale=wg_scale[a][:, cols],
-                rhs=v_codes[a][:].bitcast(FP8X4), rhs_scale=v_scale[a][:],
+                out=acc[:, lo:hi],
+                lhsT=wg_codes[a, t].bitcast(FP8X4), lhsT_scale=wg_scale[a, t],
+                rhs=v_codes[a][:, lo:hi].bitcast(FP8X4), rhs_scale=v_scale[a][:, lo:hi],
                 start=(a == 0), stop=(a == PASSES - 1),
             )
 
-        def feat_pass(t, a):
+        def feat_pass(acc, t, a, lo=0, hi=S):
             c0 = a * H + P * t
-            nc.tensor.matmul_mx(
-                out=feat[t][:],
-                lhsT=w4_codes[:, 2 * c0 : 2 * (c0 + P)].bitcast(FP4X4),
-                lhsT_scale=w4_scale[:, c0 : c0 + P],
-                rhs=v_codes[a][:].bitcast(FP8X4), rhs_scale=v_scale[a][:],
-                start=(a == 0), stop=(a == PASSES - 1),
+            width = S if hi - lo == S else P
+            for n in range(lo, hi, width):
+                nc.tensor.matmul_mx(
+                    out=acc[:, n : n + width],
+                    lhsT=w4_codes[:, 2 * c0 : 2 * (c0 + P)].bitcast(FP4X4),
+                    lhsT_scale=w4_scale[:, c0 : c0 + P],
+                    rhs=v_codes[a][:, n : n + width].bitcast(FP8X4), rhs_scale=v_scale[a][:, n : n + width],
+                    start=(a == 0 and n == lo), stop=(a == PASSES - 1 and n + width == hi),
+                )
+
+        def on_piece(shape, dtype, name, c, shift=0):
+            return links.tile(shape, dtype, name=name, align_bytes=64, offset=2 * PACK * PIECES[c][0] + shift)
+
+        sigs = [
+            fresh([P, S], F32, "sig0"), fresh([P, S], F32, "sig1"),
+            on_piece([P, S], F32, "sig2", 0, 1024), on_piece([P, S], F32, "sig3", 2),
+        ]
+
+        def sigmoid(acc, t, lo=0, hi=S):
+            nc.scalar.activation(out=sigs[t][:, lo:hi], in_=acc[:, lo:hi], func=ACT.Sigmoid)
+
+        def weigh(h, acc, t, lo=0, hi=S):
+            nc.vector.tensor_tensor(h[:], acc[:, lo:hi], sigs[t][:, lo:hi], ALU.mult)
+
+        def put(h, t, lo=0, hi=S):
+            nc.vector.tensor_tensor(
+                page[t][:].indirect(idx3[:, lo // 16 : hi // 16]), h[:], wgs_of[t][:, lo:hi], ALU.mult
             )
 
-        for t in range(PACK):
-            gate_pass(t, 0)
-        for t in range(PACK):
-            gate_pass(t, 1)
-            sigs.append(slot([P, S], F32, "sig%d" % t, "s_sig%d" % t))
-            nc.scalar.activation(out=sigs[t][:], in_=gate[t][:], func=ACT.Sigmoid)
+        gate_cut = [bank(u) for u in range(2)]
+        feat_cut = [bank(2 + u) for u in range(2)]
+        gate, feat = {1: bank(4)}, {1: bank(5)}
+        for u, (lo, hi) in enumerate(CUTS):
+            gate_pass(gate_cut[u], 0, 0, lo, hi)
+        gate_pass(gate[1], 1, 0)
+        for u, (lo, hi) in enumerate(CUTS):
+            feat_pass(feat_cut[u], 0, 0, lo, hi)
+        feat_pass(feat[1], 1, 0)
+        h_cut = [slot([P, S // 2], F32, "h0_%d" % u, "s_h%d" % u) for u in range(2)]
+        for u, (lo, hi) in enumerate(CUTS):
+            gate_pass(gate_cut[u], 0, 1, lo, hi)
+            sigmoid(gate_cut[u], 0, lo, hi)
+            feat_pass(feat_cut[u], 0, 1, lo, hi)
+            weigh(h_cut[u], feat_cut[u], 0, lo, hi)
+        gate_pass(gate[1], 1, 1)
+        sigmoid(gate[1], 1)
+        feat_pass(feat[1], 1, 1)
+        for t in (2, 3):
+            gate[t] = bank(t - 2)
             for a in range(PASSES):
-                feat_pass(t, a)
+                gate_pass(gate[t], t, a)
+            sigmoid(gate[t], t)
+        for t in (2, 3):
+            feat[t] = bank(t)
+            for a in range(PASSES):
+                feat_pass(feat[t], t, a)
 
         half = S2 // 2
-
-        def on_piece(shape, dtype, name, c):
-            return links.tile(shape, dtype, name=name, align_bytes=64, offset=2 * PACK * PIECES[c][0])
-
-        warm_exp = on_piece([P, 2 * T2], F32, "warm_exp", 0)
-        nc.scalar.activation(out=warm_exp[:, 0:1], in_=sigs[PACK - 1][:, 0:1], func=ACT.Exp)
+        warm_exp = keep.tile([P, 1], F32, name="warm_exp")
+        nc.scalar.activation(out=warm_exp[:], in_=sigs[PACK - 1][:, 0:1], func=ACT.Exp)
 
         page_bf = [on_piece([P, hi - lo, PACK], BF16, "page_bf%d" % c, c) for c, (lo, hi) in enumerate(PIECES)]
-        hs = []
+        hs = {}
 
-        def product(t):
-            hs.append(slot([P, S], F32, "h%d" % t, ("s_h0", "s_h1", "s_h0", "s_wgs0")[t]))
-            nc.vector.tensor_tensor(hs[t][:], feat[t][:], sigs[t][:], ALU.mult)
+        def product(t, tag):
+            hs[t] = slot([P, S], F32, "h%d" % t, tag)
+            weigh(hs[t], feat[t], t)
 
+        put(h_cut[0], 0, *CUTS[0])
+        product(1, "s_h0")
+        put(h_cut[1], 0, *CUTS[1])
+        product(2, "s_wgs0")
+        product(3, "s_h1")
         for t in range(PACK):
-            for ahead in ((0, 1), (2, 3), (), ())[t]:
-                product(ahead)
-            nc.vector.tensor_tensor(page[t][:].indirect(idx3[:]), hs[t][:], wgs_of[t], ALU.mult)
+            if t > 0:
+                put(hs[t], t)
             for c, (lo, hi) in enumerate(PIECES):
                 nc.scalar.copy(out=page_bf[c][:, :, t], in_=page[t][:, lo:hi])
 

@@ -25,7 +25,7 @@ BANKS = 8
 TILES = S2 // P
 HALVES = T2 // BANK
 CUTS = ((0, S // 2), (S // 2, S))
-PIECES = ((0, 256), (256, 512), (512, 1024))
+PIECES = ((0, 256), (256, 512), (512, 768), (768, 1024))
 
 
 def load_scale_rows(queue, plane, scales, row):
@@ -84,9 +84,9 @@ def tile_list_auction_slot_scores_kernel(
         def load_page(t):
             nc.sync.dma_start(out=page[t][:], in_=page_rows[t])
 
-        def load_wgs(tile, first, last):
+        def load_wgs(tile, lo, hi):
             for q in (0, 2, 1, 3):
-                nc.sync.dma_start(out=tile[32 * q : 32 * (q + 1), :], in_=wgs_rows[:, S * first : S * last])
+                nc.sync.dma_start(out=tile[32 * q : 32 * (q + 1), :], in_=wgs_rows[:, lo:hi])
 
         w4_raw = slot([P, PASSES * 2 * H], U8, "w4_raw", "s_w4r")
         wg_raw = [slot([P, PACK, H], F32, "wg_raw%d" % a, "s_raw%d" % a) for a in range(PASSES)]
@@ -94,10 +94,10 @@ def tile_list_auction_slot_scores_kernel(
         page_rows = page0.rearrange("(p t) c -> t p c", t=PACK)
         page = [keep.tile([P, T2], F32, name="page%d" % t) for t in range(PACK)]
         wgs_rows = wgs.rearrange("(p t) j -> p (t j)", t=PACK)
-        wgs_first = slot([P, S], F32, "wgs_first", "s_wgs0")
+        wgs_cut = [slot([P, S // 2], F32, "wgs0_%d" % u, "s_wgs0_%d" % u) for u in range(2)]
         wgs_second = slot([P, S], F32, "wgs_second", "s_wgs1")
         wgs_rest = slot([P, 2 * S], F32, "wgs_rest", "s_wgs")
-        wgs_of = [wgs_first[:], wgs_second[:], wgs_rest[:, 0:S], wgs_rest[:, S : 2 * S]]
+        wgs_of = {1: wgs_second[:], 2: wgs_rest[:, 0:S], 3: wgs_rest[:, S : 2 * S]}
         tab2 = slot([P, T3], U32, "tab2", "s_tab2")
         reserve_sb = [keep.tile([P, 4, PICKS], F32, name="reserve%d" % u) for u in range(2)]
 
@@ -115,15 +115,16 @@ def tile_list_auction_slot_scores_kernel(
         load_scale_rows(nc.sync, w4_plane, w4_scales, 0)
         load_wg(1)
         load_words(tab[1], tab_words[1])
-        load_page(0)
-        load_wgs(wgs_first, 0, 1)
         nc.sync.dma_start(idx3[:], offs3)
+        load_page(0)
+        for u, (lo, hi) in enumerate(CUTS):
+            load_wgs(wgs_cut[u], lo, hi)
         load_page(1)
-        load_wgs(wgs_second, 1, 2)
-        load_page(2)
-        load_wgs(wgs_rest, 2, PACK)
+        load_wgs(wgs_second, S, 2 * S)
         load_words(tab2, tab2_words[0])
+        load_page(2)
         load_page(3)
+        load_wgs(wgs_rest, 2 * S, PACK * S)
         nc.sync.dma_start(idx4[:], offs4)
         for u in range(2):
             nc.sync.dma_start(
@@ -188,10 +189,10 @@ def tile_list_auction_slot_scores_kernel(
             in_=w4_plane[:].rearrange("p (a m i t) -> p a m t i", a=PASSES, t=PACK, i=16),
         )
 
-        low = round_wg(nc.scalar.copy, 1, 0, 2, "s_bf2")
+        low = round_wg(nc.vector.tensor_copy, 1, 0, 2, "s_w4s")
         high = round_wg(nc.scalar.copy, 1, 2, PACK, "s_bf1")
-        quantise_wg(low, 1, 0, 2, "s_w4s")
-        gather_v(1, "s_bf2")
+        quantise_wg(low, 1, 0, 2, "s_wc1")
+        gather_v(1, "s_w4s")
         quantise_wg(high, 1, 2, PACK, "s_tab1")
 
         def gate_pass(acc, t, a, lo=0, hi=S):
@@ -214,12 +215,12 @@ def tile_list_auction_slot_scores_kernel(
                     start=(a == 0 and n == lo), stop=(a == PASSES - 1 and n + width == hi),
                 )
 
-        def on_piece(shape, dtype, name, c, shift=0):
-            return links.tile(shape, dtype, name=name, align_bytes=64, offset=2 * PACK * PIECES[c][0] + shift)
+        def on_piece(shape, dtype, name, c):
+            return links.tile(shape, dtype, name=name, align_bytes=64, offset=2 * PACK * PIECES[c][0])
 
         sigs = [
             fresh([P, S], F32, "sig0"), fresh([P, S], F32, "sig1"),
-            on_piece([P, S], F32, "sig2", 0, 1024), on_piece([P, S], F32, "sig3", 2),
+            fresh([P, S], F32, "sig2"), fresh([P, S], F32, "sig3"),
         ]
 
         def sigmoid(acc, t, lo=0, hi=S):
@@ -228,10 +229,8 @@ def tile_list_auction_slot_scores_kernel(
         def weigh(h, acc, t, lo=0, hi=S):
             nc.vector.tensor_tensor(h[:], acc[:, lo:hi], sigs[t][:, lo:hi], ALU.mult)
 
-        def put(h, t, lo=0, hi=S):
-            nc.vector.tensor_tensor(
-                page[t][:].indirect(idx3[:, lo // 16 : hi // 16]), h[:], wgs_of[t][:, lo:hi], ALU.mult
-            )
+        def put(h, factors, t, lo=0, hi=S):
+            nc.vector.tensor_tensor(page[t][:].indirect(idx3[:, lo // 16 : hi // 16]), h[:], factors, ALU.mult)
 
         gate_cut = [bank(u) for u in range(2)]
         feat_cut = [bank(2 + u) for u in range(2)]
@@ -272,19 +271,20 @@ def tile_list_auction_slot_scores_kernel(
             hs[t] = slot([P, S], F32, "h%d" % t, tag)
             weigh(hs[t], feat[t], t)
 
-        put(h_cut[0], 0, *CUTS[0])
+        put(h_cut[0], wgs_cut[0][:], 0, *CUTS[0])
         product(1, "s_h0")
-        put(h_cut[1], 0, *CUTS[1])
-        product(2, "s_wgs0")
+        put(h_cut[1], wgs_cut[1][:], 0, *CUTS[1])
+        product(2, "s_wgs0_1")
         product(3, "s_h1")
         for t in range(PACK):
             if t > 0:
-                put(hs[t], t)
+                put(hs[t], wgs_of[t], t)
             for c, (lo, hi) in enumerate(PIECES):
-                nc.scalar.copy(out=page_bf[c][:, :, t], in_=page[t][:, lo:hi])
+                if t < 2 or c < 3:
+                    nc.scalar.copy(out=page_bf[c][:, :, t], in_=page[t][:, lo:hi])
 
         v2_codes = []
-        page_codes = [keep.tile([P, BANK], U32, name="page_codes0", align_bytes=64), slot([P, BANK], U32, "page_codes1", "s_tab2")]
+        page_codes = [keep.tile([P, BANK], U32, name="page_codes0", align_bytes=64), fresh([P, BANK], U32, "page_codes1")]
         page_scale = [keep.tile([P, BANK], U8, name="page_scale%d" % c, align_bytes=64) for c in range(HALVES)]
 
         def gather_v2(u, codes):
@@ -301,9 +301,12 @@ def tile_list_auction_slot_scores_kernel(
 
         gather_v2(0, slot([P, half], U32, "v2_codes0", "s_wgs"))
         quantise_page(0)
+        for t in (2, 3):
+            nc.vector.tensor_copy(out=page_bf[3][:, :, t], in_=page[t][:, PIECES[3][0] : PIECES[3][1]])
         quantise_page(1)
-        gather_v2(1, on_piece([P, half], U32, "v2_codes1", 1))
+        quantise_page(3)
         quantise_page(2)
+        gather_v2(1, on_piece([P, half], U32, "v2_codes1", 2))
 
         picked, scores = {}, {}
 
@@ -312,17 +315,17 @@ def tile_list_auction_slot_scores_kernel(
 
         def score(i, c):
             if c == 0:
-                scores[i] = on_piece([P, T2], F32, "e2", 2) if i == 2 else slot([P, T2], F32, "e%d" % i, "s_e%d" % (i % 4))
+                scores[i] = slot([P, T2], F32, "e%d" % i, "s_tab2" if i == 1 else "s_e%d" % (i % 4))
             acc = bank(4 * c + i % 4)
             entries = slice((i % 4) * P, (i % 4 + 1) * P)
-            for lo, hi in PIECES[:2] if (i, c) == (0, 0) else ((0, BANK),):
+            for lo, hi in (PIECES[:2], PIECES[1::-1])[c] if i == 0 else ((0, BANK),):
                 nc.tensor.matmul_mx(
                     out=acc[:, lo:hi],
                     lhsT=v2_codes[i // 4][:, entries].bitcast(FP8X4), lhsT_scale=v2_scale[:, i * P : (i + 1) * P],
                     rhs=page_codes[c][:, lo:hi].bitcast(FP8X4), rhs_scale=page_scale[c][:, lo:hi],
                     start=True, stop=True,
                 )
-            empty = nc.vector.tensor_copy if (i, c) in ((2, 0), (1, 1), (5, 1)) else nc.scalar.copy
+            empty = nc.vector.tensor_copy if (i, c) in ((1, 0), (3, 1), (5, 1)) else nc.scalar.copy
             empty(out=scores[i][:, c * BANK : (c + 1) * BANK], in_=acc[:])
 
         def pick(i):
@@ -346,18 +349,19 @@ def tile_list_auction_slot_scores_kernel(
                 nc.sync.dma_start(out=out[i * P : (i + 1) * P, lo:hi], in_=res[:])
 
         for c in range(HALVES):
-            for i in range(3):
+            for i in range(2):
                 score(i, c)
         for c in range(HALVES):
-            score(3, c)
+            score(2, c)
+        score(3, 0)
         pick(0)
-        rest = [(i, c) for i in range(4, TILES) for c in range(HALVES)]
+        rest = [(3, 1)] + [(i, c) for i in range(4, TILES) for c in range(HALVES)]
         taken = 0
         for i in range(TILES):
             if i + 1 < TILES:
                 pick(i + 1)
             back(i)
-            count = {3: 2, 4: 3}.get(i, 1)
+            count = {0: 2, 2: 3, 4: 2}.get(i, 1)
             for tile, c in rest[taken : taken + count]:
                 score(tile, c)
             taken = taken + count

@@ -24,6 +24,7 @@ BANK = 512
 BANKS = 8
 TILES = S2 // P
 HALVES = T2 // BANK
+ORDER = (2, 0, 1, 3)
 CUTS = ((0, S // 2), (S // 2, S))
 PIECES = ((0, 256), (256, 512), (512, 768), (768, 1024))
 
@@ -65,8 +66,8 @@ def tile_list_auction_slot_scores_kernel(
         one = keep.tile([P, 1], F32, name="one")
         bid_rows = keep.tile([P, P], F32, name="bid_rows")
         identity = keep.tile([P, P], F32, name="identity")
-        for plane in (tab2_plane, tab_plane):
-            nc.vector.memset(plane[:].bitcast(I32), 0)
+        nc.gpsimd.memset(tab2_plane[:].bitcast(I32), 0)
+        nc.vector.memset(tab_plane[:].bitcast(I32), 0)
         nc.gpsimd.memset(one[:], 1.0)
         nc.gpsimd.memset(bid_rows[:], 0.0)
         nc.gpsimd.memset(w4_plane[:].bitcast(I32), 0)
@@ -84,47 +85,47 @@ def tile_list_auction_slot_scores_kernel(
         def load_page(t):
             nc.sync.dma_start(out=page[t][:], in_=page_rows[t])
 
-        def load_wgs(tile, lo, hi):
+        def load_wgs(tile, rows):
             for q in (0, 2, 1, 3):
-                nc.sync.dma_start(out=tile[32 * q : 32 * (q + 1), :], in_=wgs_rows[:, lo:hi])
+                nc.sync.dma_start(out=tile[32 * q : 32 * (q + 1)], in_=rows)
 
         w4_raw = slot([P, PASSES * 2 * H], U8, "w4_raw", "s_w4r")
         wg_raw = [slot([P, PACK, H], F32, "wg_raw%d" % a, "s_raw%d" % a) for a in range(PASSES)]
         tab = [slot([P, T], U32, "tab%d" % a, "s_tab%d" % a) for a in range(PASSES)]
         page_rows = page0.rearrange("(p t) c -> t p c", t=PACK)
         page = [keep.tile([P, T2], F32, name="page%d" % t) for t in range(PACK)]
-        wgs_rows = wgs.rearrange("(p t) j -> p (t j)", t=PACK)
-        wgs_cut = [slot([P, S // 2], F32, "wgs0_%d" % u, "s_wgs0_%d" % u) for u in range(2)]
+        first, second, third, last = ORDER
+        wgs_rows = wgs.rearrange("(p t) j -> p t j", t=PACK)
+        wgs_first = slot([P, S], F32, "wgs_first", "s_wgs0")
         wgs_second = slot([P, S], F32, "wgs_second", "s_wgs1")
-        wgs_rest = slot([P, 2 * S], F32, "wgs_rest", "s_wgs")
-        wgs_of = {1: wgs_second[:], 2: wgs_rest[:, 0:S], 3: wgs_rest[:, S : 2 * S]}
+        wgs_rest = slot([P, 2, S], F32, "wgs_rest", "s_wgs")
+        wgs_of = {second: wgs_second[:], third: wgs_rest[:, 0, :], last: wgs_rest[:, 1, :]}
         tab2 = slot([P, T3], U32, "tab2", "s_tab2")
         reserve_sb = [keep.tile([P, 4, PICKS], F32, name="reserve%d" % u) for u in range(2)]
 
-        nc.sync.dma_start(idx2[:], offs2)
-        nc.sync.dma_start(idx[:], offs)
         nc.sync.dma_start(
             out=w4_raw[:].bitcast(I32).rearrange("p (a n) -> p a n", a=PASSES),
             in_=w4_words.bitcast(I32).rearrange("a p n -> p a n"),
         )
+        nc.sync.dma_start(idx2[:], offs2)
+        nc.sync.dma_start(idx[:], offs)
         nc.sync.dma_start(out=tab2_plane[0:P:8, :].bitcast(I32), in_=tab2_scales[0].bitcast(I32))
-        nc.sync.dma_start(out=bid_rows[0:TILES, :], in_=bid.rearrange("(i p) -> i p", p=P))
         load_wg(0)
         load_scale_rows(nc.sync, tab_plane, tab_scales, 0)
         load_words(tab[0], tab_words[0])
+        nc.sync.dma_start(out=bid_rows[0:TILES, :], in_=bid.rearrange("(i p) -> i p", p=P))
         load_scale_rows(nc.sync, w4_plane, w4_scales, 0)
         load_wg(1)
         load_words(tab[1], tab_words[1])
         nc.sync.dma_start(idx3[:], offs3)
-        load_page(0)
-        for u, (lo, hi) in enumerate(CUTS):
-            load_wgs(wgs_cut[u], lo, hi)
-        load_page(1)
-        load_wgs(wgs_second, S, 2 * S)
+        load_page(first)
+        load_wgs(wgs_first, wgs_rows[:, first, :])
+        load_page(second)
+        load_wgs(wgs_second, wgs_rows[:, second, :])
+        load_page(third)
+        load_wgs(wgs_rest, wgs_rows[:, third : PACK : last - third, :])
         load_words(tab2, tab2_words[0])
-        load_page(2)
-        load_page(3)
-        load_wgs(wgs_rest, 2 * S, PACK * S)
+        load_page(last)
         nc.sync.dma_start(idx4[:], offs4)
         for u in range(2):
             nc.sync.dma_start(
@@ -135,31 +136,36 @@ def tile_list_auction_slot_scores_kernel(
         def fresh(shape, dtype, name):
             return keep.tile(shape, dtype, name=name, align_bytes=64)
 
-        v2_rows = fresh([P, S2], U8, "v2_rows")
+        w4_codes = fresh([P, PASSES * 2 * H], U8, "w4_codes")
+        nc.vector.tensor_copy(
+            out=w4_codes[:].bitcast(U16).rearrange("p (a t m i) -> p a m t i", a=PASSES, t=PACK, i=8),
+            in_=w4_raw[:].bitcast(U16).rearrange("p (a m i t) -> p a m t i", a=PASSES, t=PACK, i=8),
+        )
+        v2_rows = slot([P, S2], U8, "v2_rows", "s_w4r")
         nc.vector.tensor_copy(v2_rows[:], tab2_plane[:].indirect(idx2[:]))
         for r in range(4):
             nc.sync.dma_start(out=v2_scale[r:P:32, :].bitcast(I32), in_=v2_rows[8 * r : P : 32, :].bitcast(I32))
-        v_scale = [fresh([P, S], U8, "v_scale%d" % a) for a in range(PASSES)]
+        v_scale = [slot([P, S], U8, "v_scale%d" % a, ("s_t2s", "s_vs1")[a]) for a in range(PASSES)]
         for a in range(PASSES):
             nc.vector.tensor_copy(v_scale[a][:], tab_plane[:, a * T : (a + 1) * T].indirect(idx[:]))
 
         wg_codes, wg_scale = {}, {}
         v_codes = []
 
-        def round_wg(copy, a, first, last, tag):
-            wg_bf = slot([P, (last - first) * P * PACK], BF16, "wg_bf%d_%d" % (a, first), tag)
+        def round_wg(copy, a, t0, t1, tag):
+            wg_bf = slot([P, (t1 - t0) * P * PACK], BF16, "wg_bf%d_%d" % (a, t0), tag)
             copy(
                 out=wg_bf[:].rearrange("p (t m j) -> p m t j", m=P, j=PACK),
-                in_=wg_raw[a][:].rearrange("p j (m t) -> p m t j", t=PACK)[:, :, first:last, :],
+                in_=wg_raw[a][:].rearrange("p j (m t) -> p m t j", t=PACK)[:, :, t0:t1, :],
             )
             return wg_bf
 
-        def quantise_wg(wg_bf, a, first, last, tag):
-            codes = slot([P, P * (last - first)], U32, "wg_codes%d_%d" % (a, first), tag)
-            scale = fresh([P, P * (last - first)], U8, "wg_scale%d_%d" % (a, first))
+        def quantise_wg(wg_bf, a, t0, t1, tag):
+            codes = slot([P, P * (t1 - t0)], U32, "wg_codes%d_%d" % (a, t0), tag)
+            scale = fresh([P, P * (t1 - t0)], U8, "wg_scale%d_%d" % (a, t0))
             nc.vector.quantize_mx(out=codes[:].bitcast(FP8X4), scales=scale[:], in_=wg_bf[:])
-            for t in range(first, last):
-                cols = slice(P * (t - first), P * (t - first + 1))
+            for t in range(t0, t1):
+                cols = slice(P * (t - t0), P * (t - t0 + 1))
                 wg_codes[a, t] = codes[:, cols]
                 wg_scale[a, t] = scale[:, cols]
 
@@ -168,6 +174,15 @@ def tile_list_auction_slot_scores_kernel(
             for lo, hi in ((0, S),) if a == 0 else CUTS:
                 nc.vector.tensor_copy(v_codes[a][:, lo:hi], tab[a][:].indirect(idx[:, lo // 16 : hi // 16]))
 
+        whole = round_wg(nc.scalar.copy, 0, 0, PACK, "s_bf0")
+        gather_v(0, "s_ts")
+        quantise_wg(whole, 0, 0, PACK, "s_tab0")
+        w4_scale = slot([P, PASSES * H], U8, "w4_scale", "s_bf0")
+        nc.vector.tensor_copy(
+            out=w4_scale[:].rearrange("p (a t m i) -> p a m t i", a=PASSES, t=PACK, i=16),
+            in_=w4_plane[:].rearrange("p (a m i t) -> p a m t i", a=PASSES, t=PACK, i=16),
+        )
+
         bid_turned = bank(BANKS - 1)
         nc.tensor.transpose(bid_turned[:, 0:P], bid_rows[:], identity[:])
         ln_bid = fresh([P, TILES], F32, "ln_bid")
@@ -175,25 +190,11 @@ def tile_list_auction_slot_scores_kernel(
         warm_sigmoid = keep.tile([P, 1], F32, name="warm_sigmoid")
         nc.scalar.activation(out=warm_sigmoid[:], in_=ln_bid[:, 0:1], func=ACT.Sigmoid)
 
-        whole = round_wg(nc.scalar.copy, 0, 0, PACK, "s_bf0")
-        gather_v(0, "s_ts")
-        quantise_wg(whole, 0, 0, PACK, "s_tab0")
-        w4_codes = fresh([P, PASSES * 2 * H], U8, "w4_codes")
-        nc.vector.tensor_copy(
-            out=w4_codes[:].bitcast(U16).rearrange("p (a t m i) -> p a m t i", a=PASSES, t=PACK, i=8),
-            in_=w4_raw[:].bitcast(U16).rearrange("p (a m i t) -> p a m t i", a=PASSES, t=PACK, i=8),
-        )
-        w4_scale = slot([P, PASSES * H], U8, "w4_scale", "s_bf0")
-        nc.vector.tensor_copy(
-            out=w4_scale[:].rearrange("p (a t m i) -> p a m t i", a=PASSES, t=PACK, i=16),
-            in_=w4_plane[:].rearrange("p (a m i t) -> p a m t i", a=PASSES, t=PACK, i=16),
-        )
-
-        low = round_wg(nc.vector.tensor_copy, 1, 0, 2, "s_w4s")
-        high = round_wg(nc.scalar.copy, 1, 2, PACK, "s_bf1")
-        quantise_wg(low, 1, 0, 2, "s_wc1")
+        high = round_wg(nc.vector.tensor_copy, 1, 2, PACK, "s_w4s")
+        low = round_wg(nc.scalar.copy, 1, 0, 2, "s_bf1")
+        quantise_wg(high, 1, 2, PACK, "s_wc1")
         gather_v(1, "s_w4s")
-        quantise_wg(high, 1, 2, PACK, "s_tab1")
+        quantise_wg(low, 1, 0, 2, "s_tab1")
 
         def gate_pass(acc, t, a, lo=0, hi=S):
             nc.tensor.matmul_mx(
@@ -234,35 +235,35 @@ def tile_list_auction_slot_scores_kernel(
 
         gate_cut = [bank(u) for u in range(2)]
         feat_cut = [bank(2 + u) for u in range(2)]
-        gate, feat = {1: bank(4)}, {1: bank(5)}
+        gate, feat = {second: bank(4)}, {second: bank(5)}
         for u, (lo, hi) in enumerate(CUTS):
-            gate_pass(gate_cut[u], 0, 0, lo, hi)
-        gate_pass(gate[1], 1, 0)
+            gate_pass(gate_cut[u], first, 0, lo, hi)
+        gate_pass(gate[second], second, 0)
         for u, (lo, hi) in enumerate(CUTS):
-            feat_pass(feat_cut[u], 0, 0, lo, hi)
-        feat_pass(feat[1], 1, 0)
-        h_cut = [slot([P, S // 2], F32, "h0_%d" % u, "s_h%d" % u) for u in range(2)]
+            feat_pass(feat_cut[u], first, 0, lo, hi)
+        feat_pass(feat[second], second, 0)
+        h_cut = [slot([P, S // 2], F32, "h_cut%d" % u, "s_h%d" % u) for u in range(2)]
         for u, (lo, hi) in enumerate(CUTS):
-            gate_pass(gate_cut[u], 0, 1, lo, hi)
-            sigmoid(gate_cut[u], 0, lo, hi)
-            feat_pass(feat_cut[u], 0, 1, lo, hi)
-            weigh(h_cut[u], feat_cut[u], 0, lo, hi)
-        gate_pass(gate[1], 1, 1)
-        sigmoid(gate[1], 1)
-        feat_pass(feat[1], 1, 1)
-        for t in (2, 3):
-            gate[t] = bank(t - 2)
+            gate_pass(gate_cut[u], first, 1, lo, hi)
+            sigmoid(gate_cut[u], first, lo, hi)
+            feat_pass(feat_cut[u], first, 1, lo, hi)
+            weigh(h_cut[u], feat_cut[u], first, lo, hi)
+        gate_pass(gate[second], second, 1)
+        sigmoid(gate[second], second)
+        feat_pass(feat[second], second, 1)
+        for u, t in enumerate((third, last)):
+            gate[t] = bank(u)
             for a in range(PASSES):
                 gate_pass(gate[t], t, a)
             sigmoid(gate[t], t)
-        for t in (2, 3):
-            feat[t] = bank(t)
+        for u, t in enumerate((third, last)):
+            feat[t] = bank(2 + u)
             for a in range(PASSES):
                 feat_pass(feat[t], t, a)
 
         half = S2 // 2
         warm_exp = keep.tile([P, 1], F32, name="warm_exp")
-        nc.scalar.activation(out=warm_exp[:], in_=sigs[PACK - 1][:, 0:1], func=ACT.Exp)
+        nc.scalar.activation(out=warm_exp[:], in_=sigs[last][:, 0:1], func=ACT.Exp)
 
         page_bf = [on_piece([P, hi - lo, PACK], BF16, "page_bf%d" % c, c) for c, (lo, hi) in enumerate(PIECES)]
         hs = {}
@@ -271,17 +272,21 @@ def tile_list_auction_slot_scores_kernel(
             hs[t] = slot([P, S], F32, "h%d" % t, tag)
             weigh(hs[t], feat[t], t)
 
-        put(h_cut[0], wgs_cut[0][:], 0, *CUTS[0])
-        product(1, "s_h0")
-        put(h_cut[1], wgs_cut[1][:], 0, *CUTS[1])
-        product(2, "s_wgs0_1")
-        product(3, "s_h1")
-        for t in range(PACK):
-            if t > 0:
+        def round_page(copy, t, c):
+            lo, hi = PIECES[c]
+            copy(out=page_bf[c][:, :, t], in_=page[t][:, lo:hi])
+
+        put(h_cut[0], wgs_first[:, 0 : S // 2], first, *CUTS[0])
+        product(second, "s_h0")
+        put(h_cut[1], wgs_first[:, S // 2 : S], first, *CUTS[1])
+        product(third, "s_wgs0")
+        product(last, "s_h1")
+        round_page(nc.vector.tensor_copy, first, 3)
+        for t in ORDER:
+            if t != first:
                 put(hs[t], wgs_of[t], t)
-            for c, (lo, hi) in enumerate(PIECES):
-                if t < 2 or c < 3:
-                    nc.scalar.copy(out=page_bf[c][:, :, t], in_=page[t][:, lo:hi])
+            for c in range(3 if t in (first, last) else 4):
+                round_page(nc.scalar.copy, t, c)
 
         v2_codes = []
         page_codes = [keep.tile([P, BANK], U32, name="page_codes0", align_bytes=64), fresh([P, BANK], U32, "page_codes1")]
@@ -301,8 +306,7 @@ def tile_list_auction_slot_scores_kernel(
 
         gather_v2(0, slot([P, half], U32, "v2_codes0", "s_wgs"))
         quantise_page(0)
-        for t in (2, 3):
-            nc.vector.tensor_copy(out=page_bf[3][:, :, t], in_=page[t][:, PIECES[3][0] : PIECES[3][1]])
+        round_page(nc.vector.tensor_copy, last, 3)
         quantise_page(1)
         quantise_page(3)
         quantise_page(2)

@@ -59,10 +59,11 @@ def tile_list_auction_slot_scores_kernel(
         def bank(k):
             return psum.tile([P, BANK], F32, name="bank%d" % k, tag="bank%d" % k)
 
-        tab_plane = slot([P, PASSES * T], U8, "tab_plane", "s_ts")
+        tab_plane = slot([P, T], U8, "tab_plane", "s_ts")
         w4_plane = slot([P, PASSES * H], U8, "w4_plane", "s_w4s")
         tab2_plane = slot([P, T3], U8, "tab2_plane", "s_t2s")
         v2_scale = keep.tile([P, S2], U8, name="v2_scale", align_bytes=64)
+        v_late = keep.tile([P, S], U8, name="v_late", align_bytes=64)
         one = keep.tile([P, 1], F32, name="one")
         bid_rows = keep.tile([P, P], F32, name="bid_rows")
         identity = keep.tile([P, P], F32, name="identity")
@@ -72,6 +73,7 @@ def tile_list_auction_slot_scores_kernel(
         nc.gpsimd.memset(bid_rows[:], 0.0)
         nc.gpsimd.memset(w4_plane[:].bitcast(I32), 0)
         make_identity(nc, identity[:])
+        nc.gpsimd.memset(v_late[:].bitcast(I32), 0)
         nc.gpsimd.memset(v2_scale[:].bitcast(I32), 0)
         warm_ln = keep.tile([P, 1], F32, name="warm_ln")
         nc.scalar.activation(out=warm_ln[:], in_=one[:], func=ACT.Ln)
@@ -96,7 +98,7 @@ def tile_list_auction_slot_scores_kernel(
         page = [keep.tile([P, T2], F32, name="page%d" % t) for t in range(PACK)]
         first, second, third, last = ORDER
         wgs_rows = wgs.rearrange("(p t) j -> p t j", t=PACK)
-        wgs_first = slot([P, S], F32, "wgs_first", "s_wgs0")
+        wgs_cut = [slot([P, S // 2], F32, "wgs_cut%d" % u, "s_wgs0_%d" % u) for u in range(2)]
         wgs_second = slot([P, S], F32, "wgs_second", "s_wgs1")
         wgs_rest = slot([P, 2, S], F32, "wgs_rest", "s_wgs")
         wgs_of = {second: wgs_second[:], third: wgs_rest[:, 0, :], last: wgs_rest[:, 1, :]}
@@ -111,7 +113,8 @@ def tile_list_auction_slot_scores_kernel(
         nc.sync.dma_start(idx[:], offs)
         nc.sync.dma_start(out=tab2_plane[0:P:8, :].bitcast(I32), in_=tab2_scales[0].bitcast(I32))
         load_wg(0)
-        load_scale_rows(nc.sync, tab_plane, tab_scales, 0)
+        load_scale_rows(nc.sync, tab_plane, tab_scales[0:1], 0)
+        nc.sync.dma_start(out=tab_plane[4:P:8, :].bitcast(I32), in_=tab_scales[1].bitcast(I32))
         load_words(tab[0], tab_words[0])
         nc.sync.dma_start(out=bid_rows[0:TILES, :], in_=bid.rearrange("(i p) -> i p", p=P))
         load_scale_rows(nc.sync, w4_plane, w4_scales, 0)
@@ -119,8 +122,9 @@ def tile_list_auction_slot_scores_kernel(
         load_words(tab[1], tab_words[1])
         nc.sync.dma_start(idx3[:], offs3)
         load_page(first)
-        load_wgs(wgs_first, wgs_rows[:, first, :])
+        load_wgs(wgs_cut[0], wgs_rows[:, first, 0 : S // 2])
         load_page(second)
+        load_wgs(wgs_cut[1], wgs_rows[:, first, S // 2 : S])
         load_wgs(wgs_second, wgs_rows[:, second, :])
         load_page(third)
         load_wgs(wgs_rest, wgs_rows[:, third : PACK : last - third, :])
@@ -145,9 +149,10 @@ def tile_list_auction_slot_scores_kernel(
         nc.vector.tensor_copy(v2_rows[:], tab2_plane[:].indirect(idx2[:]))
         for r in range(4):
             nc.sync.dma_start(out=v2_scale[r:P:32, :].bitcast(I32), in_=v2_rows[8 * r : P : 32, :].bitcast(I32))
-        v_scale = [slot([P, S], U8, "v_scale%d" % a, ("s_t2s", "s_vs1")[a]) for a in range(PASSES)]
-        for a in range(PASSES):
-            nc.vector.tensor_copy(v_scale[a][:], tab_plane[:, a * T : (a + 1) * T].indirect(idx[:]))
+        v_scale = [slot([P, S], U8, "v_rows", "s_t2s"), v_late]
+        nc.vector.tensor_copy(v_scale[0][:], tab_plane[:].indirect(idx[:]))
+        for r in range(4):
+            nc.gpsimd.dma_start(out=v_late[r:P:32, :].bitcast(I32), in_=v_scale[0][8 * r + 4 : P : 32, :].bitcast(I32))
 
         wg_codes, wg_scale = {}, {}
         v_codes = []
@@ -276,10 +281,10 @@ def tile_list_auction_slot_scores_kernel(
             lo, hi = PIECES[c]
             copy(out=page_bf[c][:, :, t], in_=page[t][:, lo:hi])
 
-        put(h_cut[0], wgs_first[:, 0 : S // 2], first, *CUTS[0])
+        put(h_cut[0], wgs_cut[0][:], first, *CUTS[0])
         product(second, "s_h0")
-        put(h_cut[1], wgs_first[:, S // 2 : S], first, *CUTS[1])
-        product(third, "s_wgs0")
+        put(h_cut[1], wgs_cut[1][:], first, *CUTS[1])
+        product(third, "s_wgs0_1")
         product(last, "s_h1")
         round_page(nc.vector.tensor_copy, first, 3)
         for t in ORDER:

@@ -63,17 +63,17 @@ def tile_list_auction_slot_scores_kernel(
         w4_plane = slot([P, PASSES * H], U8, "w4_plane", "s_w4s")
         tab2_plane = slot([P, T3], U8, "tab2_plane", "s_t2s")
         v2_scale = keep.tile([P, S2], U8, name="v2_scale", align_bytes=64)
-        v_late = keep.tile([P, S], U8, name="v_late", align_bytes=64)
+        v_early = keep.tile([P, S], U8, name="v_early", align_bytes=64)
         one = keep.tile([P, 1], F32, name="one")
         bid_rows = keep.tile([P, P], F32, name="bid_rows")
         identity = keep.tile([P, P], F32, name="identity")
-        nc.gpsimd.memset(tab2_plane[:].bitcast(I32), 0)
-        nc.vector.memset(tab_plane[:].bitcast(I32), 0)
+        nc.gpsimd.memset(tab_plane[:].bitcast(I32), 0)
+        nc.vector.memset(tab2_plane[:].bitcast(I32), 0)
         nc.gpsimd.memset(one[:], 1.0)
         nc.gpsimd.memset(bid_rows[:], 0.0)
         nc.gpsimd.memset(w4_plane[:].bitcast(I32), 0)
         make_identity(nc, identity[:])
-        nc.gpsimd.memset(v_late[:].bitcast(I32), 0)
+        nc.gpsimd.memset(v_early[:].bitcast(I32), 0)
         nc.gpsimd.memset(v2_scale[:].bitcast(I32), 0)
         warm_ln = keep.tile([P, 1], F32, name="warm_ln")
         nc.scalar.activation(out=warm_ln[:], in_=one[:], func=ACT.Ln)
@@ -111,10 +111,10 @@ def tile_list_auction_slot_scores_kernel(
         )
         nc.sync.dma_start(idx2[:], offs2)
         nc.sync.dma_start(idx[:], offs)
-        nc.sync.dma_start(out=tab2_plane[0:P:8, :].bitcast(I32), in_=tab2_scales[0].bitcast(I32))
+        for a in range(PASSES):
+            nc.sync.dma_start(out=tab_plane[4 - 4 * a : P : 8, :].bitcast(I32), in_=tab_scales[a].bitcast(I32))
         load_wg(0)
-        load_scale_rows(nc.sync, tab_plane, tab_scales[0:1], 0)
-        nc.sync.dma_start(out=tab_plane[4:P:8, :].bitcast(I32), in_=tab_scales[1].bitcast(I32))
+        nc.sync.dma_start(out=tab2_plane[0:P:8, :].bitcast(I32), in_=tab2_scales[0].bitcast(I32))
         load_words(tab[0], tab_words[0])
         nc.sync.dma_start(out=bid_rows[0:TILES, :], in_=bid.rearrange("(i p) -> i p", p=P))
         load_scale_rows(nc.sync, w4_plane, w4_scales, 0)
@@ -145,14 +145,19 @@ def tile_list_auction_slot_scores_kernel(
             out=w4_codes[:].bitcast(U16).rearrange("p (a t m i) -> p a m t i", a=PASSES, t=PACK, i=8),
             in_=w4_raw[:].bitcast(U16).rearrange("p (a m i t) -> p a m t i", a=PASSES, t=PACK, i=8),
         )
-        v2_rows = slot([P, S2], U8, "v2_rows", "s_w4r")
+        v_rows = slot([P, S], U8, "v_rows", "s_w4r")
+        nc.vector.tensor_copy(v_rows[:], tab_plane[:].indirect(idx[:]))
+        v_scale = [v_early, fresh([P, S], U8, "v_late")]
+        nc.vector.tensor_copy(v_scale[1][:].bitcast(I32), v_rows[:].bitcast(I32))
+        for a in range(PASSES):
+            for r in range(a, 4):
+                nc.gpsimd.dma_start(
+                    out=v_scale[a][r:P:32, :].bitcast(I32), in_=v_rows[8 * r + 4 - 4 * a : P : 32, :].bitcast(I32)
+                )
+        v2_rows = slot([P, S2], U8, "v2_rows", "s_ts")
         nc.vector.tensor_copy(v2_rows[:], tab2_plane[:].indirect(idx2[:]))
         for r in range(4):
             nc.sync.dma_start(out=v2_scale[r:P:32, :].bitcast(I32), in_=v2_rows[8 * r : P : 32, :].bitcast(I32))
-        v_scale = [slot([P, S], U8, "v_rows", "s_t2s"), v_late]
-        nc.vector.tensor_copy(v_scale[0][:], tab_plane[:].indirect(idx[:]))
-        for r in range(4):
-            nc.gpsimd.dma_start(out=v_late[r:P:32, :].bitcast(I32), in_=v_scale[0][8 * r + 4 : P : 32, :].bitcast(I32))
 
         wg_codes, wg_scale = {}, {}
         v_codes = []
@@ -180,7 +185,7 @@ def tile_list_auction_slot_scores_kernel(
                 nc.vector.tensor_copy(v_codes[a][:, lo:hi], tab[a][:].indirect(idx[:, lo // 16 : hi // 16]))
 
         whole = round_wg(nc.scalar.copy, 0, 0, PACK, "s_bf0")
-        gather_v(0, "s_ts")
+        gather_v(0, "s_t2s")
         quantise_wg(whole, 0, 0, PACK, "s_tab0")
         w4_scale = slot([P, PASSES * H], U8, "w4_scale", "s_bf0")
         nc.vector.tensor_copy(

@@ -145,7 +145,7 @@ def tile_list_auction_slot_scores_kernel(
             out=w4_codes[:].bitcast(U16).rearrange("p (a t m i) -> p a m t i", a=PASSES, t=PACK, i=8),
             in_=w4_raw[:].bitcast(U16).rearrange("p (a m i t) -> p a m t i", a=PASSES, t=PACK, i=8),
         )
-        v_rows = slot([P, S], U8, "v_rows", "s_w4r")
+        v_rows = fresh([P, S], U8, "v_rows")
         nc.vector.tensor_copy(v_rows[:], tab_plane[:].indirect(idx[:]))
         v_scale = [v_early, fresh([P, S], U8, "v_late")]
         nc.vector.tensor_copy(v_scale[1][:].bitcast(I32), v_rows[:].bitcast(I32))
@@ -229,10 +229,7 @@ def tile_list_auction_slot_scores_kernel(
         def on_piece(shape, dtype, name, c):
             return links.tile(shape, dtype, name=name, align_bytes=64, offset=2 * PACK * PIECES[c][0])
 
-        sigs = [
-            fresh([P, S], F32, "sig0"), fresh([P, S], F32, "sig1"),
-            fresh([P, S], F32, "sig2"), fresh([P, S], F32, "sig3"),
-        ]
+        sigs = [slot([P, S], F32, "sig%d" % t, "s_sig%d" % t) for t in range(PACK)]
 
         def sigmoid(acc, t, lo=0, hi=S):
             nc.scalar.activation(out=sigs[t][:, lo:hi], in_=acc[:, lo:hi], func=ACT.Sigmoid)
@@ -288,13 +285,14 @@ def tile_list_auction_slot_scores_kernel(
 
         put(h_cut[0], wgs_cut[0][:], first, *CUTS[0])
         product(second, "s_h0")
+        product(third, "s_wgs0_0")
+        product(last, "s_sig%d" % second)
         put(h_cut[1], wgs_cut[1][:], first, *CUTS[1])
-        product(third, "s_wgs0_1")
-        product(last, "s_h1")
-        round_page(nc.vector.tensor_copy, first, 3)
         for t in ORDER:
             if t != first:
                 put(hs[t], wgs_of[t], t)
+            if t == second:
+                round_page(nc.vector.tensor_copy, first, 3)
             for c in range(3 if t in (first, last) else 4):
                 round_page(nc.scalar.copy, t, c)
 

@@ -25,7 +25,7 @@ BANKS = 8
 TILES = S2 // P
 HALVES = T2 // BANK
 ORDER = (2, 0, 1, 3)
-CUTS = ((0, S // 2), (S // 2, S))
+CUTS = ((0, 128), (128, 256), (256, S))
 PIECES = ((0, 256), (256, 512), (512, 768), (768, 1024))
 
 
@@ -95,12 +95,19 @@ def tile_list_auction_slot_scores_kernel(
         wg_raw = [slot([P, PACK, H], F32, "wg_raw%d" % a, "s_raw%d" % a) for a in range(PASSES)]
         tab = [slot([P, T], U32, "tab%d" % a, "s_tab%d" % a) for a in range(PASSES)]
         page_rows = page0.rearrange("(p t) c -> t p c", t=PACK)
-        page = [keep.tile([P, T2], F32, name="page%d" % t) for t in range(PACK)]
         first, second, third, last = ORDER
+        shared = 2 * PACK * T2
+        early = shared + 8 * T2 + 2 * S
+        page = [
+            links.tile([P, T2], F32, name="page%d" % t, align_bytes=64, offset=shared)
+            if t == first else keep.tile([P, T2], F32, name="page%d" % t)
+            for t in range(PACK)
+        ]
         wgs_rows = wgs.rearrange("(p t) j -> p t j", t=PACK)
-        wgs_cut = [slot([P, S // 2], F32, "wgs_cut%d" % u, "s_wgs0_%d" % u) for u in range(2)]
+        wgs_half = [slot([P, S // 2], F32, "wgs_half%d" % u, "s_wgs0_%d" % u) for u in range(2)]
+        wgs_cut = [wgs_half[0][:, 0:P], wgs_half[0][:, P : 2 * P], wgs_half[1][:]]
         wgs_second = slot([P, S], F32, "wgs_second", "s_wgs1")
-        wgs_rest = slot([P, 2, S], F32, "wgs_rest", "s_wgs")
+        wgs_rest = links.tile([P, 2, S], F32, name="wgs_rest", align_bytes=64, offset=shared + 4 * T2)
         wgs_of = {second: wgs_second[:], third: wgs_rest[:, 0, :], last: wgs_rest[:, 1, :]}
         tab2 = slot([P, T3], U32, "tab2", "s_tab2")
         reserve_sb = [keep.tile([P, 4, PICKS], F32, name="reserve%d" % u) for u in range(2)]
@@ -122,9 +129,9 @@ def tile_list_auction_slot_scores_kernel(
         load_words(tab[1], tab_words[1])
         nc.sync.dma_start(idx3[:], offs3)
         load_page(first)
-        load_wgs(wgs_cut[0], wgs_rows[:, first, 0 : S // 2])
+        load_wgs(wgs_half[0], wgs_rows[:, first, 0 : S // 2])
         load_page(second)
-        load_wgs(wgs_cut[1], wgs_rows[:, first, S // 2 : S])
+        load_wgs(wgs_half[1], wgs_rows[:, first, S // 2 : S])
         load_wgs(wgs_second, wgs_rows[:, second, :])
         load_page(third)
         load_wgs(wgs_rest, wgs_rows[:, third : PACK : last - third, :])
@@ -162,13 +169,11 @@ def tile_list_auction_slot_scores_kernel(
         wg_codes, wg_scale = {}, {}
         v_codes = []
 
-        def round_wg(copy, a, t0, t1, tag):
-            wg_bf = slot([P, (t1 - t0) * P * PACK], BF16, "wg_bf%d_%d" % (a, t0), tag)
+        def round_wg(copy, wg_bf, a, t0, t1):
             copy(
-                out=wg_bf[:].rearrange("p (t m j) -> p m t j", m=P, j=PACK),
+                out=wg_bf[:, t0 * P * PACK : t1 * P * PACK].rearrange("p (t m j) -> p m t j", m=P, j=PACK),
                 in_=wg_raw[a][:].rearrange("p j (m t) -> p m t j", t=PACK)[:, :, t0:t1, :],
             )
-            return wg_bf
 
         def quantise_wg(wg_bf, a, t0, t1, tag):
             codes = slot([P, P * (t1 - t0)], U32, "wg_codes%d_%d" % (a, t0), tag)
@@ -184,7 +189,8 @@ def tile_list_auction_slot_scores_kernel(
             for lo, hi in ((0, S),) if a == 0 else CUTS:
                 nc.vector.tensor_copy(v_codes[a][:, lo:hi], tab[a][:].indirect(idx[:, lo // 16 : hi // 16]))
 
-        whole = round_wg(nc.scalar.copy, 0, 0, PACK, "s_bf0")
+        whole = slot([P, H * PACK], BF16, "wg_bf0", "s_bf0")
+        round_wg(nc.scalar.copy, whole, 0, 0, PACK)
         gather_v(0, "s_t2s")
         quantise_wg(whole, 0, 0, PACK, "s_tab0")
         w4_scale = slot([P, PASSES * H], U8, "w4_scale", "s_bf0")
@@ -200,30 +206,33 @@ def tile_list_auction_slot_scores_kernel(
         warm_sigmoid = keep.tile([P, 1], F32, name="warm_sigmoid")
         nc.scalar.activation(out=warm_sigmoid[:], in_=ln_bid[:, 0:1], func=ACT.Sigmoid)
 
-        high = round_wg(nc.vector.tensor_copy, 1, 2, PACK, "s_w4s")
-        low = round_wg(nc.scalar.copy, 1, 0, 2, "s_bf1")
-        quantise_wg(high, 1, 2, PACK, "s_wc1")
+        late = slot([P, H * PACK], BF16, "wg_bf1", "s_w4s")
+        round_wg(nc.vector.tensor_copy, late, 1, 1, PACK)
+        round_wg(nc.scalar.copy, late, 1, 0, 1)
+        quantise_wg(late, 1, 0, PACK, "s_wc1")
         gather_v(1, "s_w4s")
-        quantise_wg(low, 1, 0, 2, "s_tab1")
+
+        def runs(lo, hi):
+            return ((lo, hi),)
 
         def gate_pass(acc, t, a, lo=0, hi=S):
-            nc.tensor.matmul_mx(
-                out=acc[:, lo:hi],
-                lhsT=wg_codes[a, t].bitcast(FP8X4), lhsT_scale=wg_scale[a, t],
-                rhs=v_codes[a][:, lo:hi].bitcast(FP8X4), rhs_scale=v_scale[a][:, lo:hi],
-                start=(a == 0), stop=(a == PASSES - 1),
-            )
+            for n0, n1 in runs(lo, hi):
+                nc.tensor.matmul_mx(
+                    out=acc[:, n0:n1],
+                    lhsT=wg_codes[a, t].bitcast(FP8X4), lhsT_scale=wg_scale[a, t],
+                    rhs=v_codes[a][:, n0:n1].bitcast(FP8X4), rhs_scale=v_scale[a][:, n0:n1],
+                    start=(a == 0 and n0 == lo), stop=(a == PASSES - 1 and n1 == hi),
+                )
 
         def feat_pass(acc, t, a, lo=0, hi=S):
             c0 = a * H + P * t
-            width = S if hi - lo == S else P
-            for n in range(lo, hi, width):
+            for n0, n1 in runs(lo, hi):
                 nc.tensor.matmul_mx(
-                    out=acc[:, n : n + width],
+                    out=acc[:, n0:n1],
                     lhsT=w4_codes[:, 2 * c0 : 2 * (c0 + P)].bitcast(FP4X4),
                     lhsT_scale=w4_scale[:, c0 : c0 + P],
-                    rhs=v_codes[a][:, n : n + width].bitcast(FP8X4), rhs_scale=v_scale[a][:, n : n + width],
-                    start=(a == 0 and n == lo), stop=(a == PASSES - 1 and n + width == hi),
+                    rhs=v_codes[a][:, n0:n1].bitcast(FP8X4), rhs_scale=v_scale[a][:, n0:n1],
+                    start=(a == 0 and n0 == lo), stop=(a == PASSES - 1 and n1 == hi),
                 )
 
         def on_piece(shape, dtype, name, c):
@@ -240,21 +249,19 @@ def tile_list_auction_slot_scores_kernel(
         def put(h, factors, t, lo=0, hi=S):
             nc.vector.tensor_tensor(page[t][:].indirect(idx3[:, lo // 16 : hi // 16]), h[:], factors, ALU.mult)
 
-        gate_cut = [bank(u) for u in range(2)]
-        feat_cut = [bank(2 + u) for u in range(2)]
-        gate, feat = {second: bank(4)}, {second: bank(5)}
+        gate_cut = [bank(u) for u in range(3)]
+        feat_cut = [bank(3 + u) for u in range(3)]
+        gate, feat = {second: bank(6)}, {second: bank(7)}
         for u, (lo, hi) in enumerate(CUTS):
             gate_pass(gate_cut[u], first, 0, lo, hi)
         gate_pass(gate[second], second, 0)
         for u, (lo, hi) in enumerate(CUTS):
             feat_pass(feat_cut[u], first, 0, lo, hi)
         feat_pass(feat[second], second, 0)
-        h_cut = [slot([P, S // 2], F32, "h_cut%d" % u, "s_h%d" % u) for u in range(2)]
         for u, (lo, hi) in enumerate(CUTS):
             gate_pass(gate_cut[u], first, 1, lo, hi)
             sigmoid(gate_cut[u], first, lo, hi)
             feat_pass(feat_cut[u], first, 1, lo, hi)
-            weigh(h_cut[u], feat_cut[u], first, lo, hi)
         gate_pass(gate[second], second, 1)
         sigmoid(gate[second], second)
         feat_pass(feat[second], second, 1)
@@ -264,7 +271,7 @@ def tile_list_auction_slot_scores_kernel(
                 gate_pass(gate[t], t, a)
             sigmoid(gate[t], t)
         for u, t in enumerate((third, last)):
-            feat[t] = bank(2 + u)
+            feat[t] = bank(3 + u)
             for a in range(PASSES):
                 feat_pass(feat[t], t, a)
 
@@ -272,29 +279,33 @@ def tile_list_auction_slot_scores_kernel(
         warm_exp = keep.tile([P, 1], F32, name="warm_exp")
         nc.scalar.activation(out=warm_exp[:], in_=sigs[last][:, 0:1], func=ACT.Exp)
 
-        page_bf = [on_piece([P, hi - lo, PACK], BF16, "page_bf%d" % c, c) for c, (lo, hi) in enumerate(PIECES)]
+        page_bf = on_piece([P, T2 * PACK], BF16, "page_bf", 0)
         hs = {}
 
         def product(t, tag):
             hs[t] = slot([P, S], F32, "h%d" % t, tag)
             weigh(hs[t], feat[t], t)
 
-        def round_page(copy, t, c):
-            lo, hi = PIECES[c]
-            copy(out=page_bf[c][:, :, t], in_=page[t][:, lo:hi])
+        def round_page(copy, t, lo, hi):
+            copy(out=page_bf[:, PACK * lo + t : PACK * hi : PACK], in_=page[t][:, lo:hi])
 
-        put(h_cut[0], wgs_cut[0][:], first, *CUTS[0])
-        product(second, "s_h0")
-        product(third, "s_wgs0_0")
+        h_ab = [links.tile([P, P], F32, name="h_cut%d" % u, align_bytes=64, offset=early + (4 * S + P) * u) for u in range(2)]
+        for u in range(2):
+            weigh(h_ab[u], feat_cut[u], first, *CUTS[u])
+        put(h_ab[0], wgs_cut[0], first, *CUTS[0])
+        h_c = links.tile([P, S // 2], F32, name="h_cut2", align_bytes=64, offset=early - 2 * S + 64)
+        weigh(h_c, feat_cut[2], first, *CUTS[2])
+        put(h_ab[1], wgs_cut[1], first, *CUTS[1])
+        hs[second] = links.tile([P, S], F32, name="h_second", align_bytes=64, offset=early + 64)
+        weigh(hs[second], feat[second], second)
+        product(third, "s_sig%d" % first)
+        put(h_c, wgs_cut[2], first, *CUTS[2])
         product(last, "s_sig%d" % second)
-        put(h_cut[1], wgs_cut[1][:], first, *CUTS[1])
         for t in ORDER:
             if t != first:
                 put(hs[t], wgs_of[t], t)
-            if t == second:
-                round_page(nc.vector.tensor_copy, first, 3)
-            for c in range(3 if t in (first, last) else 4):
-                round_page(nc.scalar.copy, t, c)
+            for lo, hi in PIECES[:3] if t == last else ((0, T2),):
+                round_page(nc.scalar.copy, t, lo, hi)
 
         v2_codes = []
         page_codes = [keep.tile([P, BANK], U32, name="page_codes0", align_bytes=64), fresh([P, BANK], U32, "page_codes1")]
@@ -309,12 +320,12 @@ def tile_list_auction_slot_scores_kernel(
             cols = slice(lo % BANK, lo % BANK + hi - lo)
             nc.vector.quantize_mx(
                 out=page_codes[lo // BANK][:, cols].bitcast(FP8X4), scales=page_scale[lo // BANK][:, cols],
-                in_=page_bf[c][:].rearrange("p c t -> p (c t)"),
+                in_=page_bf[:, PACK * lo : PACK * hi],
             )
 
-        gather_v2(0, slot([P, half], U32, "v2_codes0", "s_wgs"))
+        gather_v2(0, links.tile([P, half], U32, name="v2_codes0", align_bytes=64, offset=shared + 4 * T2 - 2 * half))
         quantise_page(0)
-        round_page(nc.vector.tensor_copy, last, 3)
+        round_page(nc.vector.tensor_copy, last, *PIECES[3])
         quantise_page(1)
         quantise_page(3)
         quantise_page(2)

@@ -107,8 +107,9 @@ def tile_list_auction_slot_scores_kernel(
         wgs_half = [slot([P, S // 2], F32, "wgs_half%d" % u, "s_wgs0_%d" % u) for u in range(2)]
         wgs_cut = [wgs_half[0][:, 0:P], wgs_half[0][:, P : 2 * P], wgs_half[1][:]]
         wgs_second = slot([P, S], F32, "wgs_second", "s_wgs1")
-        wgs_rest = links.tile([P, 2, S], F32, name="wgs_rest", align_bytes=64, offset=shared + 4 * T2)
-        wgs_of = {second: wgs_second[:], third: wgs_rest[:, 0, :], last: wgs_rest[:, 1, :]}
+        wgs_third = slot([P, S], F32, "wgs_third", "s_wgs2")
+        wgs_last = links.tile([P, S], F32, name="wgs_last", align_bytes=64, offset=shared + 4 * T2)
+        wgs_of = {second: wgs_second[:], third: wgs_third[:], last: wgs_last[:]}
         tab2 = slot([P, T3], U32, "tab2", "s_tab2")
         reserve_sb = [keep.tile([P, 4, PICKS], F32, name="reserve%d" % u) for u in range(2)]
 
@@ -130,11 +131,12 @@ def tile_list_auction_slot_scores_kernel(
         nc.sync.dma_start(idx3[:], offs3)
         load_page(first)
         load_wgs(wgs_half[0], wgs_rows[:, first, 0 : S // 2])
+        load_wgs(wgs_third, wgs_rows[:, third, :])
         load_page(second)
         load_wgs(wgs_half[1], wgs_rows[:, first, S // 2 : S])
         load_wgs(wgs_second, wgs_rows[:, second, :])
         load_page(third)
-        load_wgs(wgs_rest, wgs_rows[:, third : PACK : last - third, :])
+        load_wgs(wgs_last, wgs_rows[:, last, :])
         load_words(tab2, tab2_words[0])
         load_page(last)
         nc.sync.dma_start(idx4[:], offs4)
@@ -270,17 +272,21 @@ def tile_list_auction_slot_scores_kernel(
             for a in range(PASSES):
                 gate_pass(gate[t], t, a)
             sigmoid(gate[t], t)
-        for u, t in enumerate((third, last)):
+        for u, t in enumerate((last, third)):
             feat[t] = bank(3 + u)
             for a in range(PASSES):
                 feat_pass(feat[t], t, a)
 
         half = S2 // 2
+        hs = {third: slot([P, S], F32, "feat_third", "s_feat")}
+        nc.scalar.copy(out=hs[third][:], in_=feat[third][:])
+        gated = slot([P, S], F32, "gated", "s_gated")
+        nc.gpsimd.tensor_tensor(gated[:], sigs[third][:], wgs_of[third], ALU.mult)
+        wgs_of[third] = gated[:]
         warm_exp = keep.tile([P, 1], F32, name="warm_exp")
         nc.scalar.activation(out=warm_exp[:], in_=sigs[last][:, 0:1], func=ACT.Exp)
 
         page_bf = on_piece([P, T2 * PACK], BF16, "page_bf", 0)
-        hs = {}
 
         def product(t, tag):
             hs[t] = slot([P, S], F32, "h%d" % t, tag)
@@ -298,9 +304,8 @@ def tile_list_auction_slot_scores_kernel(
         put(h_ab[1], wgs_cut[1], first, *CUTS[1])
         hs[second] = links.tile([P, S], F32, name="h_second", align_bytes=64, offset=early + 64)
         weigh(hs[second], feat[second], second)
-        product(third, "s_sig%d" % first)
+        product(last, "s_sig%d" % first)
         put(h_c, wgs_cut[2], first, *CUTS[2])
-        product(last, "s_sig%d" % second)
         for t in ORDER:
             if t != first:
                 put(hs[t], wgs_of[t], t)

@@ -24,17 +24,9 @@ BANK = 512
 BANKS = 8
 TILES = S2 // P
 HALVES = T2 // BANK
-ORDER = (2, 0, 1, 3)
-CUTS = ((0, 128), (128, 256), (256, S))
-PIECES = ((0, 256), (256, 512), (512, 768), (768, 1024))
-
-
-def load_scale_rows(queue, plane, scales, row):
-    for r in range(4):
-        queue.dma_start(
-            out=plane[row + r : P : 32, :].bitcast(I32),
-            in_=scales.bitcast(I32).rearrange("a (q r) n -> r q a n", r=4)[r],
-        )
+QUARTER = T2 // 4
+FIRST, SECOND, THIRD, LAST = 2, 0, 1, 3
+CUTS = ((0, P), (P, 2 * P), (2 * P, S))
 
 
 def tile_list_auction_slot_scores_kernel(
@@ -44,161 +36,161 @@ def tile_list_auction_slot_scores_kernel(
     nc = tc.nc
     with ExitStack() as ctx:
         keep = ctx.enter_context(tc.tile_pool(name="keep", bufs=1))
-        ring = ctx.enter_context(tc.tile_pool(name="ring", bufs=3))
-        links = ctx.enter_context(tc.tile_pool(name="links", bufs=1))
+        ring = ctx.enter_context(tc.tile_pool(name="ring", bufs=TILES + 1))
+        placed = ctx.enter_context(tc.tile_pool(name="placed", bufs=1))
         psum = ctx.enter_context(tc.psum_pool(name="psum", bufs=1))
+
+        def fresh(shape, dtype, name):
+            return keep.tile(shape, dtype, name=name, align_bytes=64)
+
+        def slot(shape, dtype, name, tag):
+            return keep.tile(shape, dtype, name=name, tag=tag, align_bytes=64)
+
+        def at(shape, dtype, name, offset):
+            return placed.tile(shape, dtype, name=name, align_bytes=64, offset=offset)
+
+        def bank(k):
+            return psum.tile([P, BANK], F32, name="bank%d" % k, tag="bank%d" % k)
+
+        def words(ap):
+            return ap.bitcast(I32)
+
+        def entries(offsets, lo, hi):
+            return offsets[:, lo // 16 : hi // 16]
+
+        rounded_at = 0
+        first_page_at = rounded_at + 2 * PACK * T2
+        products_at = first_page_at + 4 * T2 + 2 * S
 
         idx = keep.tile([P, S // 16], U16, name="idx")
         idx2 = keep.tile([P, S2 // 16], U16, name="idx2")
         idx3 = keep.tile([P, S // 16], U16, name="idx3")
         idx4 = keep.tile([P, PICKS // 16], U16, name="idx4")
 
-        def slot(shape, dtype, name, tag):
-            return keep.tile(shape, dtype, name=name, tag=tag, align_bytes=64)
-
-        def bank(k):
-            return psum.tile([P, BANK], F32, name="bank%d" % k, tag="bank%d" % k)
-
-        tab_plane = slot([P, T], U8, "tab_plane", "s_ts")
-        w4_plane = slot([P, PASSES * H], U8, "w4_plane", "s_w4s")
-        tab2_plane = slot([P, T3], U8, "tab2_plane", "s_t2s")
-        v2_scale = keep.tile([P, S2], U8, name="v2_scale", align_bytes=64)
-        v_early = keep.tile([P, S], U8, name="v_early", align_bytes=64)
+        tab_rows = slot([P, T], U8, "tab_rows", "tab_rows")
+        tab2_rows = slot([P, T3], U8, "tab2_rows", "tab2_rows")
+        w4_rows = slot([P, PASSES * H], U8, "w4_rows", "w4_rows")
+        v_scale = [fresh([P, S], U8, "v_scale%d" % a) for a in range(PASSES)]
         one = keep.tile([P, 1], F32, name="one")
         bid_rows = keep.tile([P, P], F32, name="bid_rows")
         identity = keep.tile([P, P], F32, name="identity")
-        nc.gpsimd.memset(tab_plane[:].bitcast(I32), 0)
-        nc.vector.memset(tab2_plane[:].bitcast(I32), 0)
+        v2_scale = fresh([P, S2], U8, "v2_scale")
+        nc.gpsimd.memset(words(tab_rows[64:P, :]), 0)
+        nc.vector.memset(words(tab_rows[32:64, :]), 0)
         nc.gpsimd.memset(one[:], 1.0)
+        nc.vector.memset(words(tab2_rows[:]), 0)
         nc.gpsimd.memset(bid_rows[:], 0.0)
-        nc.gpsimd.memset(w4_plane[:].bitcast(I32), 0)
+        nc.gpsimd.memset(words(w4_rows[:]), 0)
         make_identity(nc, identity[:])
-        nc.gpsimd.memset(v_early[:].bitcast(I32), 0)
-        nc.gpsimd.memset(v2_scale[:].bitcast(I32), 0)
+        nc.gpsimd.memset(words(v_scale[1][:]), 0)
+        nc.vector.memset(words(v2_scale[:]), 0)
         warm_ln = keep.tile([P, 1], F32, name="warm_ln")
         nc.scalar.activation(out=warm_ln[:], in_=one[:], func=ACT.Ln)
+
+        w4_raw = fresh([P, PASSES * 2 * H], U8, "w4_raw")
+        wg_raw = [fresh([P, PACK, H], F32, "wg_raw%d" % a) for a in range(PASSES)]
+        tab = [slot([P, T], U32, "tab%d" % a, "tab%d" % a) for a in range(PASSES)]
+        tab2 = slot([P, T3], U32, "tab2", "tab2")
+        page = [
+            at([P, T2], F32, "page%d" % t, first_page_at) if t == FIRST else fresh([P, T2], F32, "page%d" % t)
+            for t in range(PACK)
+        ]
+        wgs_half = [fresh([P, S // 2], F32, "wgs_half%d" % u) for u in range(2)]
+        wgs_second = fresh([P, S], F32, "wgs_second")
+        wgs_rest = fresh([P, 2, S], F32, "wgs_rest")
+        factors = {SECOND: wgs_second[:], THIRD: wgs_rest[:, 0, :], LAST: wgs_rest[:, 1, :]}
+        reserve_sb = [keep.tile([P, 4, PICKS], F32, name="reserve%d" % u) for u in range(2)]
+        page_rows = page0.rearrange("(p t) c -> t p c", t=PACK)
+        wgs_rows = wgs.rearrange("(p t) j -> p t j", t=PACK)
 
         def load_wg(a):
             nc.sync.dma_start(out=wg_raw[a][:], in_=wg[512 * a : 512 * (a + 1), :].rearrange("(p j) c -> p j c", j=PACK))
 
-        def load_words(tile, words):
-            nc.sync.dma_start(out=tile[:].bitcast(I32), in_=words.rearrange("p t i -> p (t i)").bitcast(I32))
+        def load_words(tile, table, lo, hi):
+            nc.sync.dma_start(out=words(tile[:, lo:hi]), in_=words(table.rearrange("p t i -> p (t i)"))[:, lo:hi])
 
         def load_page(t):
             nc.sync.dma_start(out=page[t][:], in_=page_rows[t])
 
-        def load_wgs(tile, rows):
-            for q in (0, 2, 1, 3):
+        def load_wgs(tile, rows, quadrants):
+            for q in quadrants:
                 nc.sync.dma_start(out=tile[32 * q : 32 * (q + 1)], in_=rows)
 
-        w4_raw = slot([P, PASSES * 2 * H], U8, "w4_raw", "s_w4r")
-        wg_raw = [slot([P, PACK, H], F32, "wg_raw%d" % a, "s_raw%d" % a) for a in range(PASSES)]
-        tab = [slot([P, T], U32, "tab%d" % a, "s_tab%d" % a) for a in range(PASSES)]
-        page_rows = page0.rearrange("(p t) c -> t p c", t=PACK)
-        first, second, third, last = ORDER
-        shared = 2 * PACK * T2
-        early = shared + 8 * T2 + 2 * S
-        page = [
-            links.tile([P, T2], F32, name="page%d" % t, align_bytes=64, offset=shared)
-            if t == first else keep.tile([P, T2], F32, name="page%d" % t)
-            for t in range(PACK)
-        ]
-        wgs_rows = wgs.rearrange("(p t) j -> p t j", t=PACK)
-        wgs_half = [slot([P, S // 2], F32, "wgs_half%d" % u, "s_wgs0_%d" % u) for u in range(2)]
-        wgs_cut = [wgs_half[0][:, 0:P], wgs_half[0][:, P : 2 * P], wgs_half[1][:]]
-        wgs_second = slot([P, S], F32, "wgs_second", "s_wgs1")
-        wgs_third = slot([P, S], F32, "wgs_third", "s_wgs2")
-        wgs_last = links.tile([P, S], F32, name="wgs_last", align_bytes=64, offset=shared + 4 * T2)
-        wgs_of = {second: wgs_second[:], third: wgs_third[:], last: wgs_last[:]}
-        tab2 = slot([P, T3], U32, "tab2", "s_tab2")
-        reserve_sb = [keep.tile([P, 4, PICKS], F32, name="reserve%d" % u) for u in range(2)]
-
+        nc.sync.dma_start(idx[:], offs)
+        nc.sync.dma_start(out=words(tab_rows[0:32, :]), in_=words(tab_scales).rearrange("a q n -> (a q) n"))
         nc.sync.dma_start(
-            out=w4_raw[:].bitcast(I32).rearrange("p (a n) -> p a n", a=PASSES),
-            in_=w4_words.bitcast(I32).rearrange("a p n -> p a n"),
+            out=words(w4_raw[:]).rearrange("p (a n) -> p a n", a=PASSES), in_=words(w4_words).rearrange("a p n -> p a n")
         )
         nc.sync.dma_start(idx2[:], offs2)
-        nc.sync.dma_start(idx[:], offs)
-        for a in range(PASSES):
-            nc.sync.dma_start(out=tab_plane[4 - 4 * a : P : 8, :].bitcast(I32), in_=tab_scales[a].bitcast(I32))
         load_wg(0)
-        nc.sync.dma_start(out=tab2_plane[0:P:8, :].bitcast(I32), in_=tab2_scales[0].bitcast(I32))
-        load_words(tab[0], tab_words[0])
+        nc.sync.dma_start(out=words(tab2_rows[0:P:8, :]), in_=words(tab2_scales[0]))
+        load_words(tab[0], tab_words[0], 0, T)
         nc.sync.dma_start(out=bid_rows[0:TILES, :], in_=bid.rearrange("(i p) -> i p", p=P))
-        load_scale_rows(nc.sync, w4_plane, w4_scales, 0)
+        for r in range(4):
+            nc.sync.dma_start(out=words(w4_rows[r:P:32, :]), in_=words(w4_scales).rearrange("a (q r) n -> r q a n", r=4)[r])
         load_wg(1)
-        load_words(tab[1], tab_words[1])
+        load_words(tab[1], tab_words[1], 0, T)
         nc.sync.dma_start(idx3[:], offs3)
-        load_page(first)
-        load_wgs(wgs_half[0], wgs_rows[:, first, 0 : S // 2])
-        load_wgs(wgs_third, wgs_rows[:, third, :])
-        load_page(second)
-        load_wgs(wgs_half[1], wgs_rows[:, first, S // 2 : S])
-        load_wgs(wgs_second, wgs_rows[:, second, :])
-        load_page(third)
-        load_wgs(wgs_last, wgs_rows[:, last, :])
-        load_words(tab2, tab2_words[0])
-        load_page(last)
+        load_page(FIRST)
+        load_wgs(wgs_half[0], wgs_rows[:, FIRST, 0 : S // 2], (0, 2, 1, 3))
+        load_page(SECOND)
+        load_wgs(wgs_half[1], wgs_rows[:, FIRST, S // 2 : S], (0, 2, 1, 3))
+        load_wgs(wgs_second, wgs_rows[:, SECOND, :], (0, 2, 1, 3))
+        load_page(THIRD)
+        load_wgs(wgs_rest, wgs_rows[:, THIRD : PACK : LAST - THIRD, :], (0, 2, 1, 3))
+        load_words(tab2, tab2_words[0], 0, T3 - P)
+        load_page(LAST)
+        load_words(tab2, tab2_words[0], T3 - P, T3)
         nc.sync.dma_start(idx4[:], offs4)
         for u in range(2):
             nc.sync.dma_start(
-                out=reserve_sb[u][:],
-                in_=reserve[512 * u : 512 * (u + 1), :].rearrange("(i p) m -> p i m", p=P),
+                out=reserve_sb[u][:], in_=reserve[512 * u : 512 * (u + 1), :].rearrange("(i p) m -> p i m", p=P)
             )
 
-        def fresh(shape, dtype, name):
-            return keep.tile(shape, dtype, name=name, align_bytes=64)
+        v_rows = fresh([P, S], U8, "v_rows")
+        nc.vector.tensor_copy(v_rows[:], tab_rows[:].indirect(idx[:]))
+        nc.vector.tensor_copy(words(v_scale[0][:]), words(v_rows[:]))
+        for a in range(PASSES):
+            for q in range(1 - a, 4):
+                src = 16 * a + 4 * q
+                nc.gpsimd.dma_start(out=words(v_scale[a][32 * q : 32 * q + 4, :]), in_=words(v_rows[src : src + 4, :]))
 
         w4_codes = fresh([P, PASSES * 2 * H], U8, "w4_codes")
         nc.vector.tensor_copy(
             out=w4_codes[:].bitcast(U16).rearrange("p (a t m i) -> p a m t i", a=PASSES, t=PACK, i=8),
             in_=w4_raw[:].bitcast(U16).rearrange("p (a m i t) -> p a m t i", a=PASSES, t=PACK, i=8),
         )
-        v_rows = fresh([P, S], U8, "v_rows")
-        nc.vector.tensor_copy(v_rows[:], tab_plane[:].indirect(idx[:]))
-        v_scale = [v_early, fresh([P, S], U8, "v_late")]
-        nc.vector.tensor_copy(v_scale[1][:].bitcast(I32), v_rows[:].bitcast(I32))
-        for a in range(PASSES):
-            for r in range(a, 4):
-                nc.gpsimd.dma_start(
-                    out=v_scale[a][r:P:32, :].bitcast(I32), in_=v_rows[8 * r + 4 - 4 * a : P : 32, :].bitcast(I32)
-                )
-        v2_rows = slot([P, S2], U8, "v2_rows", "s_ts")
-        nc.vector.tensor_copy(v2_rows[:], tab2_plane[:].indirect(idx2[:]))
+        v2_rows = slot([P, S2], U8, "v2_rows", "tab_rows")
+        nc.vector.tensor_copy(v2_rows[:], tab2_rows[:].indirect(idx2[:]))
         for r in range(4):
-            nc.sync.dma_start(out=v2_scale[r:P:32, :].bitcast(I32), in_=v2_rows[8 * r : P : 32, :].bitcast(I32))
+            nc.sync.dma_start(out=words(v2_scale[r:P:32, :]), in_=words(v2_rows[8 * r : P : 32, :]))
 
-        wg_codes, wg_scale = {}, {}
-        v_codes = []
-
-        def round_wg(copy, wg_bf, a, t0, t1):
+        def round_wg(copy, rounded, a, t0, t1):
             copy(
-                out=wg_bf[:, t0 * P * PACK : t1 * P * PACK].rearrange("p (t m j) -> p m t j", m=P, j=PACK),
+                out=rounded[:, t0 * H : t1 * H].rearrange("p (t m j) -> p m t j", m=P, j=PACK),
                 in_=wg_raw[a][:].rearrange("p j (m t) -> p m t j", t=PACK)[:, :, t0:t1, :],
             )
 
-        def quantise_wg(wg_bf, a, t0, t1, tag):
-            codes = slot([P, P * (t1 - t0)], U32, "wg_codes%d_%d" % (a, t0), tag)
-            scale = fresh([P, P * (t1 - t0)], U8, "wg_scale%d_%d" % (a, t0))
-            nc.vector.quantize_mx(out=codes[:].bitcast(FP8X4), scales=scale[:], in_=wg_bf[:])
-            for t in range(t0, t1):
-                cols = slice(P * (t - t0), P * (t - t0 + 1))
-                wg_codes[a, t] = codes[:, cols]
-                wg_scale[a, t] = scale[:, cols]
+        def quantise_wg(rounded, a, tag):
+            codes = slot([P, H], U32, "wg_codes%d" % a, tag)
+            scale = fresh([P, H], U8, "wg_scale%d" % a)
+            nc.vector.quantize_mx(out=codes[:].bitcast(FP8X4), scales=scale[:], in_=rounded[:])
+            return codes, scale
 
-        def gather_v(a, tag):
-            v_codes.append(slot([P, S], U32, "v_codes%d" % a, tag))
-            for lo, hi in ((0, S),) if a == 0 else CUTS:
-                nc.vector.tensor_copy(v_codes[a][:, lo:hi], tab[a][:].indirect(idx[:, lo // 16 : hi // 16]))
+        def gather_v(a, tag, cuts):
+            codes = slot([P, S], U32, "v_codes%d" % a, tag)
+            for lo, hi in cuts:
+                nc.vector.tensor_copy(codes[:, lo:hi], tab[a][:].indirect(entries(idx, lo, hi)))
+            return codes
 
-        whole = slot([P, H * PACK], BF16, "wg_bf0", "s_bf0")
-        round_wg(nc.scalar.copy, whole, 0, 0, PACK)
-        gather_v(0, "s_t2s")
-        quantise_wg(whole, 0, 0, PACK, "s_tab0")
-        w4_scale = slot([P, PASSES * H], U8, "w4_scale", "s_bf0")
+        wg_early = slot([P, PACK * H], BF16, "wg_early", "wg_early")
+        round_wg(nc.scalar.copy, wg_early, 0, 0, PACK)
+        v_codes = [gather_v(0, "tab2_rows", ((0, S),))]
+        wg_mx = [quantise_wg(wg_early, 0, "tab0")]
+        w4_scale = slot([P, PASSES * H], U8, "w4_scale", "wg_early")
         nc.vector.tensor_copy(
             out=w4_scale[:].rearrange("p (a t m i) -> p a m t i", a=PASSES, t=PACK, i=16),
-            in_=w4_plane[:].rearrange("p (a m i t) -> p a m t i", a=PASSES, t=PACK, i=16),
+            in_=w4_rows[:].rearrange("p (a m i t) -> p a m t i", a=PASSES, t=PACK, i=16),
         )
 
         bid_turned = bank(BANKS - 1)
@@ -208,148 +200,136 @@ def tile_list_auction_slot_scores_kernel(
         warm_sigmoid = keep.tile([P, 1], F32, name="warm_sigmoid")
         nc.scalar.activation(out=warm_sigmoid[:], in_=ln_bid[:, 0:1], func=ACT.Sigmoid)
 
-        late = slot([P, H * PACK], BF16, "wg_bf1", "s_w4s")
-        round_wg(nc.vector.tensor_copy, late, 1, 1, PACK)
-        round_wg(nc.scalar.copy, late, 1, 0, 1)
-        quantise_wg(late, 1, 0, PACK, "s_wc1")
-        gather_v(1, "s_w4s")
+        wg_late = slot([P, PACK * H], BF16, "wg_late", "w4_rows")
+        round_wg(nc.vector.tensor_copy, wg_late, 1, 1, PACK)
+        round_wg(nc.scalar.copy, wg_late, 1, 0, 1)
+        wg_mx.append(quantise_wg(wg_late, 1, "wg_codes1"))
+        v_codes.append(gather_v(1, "w4_rows", CUTS))
 
-        def runs(lo, hi):
-            return ((lo, hi),)
+        def first_stage(acc, weights, scales, a, lo, hi):
+            nc.tensor.matmul_mx(
+                out=acc[:, lo:hi], lhsT=weights, lhsT_scale=scales,
+                rhs=v_codes[a][:, lo:hi].bitcast(FP8X4), rhs_scale=v_scale[a][:, lo:hi],
+                start=(a == 0), stop=(a == PASSES - 1),
+            )
 
         def gate_pass(acc, t, a, lo=0, hi=S):
-            for n0, n1 in runs(lo, hi):
-                nc.tensor.matmul_mx(
-                    out=acc[:, n0:n1],
-                    lhsT=wg_codes[a, t].bitcast(FP8X4), lhsT_scale=wg_scale[a, t],
-                    rhs=v_codes[a][:, n0:n1].bitcast(FP8X4), rhs_scale=v_scale[a][:, n0:n1],
-                    start=(a == 0 and n0 == lo), stop=(a == PASSES - 1 and n1 == hi),
-                )
+            codes, scale = wg_mx[a]
+            cols = slice(P * t, P * (t + 1))
+            first_stage(acc, codes[:, cols].bitcast(FP8X4), scale[:, cols], a, lo, hi)
 
         def feat_pass(acc, t, a, lo=0, hi=S):
             c0 = a * H + P * t
-            for n0, n1 in runs(lo, hi):
-                nc.tensor.matmul_mx(
-                    out=acc[:, n0:n1],
-                    lhsT=w4_codes[:, 2 * c0 : 2 * (c0 + P)].bitcast(FP4X4),
-                    lhsT_scale=w4_scale[:, c0 : c0 + P],
-                    rhs=v_codes[a][:, n0:n1].bitcast(FP8X4), rhs_scale=v_scale[a][:, n0:n1],
-                    start=(a == 0 and n0 == lo), stop=(a == PASSES - 1 and n1 == hi),
-                )
+            first_stage(acc, w4_codes[:, 2 * c0 : 2 * (c0 + P)].bitcast(FP4X4), w4_scale[:, c0 : c0 + P], a, lo, hi)
 
-        def on_piece(shape, dtype, name, c):
-            return links.tile(shape, dtype, name=name, align_bytes=64, offset=2 * PACK * PIECES[c][0])
-
-        sigs = [slot([P, S], F32, "sig%d" % t, "s_sig%d" % t) for t in range(PACK)]
+        sigs = [slot([P, S], F32, "sig%d" % t, "sig%d" % t) for t in range(PACK)]
 
         def sigmoid(acc, t, lo=0, hi=S):
             nc.scalar.activation(out=sigs[t][:, lo:hi], in_=acc[:, lo:hi], func=ACT.Sigmoid)
 
-        def weigh(h, acc, t, lo=0, hi=S):
-            nc.vector.tensor_tensor(h[:], acc[:, lo:hi], sigs[t][:, lo:hi], ALU.mult)
-
-        def put(h, factors, t, lo=0, hi=S):
-            nc.vector.tensor_tensor(page[t][:].indirect(idx3[:, lo // 16 : hi // 16]), h[:], factors, ALU.mult)
-
         gate_cut = [bank(u) for u in range(3)]
         feat_cut = [bank(3 + u) for u in range(3)]
-        gate, feat = {second: bank(6)}, {second: bank(7)}
+        gate, feat = {SECOND: bank(6)}, {SECOND: bank(7)}
         for u, (lo, hi) in enumerate(CUTS):
-            gate_pass(gate_cut[u], first, 0, lo, hi)
-        gate_pass(gate[second], second, 0)
+            gate_pass(gate_cut[u], FIRST, 0, lo, hi)
+        gate_pass(gate[SECOND], SECOND, 0)
         for u, (lo, hi) in enumerate(CUTS):
-            feat_pass(feat_cut[u], first, 0, lo, hi)
-        feat_pass(feat[second], second, 0)
+            feat_pass(feat_cut[u], FIRST, 0, lo, hi)
+        feat_pass(feat[SECOND], SECOND, 0)
         for u, (lo, hi) in enumerate(CUTS):
-            gate_pass(gate_cut[u], first, 1, lo, hi)
-            sigmoid(gate_cut[u], first, lo, hi)
-            feat_pass(feat_cut[u], first, 1, lo, hi)
-        gate_pass(gate[second], second, 1)
-        sigmoid(gate[second], second)
-        feat_pass(feat[second], second, 1)
-        for u, t in enumerate((third, last)):
+            gate_pass(gate_cut[u], FIRST, 1, lo, hi)
+            sigmoid(gate_cut[u], FIRST, lo, hi)
+            feat_pass(feat_cut[u], FIRST, 1, lo, hi)
+        gate_pass(gate[SECOND], SECOND, 1)
+        sigmoid(gate[SECOND], SECOND)
+        feat_pass(feat[SECOND], SECOND, 1)
+        for u, t in enumerate((THIRD, LAST)):
             gate[t] = bank(u)
             for a in range(PASSES):
                 gate_pass(gate[t], t, a)
             sigmoid(gate[t], t)
-        for u, t in enumerate((last, third)):
+        for u, t in enumerate((THIRD, LAST)):
             feat[t] = bank(3 + u)
             for a in range(PASSES):
                 feat_pass(feat[t], t, a)
 
-        half = S2 // 2
-        hs = {third: slot([P, S], F32, "feat_third", "s_feat")}
-        nc.scalar.copy(out=hs[third][:], in_=feat[third][:])
-        gated = slot([P, S], F32, "gated", "s_gated")
-        nc.gpsimd.tensor_tensor(gated[:], sigs[third][:], wgs_of[third], ALU.mult)
-        wgs_of[third] = gated[:]
         warm_exp = keep.tile([P, 1], F32, name="warm_exp")
-        nc.scalar.activation(out=warm_exp[:], in_=sigs[last][:, 0:1], func=ACT.Exp)
+        nc.scalar.activation(out=warm_exp[:], in_=sigs[LAST][:, 0:1], func=ACT.Exp)
 
-        page_bf = on_piece([P, T2 * PACK], BF16, "page_bf", 0)
+        def weigh(h, acc, t, lo=0, hi=S):
+            nc.vector.tensor_tensor(h[:], acc[:, lo:hi], sigs[t][:, lo:hi], ALU.mult)
+            return h
 
-        def product(t, tag):
-            hs[t] = slot([P, S], F32, "h%d" % t, tag)
-            weigh(hs[t], feat[t], t)
+        def put(h, weights, t, lo=0, hi=S):
+            nc.vector.tensor_tensor(page[t][:].indirect(entries(idx3, lo, hi)), h[:], weights, ALU.mult)
+
+        rounded = [at([P, PACK * BANK], BF16, "rounded%d" % c, rounded_at + 2 * PACK * BANK * c) for c in range(HALVES)]
 
         def round_page(copy, t, lo, hi):
-            copy(out=page_bf[:, PACK * lo + t : PACK * hi : PACK], in_=page[t][:, lo:hi])
+            start = PACK * (lo % BANK)
+            copy(out=rounded[lo // BANK][:, start + t : start + PACK * (hi - lo) : PACK], in_=page[t][:, lo:hi])
 
-        h_ab = [links.tile([P, P], F32, name="h_cut%d" % u, align_bytes=64, offset=early + (4 * S + P) * u) for u in range(2)]
-        for u in range(2):
-            weigh(h_ab[u], feat_cut[u], first, *CUTS[u])
-        put(h_ab[0], wgs_cut[0], first, *CUTS[0])
-        h_c = links.tile([P, S // 2], F32, name="h_cut2", align_bytes=64, offset=early - 2 * S + 64)
-        weigh(h_c, feat_cut[2], first, *CUTS[2])
-        put(h_ab[1], wgs_cut[1], first, *CUTS[1])
-        hs[second] = links.tile([P, S], F32, name="h_second", align_bytes=64, offset=early + 64)
-        weigh(hs[second], feat[second], second)
-        product(last, "s_sig%d" % first)
-        put(h_c, wgs_cut[2], first, *CUTS[2])
-        for t in ORDER:
-            if t != first:
-                put(hs[t], wgs_of[t], t)
-            for lo, hi in PIECES[:3] if t == last else ((0, T2),):
-                round_page(nc.scalar.copy, t, lo, hi)
+        h_a = weigh(at([P, P], F32, "h_a", products_at), feat_cut[0], FIRST, *CUTS[0])
+        h_b = weigh(fresh([P, P], F32, "h_b"), feat_cut[1], FIRST, *CUTS[1])
+        put(h_a, wgs_half[0][:, 0:P], FIRST, *CUTS[0])
+        h_c = weigh(at([P, 2 * P], F32, "h_c", products_at - 2 * S + 64), feat_cut[2], FIRST, *CUTS[2])
+        put(h_b, wgs_half[0][:, P : 2 * P], FIRST, *CUTS[1])
+        hs = {SECOND: weigh(at([P, S], F32, "h_second", products_at + 64), feat[SECOND], SECOND)}
+        hs[THIRD] = weigh(slot([P, S], F32, "h_third", "sig%d" % FIRST), feat[THIRD], THIRD)
+        put(h_c, wgs_half[1][:], FIRST, *CUTS[2])
+        hs[LAST] = weigh(slot([P, S], F32, "h_last", "sig%d" % SECOND), feat[LAST], LAST)
+        for c in range(HALVES):
+            round_page(nc.scalar.copy, FIRST, BANK * c, BANK * (c + 1))
+        for t in (SECOND, THIRD):
+            put(hs[t], factors[t], t)
+            for c in range(HALVES):
+                round_page(nc.scalar.copy, t, BANK * c, BANK * (c + 1))
+        put(hs[LAST], factors[LAST], LAST)
 
-        v2_codes = []
-        page_codes = [keep.tile([P, BANK], U32, name="page_codes0", align_bytes=64), fresh([P, BANK], U32, "page_codes1")]
-        page_scale = [keep.tile([P, BANK], U8, name="page_scale%d" % c, align_bytes=64) for c in range(HALVES)]
+        def round_last(copy, quarter):
+            round_page(copy, LAST, QUARTER * quarter, QUARTER * (quarter + 1))
 
-        def gather_v2(u, codes):
-            v2_codes.append(codes)
-            nc.vector.tensor_copy(v2_codes[u][:], tab2[:].indirect(idx2[:, u * half // 16 : (u + 1) * half // 16]))
+        page_codes = [fresh([P, BANK], U32, "page_codes%d" % c) for c in range(HALVES)]
+        page_scale = [fresh([P, BANK], U8, "page_scale%d" % c) for c in range(HALVES)]
+        v2_codes = {}
 
-        def quantise_page(c):
-            lo, hi = PIECES[c]
-            cols = slice(lo % BANK, lo % BANK + hi - lo)
+        def gather_v2(i0, i1, offset):
+            codes = at([P, (i1 - i0) * P], U32, "v2_codes%d" % i0, offset)
+            nc.vector.tensor_copy(codes[:], tab2[:].indirect(entries(idx2, i0 * P, i1 * P)))
+            for i in range(i0, i1):
+                v2_codes[i] = codes[:, (i - i0) * P : (i - i0 + 1) * P]
+
+        def quantise_page(quarter):
+            c, lo = divmod(QUARTER * quarter, BANK)
             nc.vector.quantize_mx(
-                out=page_codes[lo // BANK][:, cols].bitcast(FP8X4), scales=page_scale[lo // BANK][:, cols],
-                in_=page_bf[:, PACK * lo : PACK * hi],
+                out=page_codes[c][:, lo : lo + QUARTER].bitcast(FP8X4), scales=page_scale[c][:, lo : lo + QUARTER],
+                in_=rounded[c][:, PACK * lo : PACK * (lo + QUARTER)],
             )
 
-        gather_v2(0, links.tile([P, half], U32, name="v2_codes0", align_bytes=64, offset=shared + 4 * T2 - 2 * half))
+        for quarter in range(3):
+            round_last(nc.scalar.copy, quarter)
+        gather_v2(0, 2, first_page_at)
+        gather_v2(6, 8, first_page_at + T2)
         quantise_page(0)
-        round_page(nc.vector.tensor_copy, last, *PIECES[3])
+        round_last(nc.vector.tensor_copy, 3)
         quantise_page(1)
         quantise_page(3)
         quantise_page(2)
-        gather_v2(1, on_piece([P, half], U32, "v2_codes1", 2))
+        gather_v2(2, 6, rounded_at + 2 * PACK * BANK)
 
-        picked, scores = {}, {}
+        scores, picked = {}, {}
 
         def parts(i):
-            return [(0, PICKS // 2), (PICKS // 2, PICKS)] if i == TILES - 1 else [(0, PICKS)]
+            return ((0, PICKS // 2), (PICKS // 2, PICKS)) if i == TILES - 1 else ((0, PICKS),)
 
         def score(i, c):
             if c == 0:
-                scores[i] = slot([P, T2], F32, "e%d" % i, "s_tab2" if i == 1 else "s_e%d" % (i % 4))
+                scores[i] = slot([P, T2], F32, "e%d" % i, "tab2" if i == 1 else "e%d" % (i % 4))
             acc = bank(4 * c + i % 4)
-            entries = slice((i % 4) * P, (i % 4 + 1) * P)
-            for lo, hi in (PIECES[:2], PIECES[1::-1])[c] if i == 0 else ((0, BANK),):
+            for lo, hi in ((0, QUARTER), (QUARTER, BANK))[:: 1 - 2 * c] if i == 0 else ((0, BANK),):
                 nc.tensor.matmul_mx(
                     out=acc[:, lo:hi],
-                    lhsT=v2_codes[i // 4][:, entries].bitcast(FP8X4), lhsT_scale=v2_scale[:, i * P : (i + 1) * P],
+                    lhsT=v2_codes[i].bitcast(FP8X4), lhsT_scale=v2_scale[:, i * P : (i + 1) * P],
                     rhs=page_codes[c][:, lo:hi].bitcast(FP8X4), rhs_scale=page_scale[c][:, lo:hi],
                     start=True, stop=True,
                 )
@@ -357,23 +337,22 @@ def tile_list_auction_slot_scores_kernel(
             empty(out=scores[i][:, c * BANK : (c + 1) * BANK], in_=acc[:])
 
         def pick(i):
-            e = scores[i]
             picked[i] = []
             for lo, hi in parts(i):
-                x = ring.tile([P, hi - lo], F32, name="x", bufs=TILES + 1)
-                nc.vector.tensor_copy(x[:], e[:].indirect(idx4[:, lo // 16 : hi // 16]))
+                x = ring.tile([P, hi - lo], F32, name="x")
+                nc.vector.tensor_copy(x[:], scores[i][:].indirect(entries(idx4, lo, hi)))
                 picked[i].append(x)
 
-        def back(i):
-            finish = nc.vector if i >= TILES - 2 else nc.gpsimd
+        def finish(i):
+            engine = nc.vector if i >= TILES - 2 else nc.gpsimd
             for x, (lo, hi) in zip(picked[i], parts(i)):
-                ex = ring.tile([P, hi - lo], F32, name="ex", bufs=TILES + 1)
+                ex = ring.tile([P, hi - lo], F32, name="ex")
                 nc.scalar.activation(out=ex[:], in_=x[:], func=ACT.Exp, bias=ln_bid[:, i : i + 1])
                 if i == TILES - 2:
-                    res = slot([P, hi - lo], F32, "res_late", "s_e3")
+                    res = slot([P, hi - lo], F32, "res_late", "e3")
                 else:
-                    res = ring.tile([P, hi - lo], F32, name="res", bufs=TILES)
-                finish.tensor_tensor(res[:], ex[:], reserve_sb[i // 4][:, i % 4, lo:hi], ALU.subtract)
+                    res = ring.tile([P, hi - lo], F32, name="res")
+                engine.tensor_tensor(res[:], ex[:], reserve_sb[i // 4][:, i % 4, lo:hi], ALU.subtract)
                 nc.sync.dma_start(out=out[i * P : (i + 1) * P, lo:hi], in_=res[:])
 
         for c in range(HALVES):
@@ -388,7 +367,7 @@ def tile_list_auction_slot_scores_kernel(
         for i in range(TILES):
             if i + 1 < TILES:
                 pick(i + 1)
-            back(i)
+            finish(i)
             count = {0: 2, 2: 3, 4: 2}.get(i, 1)
             for tile, c in rest[taken : taken + count]:
                 score(tile, c)

@@ -75,12 +75,12 @@ def tile_list_auction_slot_scores_kernel(
         bid_rows = keep.tile([P, P], F32, name="bid_rows")
         identity = keep.tile([P, P], F32, name="identity")
         v2_scale = fresh([P, S2], U8, "v2_scale")
+        nc.gpsimd.memset(words(w4_rows[:]), 0)
         nc.gpsimd.memset(words(tab_rows[64:P, :]), 0)
         nc.vector.memset(words(tab_rows[32:64, :]), 0)
         nc.gpsimd.memset(one[:], 1.0)
         nc.vector.memset(words(tab2_rows[:]), 0)
         nc.gpsimd.memset(bid_rows[:], 0.0)
-        nc.gpsimd.memset(words(w4_rows[:]), 0)
         make_identity(nc, identity[:])
         nc.gpsimd.memset(words(v_scale[1][:]), 0)
         nc.vector.memset(words(v2_scale[:]), 0)
@@ -121,13 +121,13 @@ def tile_list_auction_slot_scores_kernel(
         nc.sync.dma_start(
             out=words(w4_raw[:]).rearrange("p (a n) -> p a n", a=PASSES), in_=words(w4_words).rearrange("a p n -> p a n")
         )
-        nc.sync.dma_start(idx2[:], offs2)
+        for r in range(4):
+            nc.sync.dma_start(out=words(w4_rows[r:P:32, :]), in_=words(w4_scales).rearrange("a (q r) n -> r q a n", r=4)[r])
         load_wg(0)
+        nc.sync.dma_start(idx2[:], offs2)
         nc.sync.dma_start(out=words(tab2_rows[0:P:8, :]), in_=words(tab2_scales[0]))
         load_words(tab[0], tab_words[0], 0, T)
         nc.sync.dma_start(out=bid_rows[0:TILES, :], in_=bid.rearrange("(i p) -> i p", p=P))
-        for r in range(4):
-            nc.sync.dma_start(out=words(w4_rows[r:P:32, :]), in_=words(w4_scales).rearrange("a (q r) n -> r q a n", r=4)[r])
         load_wg(1)
         load_words(tab[1], tab_words[1], 0, T)
         nc.sync.dma_start(idx3[:], offs3)

@@ -306,16 +306,15 @@ def tile_list_auction_slot_scores_kernel(
                 in_=rounded[c][:, PACK * lo : PACK * (lo + QUARTER)],
             )
 
-        for quarter in range(3):
-            round_last(nc.scalar.copy, quarter)
+        for c in range(HALVES):
+            round_last(nc.scalar.copy, 2 * c)
         gather_v2(0, 2, first_page_at)
-        gather_v2(6, 8, first_page_at + T2)
-        quantise_page(0)
-        round_last(nc.vector.tensor_copy, 3)
-        quantise_page(1)
-        quantise_page(3)
-        quantise_page(2)
-        gather_v2(2, 6, rounded_at + 2 * PACK * BANK)
+        for c in range(HALVES):
+            round_last(nc.vector.tensor_copy, 2 * c + 1)
+            quantise_page(2 * c)
+            quantise_page(2 * c + 1)
+        gather_v2(2, 4, rounded_at)
+        gather_v2(4, TILES, rounded_at + 8 * P)
 
         scores, picked = {}, {}
 
@@ -323,17 +322,17 @@ def tile_list_auction_slot_scores_kernel(
             return ((0, PICKS // 2), (PICKS // 2, PICKS)) if i == TILES - 1 else ((0, PICKS),)
 
         def score(i, c):
-            if c == 0:
-                scores[i] = slot([P, T2], F32, "e%d" % i, "tab2" if i == 1 else "e%d" % (i % 4))
+            if i not in scores:
+                scores[i] = slot([P, T2], F32, "e%d" % i, "e%d" % (i % 4))
             acc = bank(4 * c + i % 4)
-            for lo, hi in ((0, QUARTER), (QUARTER, BANK))[:: 1 - 2 * c] if i == 0 else ((0, BANK),):
+            for lo, hi in ((0, QUARTER), (QUARTER, BANK)) if i == 0 else ((0, BANK),):
                 nc.tensor.matmul_mx(
                     out=acc[:, lo:hi],
                     lhsT=v2_codes[i].bitcast(FP8X4), lhsT_scale=v2_scale[:, i * P : (i + 1) * P],
                     rhs=page_codes[c][:, lo:hi].bitcast(FP8X4), rhs_scale=page_scale[c][:, lo:hi],
                     start=True, stop=True,
                 )
-            empty = nc.vector.tensor_copy if (i, c) in ((1, 0), (3, 1), (5, 1)) else nc.scalar.copy
+            empty = nc.vector.tensor_copy if (i, c) in ((3, 1), (7, 1)) else nc.scalar.copy
             empty(out=scores[i][:, c * BANK : (c + 1) * BANK], in_=acc[:])
 
         def pick(i):
@@ -362,13 +361,27 @@ def tile_list_auction_slot_scores_kernel(
             score(2, c)
         score(3, 0)
         pick(0)
-        rest = [(3, 1)] + [(i, c) for i in range(4, TILES) for c in range(HALVES)]
-        taken = 0
-        for i in range(TILES):
-            if i + 1 < TILES:
-                pick(i + 1)
-            finish(i)
-            count = {0: 2, 2: 3, 4: 2}.get(i, 1)
-            for tile, c in rest[taken : taken + count]:
-                score(tile, c)
-            taken = taken + count
+        pick(1)
+        finish(0)
+        score(3, 1)
+        score(4, 0)
+        pick(2)
+        finish(1)
+        score(4, 1)
+        pick(3)
+        finish(2)
+        score(5, 0)
+        score(5, 1)
+        pick(4)
+        score(6, 0)
+        finish(3)
+        score(6, 1)
+        pick(5)
+        score(7, 1)
+        finish(4)
+        score(7, 0)
+        pick(6)
+        finish(5)
+        pick(7)
+        finish(6)
+        finish(7)

@@ -322,7 +322,7 @@ def tile_list_auction_slot_scores_kernel(
             return ((0, PICKS // 2), (PICKS // 2, PICKS)) if i == TILES - 1 else ((0, PICKS),)
 
         def score(i, c):
-            if i not in scores:
+            if c == 0:
                 scores[i] = slot([P, T2], F32, "e%d" % i, "e%d" % (i % 4))
             acc = bank(4 * c + i % 4)
             for lo, hi in ((0, QUARTER), (QUARTER, BANK)) if i == 0 else ((0, BANK),):
@@ -332,7 +332,7 @@ def tile_list_auction_slot_scores_kernel(
                     rhs=page_codes[c][:, lo:hi].bitcast(FP8X4), rhs_scale=page_scale[c][:, lo:hi],
                     start=True, stop=True,
                 )
-            empty = nc.vector.tensor_copy if (i, c) in ((3, 1), (7, 1)) else nc.scalar.copy
+            empty = nc.vector.tensor_copy if (i, c) in ((4, 1), (6, 1), (7, 1)) else nc.scalar.copy
             empty(out=scores[i][:, c * BANK : (c + 1) * BANK], in_=acc[:])
 
         def pick(i):
@@ -359,29 +359,11 @@ def tile_list_auction_slot_scores_kernel(
                 score(i, c)
         for c in range(HALVES):
             score(2, c)
-        score(3, 0)
         pick(0)
-        pick(1)
-        finish(0)
-        score(3, 1)
-        score(4, 0)
-        pick(2)
-        finish(1)
-        score(4, 1)
-        pick(3)
-        finish(2)
-        score(5, 0)
-        score(5, 1)
-        pick(4)
-        score(6, 0)
-        finish(3)
-        score(6, 1)
-        pick(5)
-        score(7, 1)
-        finish(4)
-        score(7, 0)
-        pick(6)
-        finish(5)
-        pick(7)
-        finish(6)
-        finish(7)
+        for i in range(TILES):
+            if i + 1 < TILES:
+                pick(i + 1)
+            finish(i)
+            if i + 3 < TILES:
+                for c in range(HALVES):
+                    score(i + 3, c)

@@ -308,13 +308,15 @@ def tile_list_auction_slot_scores_kernel(
 
         for c in range(HALVES):
             round_last(nc.scalar.copy, 2 * c)
+        round_page(nc.scalar.copy, LAST, 3 * QUARTER, T2 - P)
         gather_v2(0, 2, first_page_at)
+        gather_v2(7, 8, first_page_at + T2)
         for c in range(HALVES):
-            round_last(nc.vector.tensor_copy, 2 * c + 1)
+            round_page(nc.vector.tensor_copy, LAST, *((QUARTER, BANK), (T2 - P, T2))[c])
             quantise_page(2 * c)
             quantise_page(2 * c + 1)
         gather_v2(2, 4, rounded_at)
-        gather_v2(4, TILES, rounded_at + 8 * P)
+        gather_v2(4, 7, rounded_at + 8 * P)
 
         scores, picked = {}, {}
 
@@ -332,7 +334,7 @@ def tile_list_auction_slot_scores_kernel(
                     rhs=page_codes[c][:, lo:hi].bitcast(FP8X4), rhs_scale=page_scale[c][:, lo:hi],
                     start=True, stop=True,
                 )
-            empty = nc.vector.tensor_copy if (i, c) in ((4, 1), (6, 1), (7, 1)) else nc.scalar.copy
+            empty = nc.vector.tensor_copy if (i, c) in ((4, 1), (6, 1)) else nc.scalar.copy
             empty(out=scores[i][:, c * BANK : (c + 1) * BANK], in_=acc[:])
 
         def pick(i):

@@ -26,7 +26,7 @@ TILES = S2 // P
 HALVES = T2 // BANK
 QUARTER = T2 // 4
 FIRST, SECOND, THIRD, LAST = 2, 0, 1, 3
-CUTS = ((0, P), (P, 2 * P), (2 * P, S))
+CUTS = ((2 * P, 3 * P), (3 * P, S), (0, 2 * P))
 
 
 def tile_list_auction_slot_scores_kernel(
@@ -61,6 +61,7 @@ def tile_list_auction_slot_scores_kernel(
         rounded_at = 0
         first_page_at = rounded_at + 2 * PACK * T2
         products_at = first_page_at + 4 * T2 + 2 * S
+        first_sig_at = products_at + 8 * S
 
         idx = keep.tile([P, S // 16], U16, name="idx")
         idx2 = keep.tile([P, S2 // 16], U16, name="idx2")
@@ -95,10 +96,11 @@ def tile_list_auction_slot_scores_kernel(
             at([P, T2], F32, "page%d" % t, first_page_at) if t == FIRST else fresh([P, T2], F32, "page%d" % t)
             for t in range(PACK)
         ]
-        wgs_half = [fresh([P, S // 2], F32, "wgs_half%d" % u) for u in range(2)]
+        wgs_early = fresh([P, S // 2], F32, "wgs_early")
+        wgs_next = fresh([P, S + S // 2], F32, "wgs_next")
         wgs_second = fresh([P, S], F32, "wgs_second")
-        wgs_rest = fresh([P, 2, S], F32, "wgs_rest")
-        factors = {SECOND: wgs_second[:], THIRD: wgs_rest[:, 0, :], LAST: wgs_rest[:, 1, :]}
+        wgs_last = fresh([P, S], F32, "wgs_last")
+        factors = {SECOND: wgs_second[:], LAST: wgs_last[:]}
         reserve_sb = [keep.tile([P, 4, PICKS], F32, name="reserve%d" % u) for u in range(2)]
         page_rows = page0.rearrange("(p t) c -> t p c", t=PACK)
         wgs_rows = wgs.rearrange("(p t) j -> p t j", t=PACK)
@@ -132,12 +134,12 @@ def tile_list_auction_slot_scores_kernel(
         load_words(tab[1], tab_words[1], 0, T)
         nc.sync.dma_start(idx3[:], offs3)
         load_page(FIRST)
-        load_wgs(wgs_half[0], wgs_rows[:, FIRST, 0 : S // 2], (0, 2, 1, 3))
+        load_wgs(wgs_early, wgs_rows[:, FIRST, S // 2 : S], (0, 2, 1, 3))
+        load_wgs(wgs_next, wgs.rearrange("(p t) j -> p (t j)", t=PACK)[:, THIRD * S : FIRST * S + S // 2], (0, 2, 1, 3))
         load_page(SECOND)
-        load_wgs(wgs_half[1], wgs_rows[:, FIRST, S // 2 : S], (0, 2, 1, 3))
         load_wgs(wgs_second, wgs_rows[:, SECOND, :], (0, 2, 1, 3))
         load_page(THIRD)
-        load_wgs(wgs_rest, wgs_rows[:, THIRD : PACK : LAST - THIRD, :], (0, 2, 1, 3))
+        load_wgs(wgs_last, wgs_rows[:, LAST, :], (0, 2, 1, 3))
         load_words(tab2, tab2_words[0], 0, T3 - P)
         load_page(LAST)
         load_words(tab2, tab2_words[0], T3 - P, T3)
@@ -222,7 +224,7 @@ def tile_list_auction_slot_scores_kernel(
             c0 = a * H + P * t
             first_stage(acc, w4_codes[:, 2 * c0 : 2 * (c0 + P)].bitcast(FP4X4), w4_scale[:, c0 : c0 + P], a, lo, hi)
 
-        sigs = [slot([P, S], F32, "sig%d" % t, "sig%d" % t) for t in range(PACK)]
+        sigs = [at([P, S], F32, "sig%d" % t, first_sig_at) if t == FIRST else fresh([P, S], F32, "sig%d" % t) for t in range(PACK)]
 
         def sigmoid(acc, t, lo=0, hi=S):
             nc.scalar.activation(out=sigs[t][:, lo:hi], in_=acc[:, lo:hi], func=ACT.Sigmoid)
@@ -248,7 +250,7 @@ def tile_list_auction_slot_scores_kernel(
             for a in range(PASSES):
                 gate_pass(gate[t], t, a)
             sigmoid(gate[t], t)
-        for u, t in enumerate((THIRD, LAST)):
+        for u, t in enumerate((LAST, THIRD)):
             feat[t] = bank(3 + u)
             for a in range(PASSES):
                 feat_pass(feat[t], t, a)
@@ -271,13 +273,17 @@ def tile_list_auction_slot_scores_kernel(
 
         h_a = weigh(at([P, P], F32, "h_a", products_at), feat_cut[0], FIRST, *CUTS[0])
         h_b = weigh(fresh([P, P], F32, "h_b"), feat_cut[1], FIRST, *CUTS[1])
-        put(h_a, wgs_half[0][:, 0:P], FIRST, *CUTS[0])
+        put(h_a, wgs_early[:, 0:P], FIRST, *CUTS[0])
         h_c = weigh(at([P, 2 * P], F32, "h_c", products_at - 2 * S + 64), feat_cut[2], FIRST, *CUTS[2])
-        put(h_b, wgs_half[0][:, P : 2 * P], FIRST, *CUTS[1])
+        put(h_b, wgs_early[:, P : 2 * P], FIRST, *CUTS[1])
         hs = {SECOND: weigh(at([P, S], F32, "h_second", products_at + 64), feat[SECOND], SECOND)}
-        hs[THIRD] = weigh(slot([P, S], F32, "h_third", "sig%d" % FIRST), feat[THIRD], THIRD)
-        put(h_c, wgs_half[1][:], FIRST, *CUTS[2])
-        hs[LAST] = weigh(slot([P, S], F32, "h_last", "sig%d" % SECOND), feat[LAST], LAST)
+        hs[LAST] = weigh(at([P, S], F32, "h_last", first_sig_at + 2 * S), feat[LAST], LAST)
+        gated = at([P, S], F32, "gated", first_sig_at - 2 * S)
+        nc.gpsimd.tensor_tensor(gated[:], sigs[THIRD][:], wgs_next[:, 0:S], ALU.mult)
+        factors[THIRD] = gated[:]
+        hs[THIRD] = fresh([P, S], F32, "feat_third")
+        nc.scalar.copy(out=hs[THIRD][:], in_=feat[THIRD][:])
+        put(h_c, wgs_next[:, S:], FIRST, *CUTS[2])
         for c in range(HALVES):
             round_page(nc.scalar.copy, FIRST, BANK * c, BANK * (c + 1))
         for t in (SECOND, THIRD):
@@ -353,8 +359,11 @@ def tile_list_auction_slot_scores_kernel(
                     res = slot([P, hi - lo], F32, "res_late", "e3")
                 else:
                     res = ring.tile([P, hi - lo], F32, name="res")
-                engine.tensor_tensor(res[:], ex[:], reserve_sb[i // 4][:, i % 4, lo:hi], ALU.subtract)
-                nc.sync.dma_start(out=out[i * P : (i + 1) * P, lo:hi], in_=res[:])
+                width = PICKS // 2 if i >= TILES - 2 else PICKS
+                for n in range(0, hi - lo, width):
+                    cols = slice(lo + n, lo + n + width)
+                    engine.tensor_tensor(res[:, n : n + width], ex[:, n : n + width], reserve_sb[i // 4][:, i % 4, cols], ALU.subtract)
+                    nc.sync.dma_start(out=out[i * P : (i + 1) * P, cols], in_=res[:, n : n + width])
 
         for c in range(HALVES):
             for i in range(2):

@@ -340,8 +340,10 @@ def tile_list_auction_slot_scores_kernel(
                     rhs=page_codes[c][:, lo:hi].bitcast(FP8X4), rhs_scale=page_scale[c][:, lo:hi],
                     start=True, stop=True,
                 )
-            empty = nc.vector.tensor_copy if (i, c) in ((4, 1), (6, 1)) else nc.scalar.copy
-            empty(out=scores[i][:, c * BANK : (c + 1) * BANK], in_=acc[:])
+            split = {(1, 0): QUARTER, (4, 1): 0, (6, 1): 0}.get((i, c), BANK)
+            for empty, lo, hi in ((nc.scalar.copy, 0, split), (nc.vector.tensor_copy, split, BANK)):
+                if lo < hi:
+                    empty(out=scores[i][:, c * BANK + lo : c * BANK + hi], in_=acc[:, lo:hi])
 
         def pick(i):
             picked[i] = []

@@ -125,12 +125,33 @@ def tile_list_auction_slot_scores_kernel(
         )
         for r in range(4):
             nc.sync.dma_start(out=words(w4_rows[r:P:32, :]), in_=words(w4_scales).rearrange("a (q r) n -> r q a n", r=4)[r])
+        v_rows = fresh([P, S], U8, "v_rows")
+        nc.vector.tensor_copy(v_rows[:], tab_rows[:].indirect(idx[:]))
+        w4_codes = fresh([P, PASSES * 2 * H], U8, "w4_codes")
+        nc.vector.tensor_copy(
+            out=w4_codes[:].bitcast(U16).rearrange("p (a t m i) -> p a m t i", a=PASSES, t=PACK, i=8),
+            in_=w4_raw[:].bitcast(U16).rearrange("p (a m i t) -> p a m t i", a=PASSES, t=PACK, i=8),
+        )
+        nc.vector.tensor_copy(words(v_scale[0][:]), words(v_rows[:]))
+        w4_scale = fresh([P, PASSES * H], U8, "w4_scale")
+        nc.vector.tensor_copy(
+            out=w4_scale[:].rearrange("p (a t m i) -> p a m t i", a=PASSES, t=PACK, i=16),
+            in_=w4_rows[:].rearrange("p (a m i t) -> p a m t i", a=PASSES, t=PACK, i=16),
+        )
+
+        def carry(a):
+            for q in range(1 - a, 4):
+                src = 16 * a + 4 * q
+                nc.sync.dma_start(out=words(v_scale[a][32 * q : 32 * q + 4, :]), in_=words(v_rows[src : src + 4, :]))
+
         load_wg(0)
         nc.sync.dma_start(idx2[:], offs2)
         nc.sync.dma_start(out=words(tab2_rows[0:P:8, :]), in_=words(tab2_scales[0]))
         load_words(tab[0], tab_words[0], 0, T)
         nc.sync.dma_start(out=bid_rows[0:TILES, :], in_=bid.rearrange("(i p) -> i p", p=P))
+        carry(0)
         load_wg(1)
+        carry(1)
         load_words(tab[1], tab_words[1], 0, T)
         nc.sync.dma_start(idx3[:], offs3)
         load_page(FIRST)
@@ -149,19 +170,6 @@ def tile_list_auction_slot_scores_kernel(
                 out=reserve_sb[u][:], in_=reserve[512 * u : 512 * (u + 1), :].rearrange("(i p) m -> p i m", p=P)
             )
 
-        v_rows = fresh([P, S], U8, "v_rows")
-        nc.vector.tensor_copy(v_rows[:], tab_rows[:].indirect(idx[:]))
-        nc.vector.tensor_copy(words(v_scale[0][:]), words(v_rows[:]))
-        for a in range(PASSES):
-            for q in range(1 - a, 4):
-                src = 16 * a + 4 * q
-                nc.gpsimd.dma_start(out=words(v_scale[a][32 * q : 32 * q + 4, :]), in_=words(v_rows[src : src + 4, :]))
-
-        w4_codes = fresh([P, PASSES * 2 * H], U8, "w4_codes")
-        nc.vector.tensor_copy(
-            out=w4_codes[:].bitcast(U16).rearrange("p (a t m i) -> p a m t i", a=PASSES, t=PACK, i=8),
-            in_=w4_raw[:].bitcast(U16).rearrange("p (a m i t) -> p a m t i", a=PASSES, t=PACK, i=8),
-        )
         v2_rows = slot([P, S2], U8, "v2_rows", "tab_rows")
         nc.vector.tensor_copy(v2_rows[:], tab2_rows[:].indirect(idx2[:]))
         for r in range(4):
@@ -189,11 +197,6 @@ def tile_list_auction_slot_scores_kernel(
         round_wg(nc.scalar.copy, wg_early, 0, 0, PACK)
         v_codes = [gather_v(0, "tab2_rows", ((0, S),))]
         wg_mx = [quantise_wg(wg_early, 0, "tab0")]
-        w4_scale = slot([P, PASSES * H], U8, "w4_scale", "wg_early")
-        nc.vector.tensor_copy(
-            out=w4_scale[:].rearrange("p (a t m i) -> p a m t i", a=PASSES, t=PACK, i=16),
-            in_=w4_rows[:].rearrange("p (a m i t) -> p a m t i", a=PASSES, t=PACK, i=16),
-        )
 
         bid_turned = bank(BANKS - 1)
         nc.tensor.transpose(bid_turned[:, 0:P], bid_rows[:], identity[:])
@@ -202,11 +205,11 @@ def tile_list_auction_slot_scores_kernel(
         warm_sigmoid = keep.tile([P, 1], F32, name="warm_sigmoid")
         nc.scalar.activation(out=warm_sigmoid[:], in_=ln_bid[:, 0:1], func=ACT.Sigmoid)
 
-        wg_late = slot([P, PACK * H], BF16, "wg_late", "w4_rows")
+        wg_late = slot([P, PACK * H], BF16, "wg_late", "wg_early")
         round_wg(nc.vector.tensor_copy, wg_late, 1, 1, PACK)
         round_wg(nc.scalar.copy, wg_late, 1, 0, 1)
         wg_mx.append(quantise_wg(wg_late, 1, "wg_codes1"))
-        v_codes.append(gather_v(1, "w4_rows", CUTS))
+        v_codes.append(gather_v(1, "wg_early", CUTS))
 
         def first_stage(acc, weights, scales, a, lo, hi):
             nc.tensor.matmul_mx(

@@ -26,6 +26,7 @@ TILES = S2 // P
 HALVES = T2 // BANK
 QUARTER = T2 // 4
 FIRST, SECOND, THIRD, LAST = 2, 0, 1, 3
+REST = 64
 CUTS = ((2 * P, 3 * P), (3 * P, S), (0, 2 * P))
 
 
@@ -62,6 +63,7 @@ def tile_list_auction_slot_scores_kernel(
         first_page_at = rounded_at + 2 * PACK * T2
         products_at = first_page_at + 4 * T2 + 2 * S
         first_sig_at = products_at + 8 * S
+        page_at = {FIRST: first_page_at, THIRD: first_sig_at + 6 * S, LAST: first_sig_at + 6 * S + 4 * T2}
 
         idx = keep.tile([P, S // 16], U16, name="idx")
         idx2 = keep.tile([P, S2 // 16], U16, name="idx2")
@@ -93,7 +95,7 @@ def tile_list_auction_slot_scores_kernel(
         tab = [slot([P, T], U32, "tab%d" % a, "tab%d" % a) for a in range(PASSES)]
         tab2 = slot([P, T3], U32, "tab2", "tab2")
         page = [
-            at([P, T2], F32, "page%d" % t, first_page_at) if t == FIRST else fresh([P, T2], F32, "page%d" % t)
+            at([P, T2], F32, "page%d" % t, page_at[t]) if t in page_at else fresh([P, T2], F32, "page%d" % t)
             for t in range(PACK)
         ]
         wgs_early = fresh([P, S // 2], F32, "wgs_early")
@@ -292,7 +294,7 @@ def tile_list_auction_slot_scores_kernel(
         for t in (SECOND, THIRD):
             put(hs[t], factors[t], t)
             for c in range(HALVES):
-                round_page(nc.scalar.copy, t, BANK * c, BANK * (c + 1))
+                round_page(nc.scalar.copy, t, BANK * c, min(BANK * (c + 1), T2 - (REST if t == THIRD else 0)))
         put(hs[LAST], factors[LAST], LAST)
 
         def round_last(copy, quarter):
@@ -315,17 +317,21 @@ def tile_list_auction_slot_scores_kernel(
                 in_=rounded[c][:, PACK * lo : PACK * (lo + QUARTER)],
             )
 
-        for c in range(HALVES):
-            round_last(nc.scalar.copy, 2 * c)
+        round_last(nc.scalar.copy, 0)
+        round_page(nc.scalar.copy, THIRD, T2 - REST, T2)
+        round_last(nc.scalar.copy, 2)
         round_page(nc.scalar.copy, LAST, 3 * QUARTER, T2 - P)
-        gather_v2(0, 2, first_page_at)
-        gather_v2(7, 8, first_page_at + T2)
-        for c in range(HALVES):
-            round_page(nc.vector.tensor_copy, LAST, *((QUARTER, BANK), (T2 - P, T2))[c])
-            quantise_page(2 * c)
-            quantise_page(2 * c + 1)
-        gather_v2(2, 4, rounded_at)
-        gather_v2(4, 7, rounded_at + 8 * P)
+        gather_v2(0, 1, page_at[FIRST])
+        round_last(nc.vector.tensor_copy, 1)
+        round_page(nc.vector.tensor_copy, LAST, T2 - P, T2)
+        quantise_page(1)
+        quantise_page(0)
+        gather_v2(1, 2, page_at[THIRD])
+        gather_v2(7, 8, page_at[THIRD] + T2)
+        quantise_page(2)
+        quantise_page(3)
+        gather_v2(2, 4, page_at[LAST])
+        gather_v2(4, 7, page_at[LAST] + T2)
 
         scores, picked = {}, {}
 
@@ -336,14 +342,14 @@ def tile_list_auction_slot_scores_kernel(
             if c == 0:
                 scores[i] = slot([P, T2], F32, "e%d" % i, "e%d" % (i % 4))
             acc = bank(4 * c + i % 4)
-            for lo, hi in ((0, QUARTER), (QUARTER, BANK)) if i == 0 else ((0, BANK),):
+            for lo, hi in {(0, 0): ((QUARTER, BANK), (0, QUARTER)), (0, 1): ((0, QUARTER), (QUARTER, BANK))}.get((i, c), ((0, BANK),)):
                 nc.tensor.matmul_mx(
                     out=acc[:, lo:hi],
                     lhsT=v2_codes[i].bitcast(FP8X4), lhsT_scale=v2_scale[:, i * P : (i + 1) * P],
                     rhs=page_codes[c][:, lo:hi].bitcast(FP8X4), rhs_scale=page_scale[c][:, lo:hi],
                     start=True, stop=True,
                 )
-            split = {(1, 0): QUARTER, (4, 1): 0, (6, 1): 0}.get((i, c), BANK)
+            split = {(4, 1): 0, (6, 1): 0}.get((i, c), BANK)
             for empty, lo, hi in ((nc.scalar.copy, 0, split), (nc.vector.tensor_copy, split, BANK)):
                 if lo < hi:
                     empty(out=scores[i][:, c * BANK + lo : c * BANK + hi], in_=acc[:, lo:hi])

@@ -26,7 +26,7 @@ TILES = S2 // P
 HALVES = T2 // BANK
 QUARTER = T2 // 4
 FIRST, SECOND, THIRD, LAST = 2, 0, 1, 3
-REST = 64
+REST = 16
 CUTS = ((2 * P, 3 * P), (3 * P, S), (0, 2 * P))
 
 
@@ -61,8 +61,8 @@ def tile_list_auction_slot_scores_kernel(
 
         rounded_at = 0
         first_page_at = rounded_at + 2 * PACK * T2
-        products_at = first_page_at + 4 * T2 + 2 * S
-        first_sig_at = products_at + 8 * S
+        products_at = first_page_at + 4 * T2 + 4 * S
+        first_sig_at = products_at + 12 * S
         page_at = {FIRST: first_page_at, THIRD: first_sig_at + 6 * S, LAST: first_sig_at + 6 * S + 4 * T2}
 
         idx = keep.tile([P, S // 16], U16, name="idx")
@@ -120,11 +120,11 @@ def tile_list_auction_slot_scores_kernel(
             for q in quadrants:
                 nc.sync.dma_start(out=tile[32 * q : 32 * (q + 1)], in_=rows)
 
-        nc.sync.dma_start(idx[:], offs)
-        nc.sync.dma_start(out=words(tab_rows[0:32, :]), in_=words(tab_scales).rearrange("a q n -> (a q) n"))
         nc.sync.dma_start(
             out=words(w4_raw[:]).rearrange("p (a n) -> p a n", a=PASSES), in_=words(w4_words).rearrange("a p n -> p a n")
         )
+        nc.sync.dma_start(idx[:], offs)
+        nc.sync.dma_start(out=words(tab_rows[0:32, :]), in_=words(tab_scales).rearrange("a q n -> (a q) n"))
         for r in range(4):
             nc.sync.dma_start(out=words(w4_rows[r:P:32, :]), in_=words(w4_scales).rearrange("a (q r) n -> r q a n", r=4)[r])
         v_rows = fresh([P, S], U8, "v_rows")
@@ -156,8 +156,8 @@ def tile_list_auction_slot_scores_kernel(
         carry(1)
         load_words(tab[1], tab_words[1], 0, T)
         nc.sync.dma_start(idx3[:], offs3)
-        load_page(FIRST)
         load_wgs(wgs_early, wgs_rows[:, FIRST, S // 2 : S], (0, 2, 1, 3))
+        load_page(FIRST)
         load_wgs(wgs_next, wgs.rearrange("(p t) j -> p (t j)", t=PACK)[:, THIRD * S : FIRST * S + S // 2], (0, 2, 1, 3))
         load_page(SECOND)
         load_wgs(wgs_second, wgs_rows[:, SECOND, :], (0, 2, 1, 3))
@@ -213,58 +213,61 @@ def tile_list_auction_slot_scores_kernel(
         wg_mx.append(quantise_wg(wg_late, 1, "wg_codes1"))
         v_codes.append(gather_v(1, "wg_early", CUTS))
 
-        def first_stage(acc, weights, scales, a, lo, hi):
+        def first_stage(acc, weights, scales, a, lo, hi, start, stop):
             nc.tensor.matmul_mx(
-                out=acc[:, lo:hi], lhsT=weights, lhsT_scale=scales,
+                out=acc, lhsT=weights, lhsT_scale=scales,
                 rhs=v_codes[a][:, lo:hi].bitcast(FP8X4), rhs_scale=v_scale[a][:, lo:hi],
-                start=(a == 0), stop=(a == PASSES - 1),
+                start=(a == 0) if start is None else start, stop=(a == PASSES - 1) if stop is None else stop,
             )
 
-        def gate_pass(acc, t, a, lo=0, hi=S):
+        def gate_pass(acc, t, a, lo=0, hi=S, start=None, stop=None):
             codes, scale = wg_mx[a]
             cols = slice(P * t, P * (t + 1))
-            first_stage(acc, codes[:, cols].bitcast(FP8X4), scale[:, cols], a, lo, hi)
+            first_stage(acc, codes[:, cols].bitcast(FP8X4), scale[:, cols], a, lo, hi, start, stop)
 
-        def feat_pass(acc, t, a, lo=0, hi=S):
+        def feat_pass(acc, t, a, lo=0, hi=S, start=None, stop=None):
             c0 = a * H + P * t
-            first_stage(acc, w4_codes[:, 2 * c0 : 2 * (c0 + P)].bitcast(FP4X4), w4_scale[:, c0 : c0 + P], a, lo, hi)
+            first_stage(acc, w4_codes[:, 2 * c0 : 2 * (c0 + P)].bitcast(FP4X4), w4_scale[:, c0 : c0 + P], a, lo, hi, start, stop)
 
-        sigs = [at([P, S], F32, "sig%d" % t, first_sig_at) if t == FIRST else fresh([P, S], F32, "sig%d" % t) for t in range(PACK)]
+        sigs = {t: fresh([P, S], F32, "sig%d" % t) for t in (SECOND, THIRD, LAST)}
+        cut_sigs = [fresh([P, P], F32, "sig_a"), fresh([P, P], F32, "sig_b"), at([P, 2 * P], F32, "sig_c", first_sig_at + S)]
 
-        def sigmoid(acc, t, lo=0, hi=S):
-            nc.scalar.activation(out=sigs[t][:, lo:hi], in_=acc[:, lo:hi], func=ACT.Sigmoid)
+        def sigmoid(acc, gates):
+            nc.scalar.activation(out=gates[:], in_=acc, func=ACT.Sigmoid)
 
-        gate_cut = [bank(u) for u in range(3)]
-        feat_cut = [bank(3 + u) for u in range(3)]
-        gate, feat = {SECOND: bank(6)}, {SECOND: bank(7)}
+        cut_bank = [bank(u) for u in range(3)]
+        gate_cut = [cut_bank[u][:, 0 : hi - lo] for u, (lo, hi) in enumerate(CUTS)]
+        feat_cut = [cut_bank[u][:, BANK // 2 : BANK // 2 + hi - lo] for u, (lo, hi) in enumerate(CUTS)]
+        feat_cut[0] = bank(6)[:, 0:P]
+        gate = {SECOND: bank(3)[:], LAST: bank(5)[:], THIRD: bank(7)[:]}
+        feat = {SECOND: bank(4)[:]}
         for u, (lo, hi) in enumerate(CUTS):
-            gate_pass(gate_cut[u], FIRST, 0, lo, hi)
-        gate_pass(gate[SECOND], SECOND, 0)
-        for u, (lo, hi) in enumerate(CUTS):
-            feat_pass(feat_cut[u], FIRST, 0, lo, hi)
+            feat_pass(feat_cut[u], FIRST, 0, lo, hi, start=True, stop=False)
         feat_pass(feat[SECOND], SECOND, 0)
         for u, (lo, hi) in enumerate(CUTS):
-            gate_pass(gate_cut[u], FIRST, 1, lo, hi)
-            sigmoid(gate_cut[u], FIRST, lo, hi)
-            feat_pass(feat_cut[u], FIRST, 1, lo, hi)
-        gate_pass(gate[SECOND], SECOND, 1)
-        sigmoid(gate[SECOND], SECOND)
+            gate_pass(gate_cut[u], FIRST, 0, lo, hi, start=(u == 0), stop=False)
+        for t in (SECOND, THIRD, LAST):
+            gate_pass(gate[t], t, 0)
+        for u, (lo, hi) in enumerate(CUTS):
+            gate_pass(gate_cut[u], FIRST, 1, lo, hi, start=False, stop=(u == 0))
+            feat_pass(feat_cut[u], FIRST, 1, lo, hi, start=False, stop=True)
+            sigmoid(gate_cut[u], cut_sigs[u])
+        for t in (SECOND, THIRD):
+            gate_pass(gate[t], t, 1)
+            sigmoid(gate[t], sigs[t])
         feat_pass(feat[SECOND], SECOND, 1)
-        for u, t in enumerate((THIRD, LAST)):
-            gate[t] = bank(u)
-            for a in range(PASSES):
-                gate_pass(gate[t], t, a)
-            sigmoid(gate[t], t)
-        for u, t in enumerate((LAST, THIRD)):
-            feat[t] = bank(3 + u)
+        gate_pass(gate[LAST], LAST, 1)
+        sigmoid(gate[LAST], sigs[LAST])
+        for t, k in ((LAST, 0), (THIRD, 6)):
+            feat[t] = bank(k)[:]
             for a in range(PASSES):
                 feat_pass(feat[t], t, a)
 
         warm_exp = keep.tile([P, 1], F32, name="warm_exp")
         nc.scalar.activation(out=warm_exp[:], in_=sigs[LAST][:, 0:1], func=ACT.Exp)
 
-        def weigh(h, acc, t, lo=0, hi=S):
-            nc.vector.tensor_tensor(h[:], acc[:, lo:hi], sigs[t][:, lo:hi], ALU.mult)
+        def weigh(h, acc, factor):
+            nc.vector.tensor_tensor(h[:], acc, factor, ALU.mult)
             return h
 
         def put(h, weights, t, lo=0, hi=S):
@@ -276,18 +279,20 @@ def tile_list_auction_slot_scores_kernel(
             start = PACK * (lo % BANK)
             copy(out=rounded[lo // BANK][:, start + t : start + PACK * (hi - lo) : PACK], in_=page[t][:, lo:hi])
 
-        h_a = weigh(at([P, P], F32, "h_a", products_at), feat_cut[0], FIRST, *CUTS[0])
-        h_b = weigh(fresh([P, P], F32, "h_b"), feat_cut[1], FIRST, *CUTS[1])
-        put(h_a, wgs_early[:, 0:P], FIRST, *CUTS[0])
-        h_c = weigh(at([P, 2 * P], F32, "h_c", products_at - 2 * S + 64), feat_cut[2], FIRST, *CUTS[2])
-        put(h_b, wgs_early[:, P : 2 * P], FIRST, *CUTS[1])
-        hs = {SECOND: weigh(at([P, S], F32, "h_second", products_at + 64), feat[SECOND], SECOND)}
-        hs[LAST] = weigh(at([P, S], F32, "h_last", first_sig_at + 2 * S), feat[LAST], LAST)
+        h_a = at([P, P], F32, "h_a", products_at)
+        h_b = fresh([P, P], F32, "h_b")
+        for u, h in enumerate((h_a, h_b)):
+            nc.vector.tensor_tensor(h[:], feat_cut[u], wgs_early[:, u * P : (u + 1) * P], ALU.mult)
+        put(h_a, cut_sigs[0][:], FIRST, *CUTS[0])
+        h_c = weigh(at([P, 2 * P], F32, "h_c", products_at - 2 * S + 64), feat_cut[2], cut_sigs[2][:])
+        put(h_b, cut_sigs[1][:], FIRST, *CUTS[1])
+        hs = {SECOND: weigh(at([P, S], F32, "h_second", products_at + 64), feat[SECOND], sigs[SECOND][:])}
+        hs[LAST] = weigh(at([P, S], F32, "h_last", first_sig_at + 2 * S), feat[LAST], sigs[LAST][:])
         gated = at([P, S], F32, "gated", first_sig_at - 2 * S)
         nc.gpsimd.tensor_tensor(gated[:], sigs[THIRD][:], wgs_next[:, 0:S], ALU.mult)
         factors[THIRD] = gated[:]
         hs[THIRD] = fresh([P, S], F32, "feat_third")
-        nc.scalar.copy(out=hs[THIRD][:], in_=feat[THIRD][:])
+        nc.scalar.copy(out=hs[THIRD][:], in_=feat[THIRD])
         put(h_c, wgs_next[:, S:], FIRST, *CUTS[2])
         for c in range(HALVES):
             round_page(nc.scalar.copy, FIRST, BANK * c, BANK * (c + 1))
@@ -320,18 +325,14 @@ def tile_list_auction_slot_scores_kernel(
         round_last(nc.scalar.copy, 0)
         round_page(nc.scalar.copy, THIRD, T2 - REST, T2)
         round_last(nc.scalar.copy, 2)
-        round_page(nc.scalar.copy, LAST, 3 * QUARTER, T2 - P)
         gather_v2(0, 1, page_at[FIRST])
         round_last(nc.vector.tensor_copy, 1)
-        round_page(nc.vector.tensor_copy, LAST, T2 - P, T2)
-        quantise_page(1)
-        quantise_page(0)
-        gather_v2(1, 2, page_at[THIRD])
-        gather_v2(7, 8, page_at[THIRD] + T2)
-        quantise_page(2)
-        quantise_page(3)
-        gather_v2(2, 4, page_at[LAST])
-        gather_v2(4, 7, page_at[LAST] + T2)
+        round_last(nc.vector.tensor_copy, 3)
+        for quarter in (1, 0, 3, 2):
+            quantise_page(quarter)
+        gather_v2(1, 2, page_at[LAST])
+        gather_v2(2, 4, page_at[LAST] + T2)
+        gather_v2(4, 6, page_at[LAST] + 2 * T2)
 
         scores, picked = {}, {}
 
@@ -342,7 +343,7 @@ def tile_list_auction_slot_scores_kernel(
             if c == 0:
                 scores[i] = slot([P, T2], F32, "e%d" % i, "e%d" % (i % 4))
             acc = bank(4 * c + i % 4)
-            for lo, hi in {(0, 0): ((QUARTER, BANK), (0, QUARTER)), (0, 1): ((0, QUARTER), (QUARTER, BANK))}.get((i, c), ((0, BANK),)):
+            for lo, hi in {(0, 0): ((QUARTER, BANK), (0, QUARTER)), (0, 1): ((QUARTER, BANK), (0, QUARTER))}.get((i, c), ((0, BANK),)):
                 nc.tensor.matmul_mx(
                     out=acc[:, lo:hi],
                     lhsT=v2_codes[i].bitcast(FP8X4), lhsT_scale=v2_scale[:, i * P : (i + 1) * P],
@@ -357,7 +358,7 @@ def tile_list_auction_slot_scores_kernel(
         def pick(i):
             picked[i] = []
             for lo, hi in parts(i):
-                x = ring.tile([P, hi - lo], F32, name="x")
+                x = at([P, PICKS], F32, "x_first", rounded_at) if i == 0 else ring.tile([P, hi - lo], F32, name="x")
                 nc.vector.tensor_copy(x[:], scores[i][:].indirect(entries(idx4, lo, hi)))
                 picked[i].append(x)
 
@@ -376,16 +377,16 @@ def tile_list_auction_slot_scores_kernel(
                     engine.tensor_tensor(res[:, n : n + width], ex[:, n : n + width], reserve_sb[i // 4][:, i % 4, cols], ALU.subtract)
                     nc.sync.dma_start(out=out[i * P : (i + 1) * P, cols], in_=res[:, n : n + width])
 
-        for c in range(HALVES):
-            for i in range(2):
+        for i in range(3):
+            for c in range(HALVES):
                 score(i, c)
-        for c in range(HALVES):
-            score(2, c)
         pick(0)
         for i in range(TILES):
             if i + 1 < TILES:
                 pick(i + 1)
             finish(i)
+            if i == 0:
+                gather_v2(6, TILES, rounded_at)
             if i + 3 < TILES:
                 for c in range(HALVES):
                     score(i + 3, c)

@@ -27,6 +27,7 @@ HALVES = T2 // BANK
 QUARTER = T2 // 4
 FIRST, SECOND, THIRD, LAST = 2, 0, 1, 3
 REST = 16
+WG_SHARE = 24
 CUTS = ((2 * P, 3 * P), (3 * P, S), (0, 2 * P))
 
 
@@ -75,6 +76,7 @@ def tile_list_auction_slot_scores_kernel(
         w4_rows = slot([P, PASSES * H], U8, "w4_rows", "w4_rows")
         v_scale = [fresh([P, S], U8, "v_scale%d" % a) for a in range(PASSES)]
         one = keep.tile([P, 1], F32, name="one")
+        no_bias = keep.tile([P, 2], F32, name="no_bias")
         bid_rows = keep.tile([P, P], F32, name="bid_rows")
         identity = keep.tile([P, P], F32, name="identity")
         v2_scale = fresh([P, S2], U8, "v2_scale")
@@ -84,6 +86,7 @@ def tile_list_auction_slot_scores_kernel(
         nc.gpsimd.memset(one[:], 1.0)
         nc.vector.memset(words(tab2_rows[:]), 0)
         nc.gpsimd.memset(bid_rows[:], 0.0)
+        nc.gpsimd.memset(no_bias[:], 0.0)
         make_identity(nc, identity[:])
         nc.gpsimd.memset(words(v_scale[1][:]), 0)
         nc.vector.memset(words(v2_scale[:]), 0)
@@ -177,16 +180,18 @@ def tile_list_auction_slot_scores_kernel(
         for r in range(4):
             nc.sync.dma_start(out=words(v2_scale[r:P:32, :]), in_=words(v2_rows[8 * r : P : 32, :]))
 
-        def round_wg(copy, rounded, a, t0, t1):
+        def round_wg(copy, rounded, a, m0, m1, t0=0, t1=PACK):
             copy(
-                out=rounded[:, t0 * H : t1 * H].rearrange("p (t m j) -> p m t j", m=P, j=PACK),
-                in_=wg_raw[a][:].rearrange("p j (m t) -> p m t j", t=PACK)[:, :, t0:t1, :],
+                out=rounded[:].rearrange("p (t m j) -> p m t j", m=P, j=PACK)[:, m0:m1, t0:t1],
+                in_=wg_raw[a][:].rearrange("p j (m t) -> p m t j", t=PACK)[:, m0:m1, t0:t1],
             )
 
-        def quantise_wg(rounded, a, tag):
+        def quantise_wg(rounded, a, tag, runs):
             codes = slot([P, H], U32, "wg_codes%d" % a, tag)
             scale = fresh([P, H], U8, "wg_scale%d" % a)
-            nc.vector.quantize_mx(out=codes[:].bitcast(FP8X4), scales=scale[:], in_=rounded[:])
+            for t0, t1 in runs:
+                cols = slice(P * t0, P * t1)
+                nc.vector.quantize_mx(out=codes[:, cols].bitcast(FP8X4), scales=scale[:, cols], in_=rounded[:, H * t0 : H * t1])
             return codes, scale
 
         def gather_v(a, tag, cuts):
@@ -196,21 +201,21 @@ def tile_list_auction_slot_scores_kernel(
             return codes
 
         wg_early = slot([P, PACK * H], BF16, "wg_early", "wg_early")
-        round_wg(nc.scalar.copy, wg_early, 0, 0, PACK)
+        round_wg(nc.scalar.copy, wg_early, 0, 0, P)
         v_codes = [gather_v(0, "tab2_rows", ((0, S),))]
-        wg_mx = [quantise_wg(wg_early, 0, "tab0")]
+        wg_mx = [quantise_wg(wg_early, 0, "tab0", ((0, PACK),))]
 
         bid_turned = bank(BANKS - 1)
         nc.tensor.transpose(bid_turned[:, 0:P], bid_rows[:], identity[:])
         ln_bid = fresh([P, TILES], F32, "ln_bid")
-        nc.scalar.activation(out=ln_bid[:], in_=bid_turned[:, 0:TILES], func=ACT.Ln)
-        warm_sigmoid = keep.tile([P, 1], F32, name="warm_sigmoid")
-        nc.scalar.activation(out=warm_sigmoid[:], in_=ln_bid[:, 0:1], func=ACT.Sigmoid)
+        nc.scalar.activation(out=ln_bid[:], in_=bid_turned[:, 0:TILES], func=ACT.Ln, bias=no_bias[:, 0:1])
+        nc.scalar.activation(out=no_bias[:, 0:1], in_=one[:], func=ACT.Sigmoid)
 
         wg_late = slot([P, PACK * H], BF16, "wg_late", "wg_early")
-        round_wg(nc.vector.tensor_copy, wg_late, 1, 1, PACK)
-        round_wg(nc.scalar.copy, wg_late, 1, 0, 1)
-        wg_mx.append(quantise_wg(wg_late, 1, "wg_codes1"))
+        round_wg(nc.vector.tensor_copy, wg_late, 1, 0, P, 2, PACK)
+        round_wg(nc.vector.tensor_copy, wg_late, 1, 0, WG_SHARE, 0, 2)
+        round_wg(nc.scalar.copy, wg_late, 1, WG_SHARE, P, 0, 2)
+        wg_mx.append(quantise_wg(wg_late, 1, "wg_codes1", ((2, PACK), (0, 2))))
         v_codes.append(gather_v(1, "wg_early", CUTS))
 
         def first_stage(acc, weights, scales, a, lo, hi, start, stop):
@@ -232,8 +237,8 @@ def tile_list_auction_slot_scores_kernel(
         sigs = {t: fresh([P, S], F32, "sig%d" % t) for t in (SECOND, THIRD, LAST)}
         cut_sigs = [fresh([P, P], F32, "sig_a"), fresh([P, P], F32, "sig_b"), at([P, 2 * P], F32, "sig_c", first_sig_at + S)]
 
-        def sigmoid(acc, gates):
-            nc.scalar.activation(out=gates[:], in_=acc, func=ACT.Sigmoid)
+        def sigmoid(acc, gates, bias=0.0):
+            nc.scalar.activation(out=gates[:], in_=acc, func=ACT.Sigmoid, bias=bias)
 
         cut_bank = [bank(u) for u in range(3)]
         gate_cut = [cut_bank[u][:, 0 : hi - lo] for u, (lo, hi) in enumerate(CUTS)]
@@ -257,14 +262,13 @@ def tile_list_auction_slot_scores_kernel(
             sigmoid(gate[t], sigs[t])
         feat_pass(feat[SECOND], SECOND, 1)
         gate_pass(gate[LAST], LAST, 1)
-        sigmoid(gate[LAST], sigs[LAST])
+        sigmoid(gate[LAST], sigs[LAST], no_bias[:, 1:2])
         for t, k in ((LAST, 0), (THIRD, 6)):
             feat[t] = bank(k)[:]
             for a in range(PASSES):
                 feat_pass(feat[t], t, a)
 
-        warm_exp = keep.tile([P, 1], F32, name="warm_exp")
-        nc.scalar.activation(out=warm_exp[:], in_=sigs[LAST][:, 0:1], func=ACT.Exp)
+        nc.scalar.activation(out=no_bias[:, 1:2], in_=one[:], func=ACT.Exp)
 
         def weigh(h, acc, factor):
             nc.vector.tensor_tensor(h[:], acc, factor, ALU.mult)

@@ -26,9 +26,8 @@ TILES = S2 // P
 HALVES = T2 // BANK
 QUARTER = T2 // 4
 FIRST, SECOND, THIRD, LAST = 2, 0, 1, 3
-REST = 16
 WG_SHARE = 24
-CUTS = ((2 * P, 3 * P), (3 * P, S), (0, 2 * P))
+CUTS = ((0, P), (P, 2 * P), (2 * P, S))
 
 
 def tile_list_auction_slot_scores_kernel(
@@ -62,9 +61,9 @@ def tile_list_auction_slot_scores_kernel(
 
         rounded_at = 0
         first_page_at = rounded_at + 2 * PACK * T2
-        products_at = first_page_at + 4 * T2 + 4 * S
-        first_sig_at = products_at + 12 * S
-        page_at = {FIRST: first_page_at, THIRD: first_sig_at + 6 * S, LAST: first_sig_at + 6 * S + 4 * T2}
+        last_sig_at = first_page_at + 4 * T2
+        products_at = last_sig_at + 4 * S
+        page_at = {FIRST: first_page_at, LAST: products_at + 4 * S}
 
         idx = keep.tile([P, S // 16], U16, name="idx")
         idx2 = keep.tile([P, S2 // 16], U16, name="idx2")
@@ -101,11 +100,7 @@ def tile_list_auction_slot_scores_kernel(
             at([P, T2], F32, "page%d" % t, page_at[t]) if t in page_at else fresh([P, T2], F32, "page%d" % t)
             for t in range(PACK)
         ]
-        wgs_early = fresh([P, S // 2], F32, "wgs_early")
-        wgs_next = fresh([P, S + S // 2], F32, "wgs_next")
-        wgs_second = fresh([P, S], F32, "wgs_second")
-        wgs_last = fresh([P, S], F32, "wgs_last")
-        factors = {SECOND: wgs_second[:], LAST: wgs_last[:]}
+        factors = [fresh([P, S], F32, "wgs%d" % t) for t in range(PACK)]
         reserve_sb = [keep.tile([P, 4, PICKS], F32, name="reserve%d" % u) for u in range(2)]
         page_rows = page0.rearrange("(p t) c -> t p c", t=PACK)
         wgs_rows = wgs.rearrange("(p t) j -> p t j", t=PACK)
@@ -119,9 +114,9 @@ def tile_list_auction_slot_scores_kernel(
         def load_page(t):
             nc.sync.dma_start(out=page[t][:], in_=page_rows[t])
 
-        def load_wgs(tile, rows, quadrants):
-            for q in quadrants:
-                nc.sync.dma_start(out=tile[32 * q : 32 * (q + 1)], in_=rows)
+        def load_wgs(t):
+            for q in (0, 2, 1, 3):
+                nc.sync.dma_start(out=factors[t][32 * q : 32 * (q + 1)], in_=wgs_rows[:, t, :])
 
         nc.sync.dma_start(
             out=words(w4_raw[:]).rearrange("p (a n) -> p a n", a=PASSES), in_=words(w4_words).rearrange("a p n -> p a n")
@@ -159,13 +154,12 @@ def tile_list_auction_slot_scores_kernel(
         carry(1)
         load_words(tab[1], tab_words[1], 0, T)
         nc.sync.dma_start(idx3[:], offs3)
-        load_wgs(wgs_early, wgs_rows[:, FIRST, S // 2 : S], (0, 2, 1, 3))
-        load_page(FIRST)
-        load_wgs(wgs_next, wgs.rearrange("(p t) j -> p (t j)", t=PACK)[:, THIRD * S : FIRST * S + S // 2], (0, 2, 1, 3))
-        load_page(SECOND)
-        load_wgs(wgs_second, wgs_rows[:, SECOND, :], (0, 2, 1, 3))
+        for t in (FIRST, SECOND):
+            load_wgs(t)
+            load_page(t)
+        load_wgs(THIRD)
+        load_wgs(LAST)
         load_page(THIRD)
-        load_wgs(wgs_last, wgs_rows[:, LAST, :], (0, 2, 1, 3))
         load_words(tab2, tab2_words[0], 0, T3 - P)
         load_page(LAST)
         load_words(tab2, tab2_words[0], T3 - P, T3)
@@ -234,11 +228,12 @@ def tile_list_auction_slot_scores_kernel(
             c0 = a * H + P * t
             first_stage(acc, w4_codes[:, 2 * c0 : 2 * (c0 + P)].bitcast(FP4X4), w4_scale[:, c0 : c0 + P], a, lo, hi, start, stop)
 
-        sigs = {t: fresh([P, S], F32, "sig%d" % t) for t in (SECOND, THIRD, LAST)}
-        cut_sigs = [fresh([P, P], F32, "sig_a"), fresh([P, P], F32, "sig_b"), at([P, 2 * P], F32, "sig_c", first_sig_at + S)]
+        sig_at = {THIRD: rounded_at + PACK * T2 - 2 * S, LAST: last_sig_at}
+        sigs = [at([P, S], F32, "sig%d" % t, sig_at[t]) if t in sig_at else fresh([P, S], F32, "sig%d" % t) for t in range(PACK)]
+        gated = {t: fresh([P, S], F32, "gated%d" % t) for t in (FIRST, SECOND, THIRD)}
 
         def sigmoid(acc, gates, bias=0.0):
-            nc.scalar.activation(out=gates[:], in_=acc, func=ACT.Sigmoid, bias=bias)
+            nc.scalar.activation(out=gates, in_=acc, func=ACT.Sigmoid, bias=bias)
 
         cut_bank = [bank(u) for u in range(3)]
         gate_cut = [cut_bank[u][:, 0 : hi - lo] for u, (lo, hi) in enumerate(CUTS)]
@@ -256,26 +251,58 @@ def tile_list_auction_slot_scores_kernel(
         for u, (lo, hi) in enumerate(CUTS):
             gate_pass(gate_cut[u], FIRST, 1, lo, hi, start=False, stop=(u == 0))
             feat_pass(feat_cut[u], FIRST, 1, lo, hi, start=False, stop=True)
-            sigmoid(gate_cut[u], cut_sigs[u])
-        for t in (SECOND, THIRD):
-            gate_pass(gate[t], t, 1)
-            sigmoid(gate[t], sigs[t])
+            sigmoid(gate_cut[u], sigs[FIRST][:, lo:hi])
+        long_run = slice(*CUTS[2])
+        nc.gpsimd.tensor_tensor(gated[FIRST][:, long_run], sigs[FIRST][:, long_run], factors[FIRST][:, long_run], ALU.mult)
+
+        sums, whole = {}, {}
+
+        def bring(t):
+            sums[t] = fresh([P, S], F32, "sums%d" % t)
+            nc.scalar.copy(out=sums[t][:], in_=feat[t])
+
+        def weigh(t):
+            nc.gpsimd.tensor_tensor(gated[t][:], sigs[t][:], factors[t][:], ALU.mult)
+
+        def join(t):
+            whole[t] = fresh([P, S], F32, "whole%d" % t)
+            nc.gpsimd.tensor_tensor(whole[t][:], sums[t][:], gated[t][:], ALU.mult)
+
+        def put(values, t, lo=0, hi=S):
+            nc.vector.tensor_copy(page[t][:].indirect(entries(idx3, lo, hi)), values)
+
+        gate_pass(gate[SECOND], SECOND, 1)
+        sigmoid(gate[SECOND], sigs[SECOND][:])
         feat_pass(feat[SECOND], SECOND, 1)
+        bring(SECOND)
+        weigh(SECOND)
+        join(SECOND)
+        gate_pass(gate[THIRD], THIRD, 1)
+        sigmoid(gate[THIRD], sigs[THIRD][:])
         gate_pass(gate[LAST], LAST, 1)
-        sigmoid(gate[LAST], sigs[LAST], no_bias[:, 1:2])
-        for t, k in ((LAST, 0), (THIRD, 6)):
+        sigmoid(gate[LAST], sigs[LAST][:], no_bias[:, 1:2])
+
+        short = [at([P, P], F32, "short0", products_at), fresh([P, P], F32, "short1")]
+        for u in range(2):
+            run = slice(*CUTS[u])
+            nc.vector.tensor_tensor(gated[FIRST][:, run], feat_cut[u], factors[FIRST][:, run], ALU.mult)
+        for u in range(2):
+            run = slice(*CUTS[u])
+            nc.vector.tensor_tensor(short[u][:], gated[FIRST][:, run], sigs[FIRST][:, run], ALU.mult)
+        for t, k in ((THIRD, 0), (LAST, 6)):
             feat[t] = bank(k)[:]
             for a in range(PASSES):
                 feat_pass(feat[t], t, a)
-
+            bring(t)
         nc.scalar.activation(out=no_bias[:, 1:2], in_=one[:], func=ACT.Exp)
+        weigh(THIRD)
+        join(THIRD)
 
-        def weigh(h, acc, factor):
-            nc.vector.tensor_tensor(h[:], acc, factor, ALU.mult)
-            return h
-
-        def put(h, weights, t, lo=0, hi=S):
-            nc.vector.tensor_tensor(page[t][:].indirect(entries(idx3, lo, hi)), h[:], weights, ALU.mult)
+        put(short[0][:], FIRST, *CUTS[0])
+        whole[FIRST] = at([P, 2 * P], F32, "whole_long", products_at)
+        nc.vector.tensor_tensor(whole[FIRST][:], feat_cut[2], gated[FIRST][:, long_run], ALU.mult)
+        put(short[1][:], FIRST, *CUTS[1])
+        put(whole[FIRST][:], FIRST, *CUTS[2])
 
         rounded = [at([P, PACK * BANK], BF16, "rounded%d" % c, rounded_at + 2 * PACK * BANK * c) for c in range(HALVES)]
 
@@ -283,28 +310,18 @@ def tile_list_auction_slot_scores_kernel(
             start = PACK * (lo % BANK)
             copy(out=rounded[lo // BANK][:, start + t : start + PACK * (hi - lo) : PACK], in_=page[t][:, lo:hi])
 
-        h_a = at([P, P], F32, "h_a", products_at)
-        h_b = fresh([P, P], F32, "h_b")
-        for u, h in enumerate((h_a, h_b)):
-            nc.vector.tensor_tensor(h[:], feat_cut[u], wgs_early[:, u * P : (u + 1) * P], ALU.mult)
-        put(h_a, cut_sigs[0][:], FIRST, *CUTS[0])
-        h_c = weigh(at([P, 2 * P], F32, "h_c", products_at - 2 * S + 64), feat_cut[2], cut_sigs[2][:])
-        put(h_b, cut_sigs[1][:], FIRST, *CUTS[1])
-        hs = {SECOND: weigh(at([P, S], F32, "h_second", products_at + 64), feat[SECOND], sigs[SECOND][:])}
-        hs[LAST] = weigh(at([P, S], F32, "h_last", first_sig_at + 2 * S), feat[LAST], sigs[LAST][:])
-        gated = at([P, S], F32, "gated", first_sig_at - 2 * S)
-        nc.gpsimd.tensor_tensor(gated[:], sigs[THIRD][:], wgs_next[:, 0:S], ALU.mult)
-        factors[THIRD] = gated[:]
-        hs[THIRD] = fresh([P, S], F32, "feat_third")
-        nc.scalar.copy(out=hs[THIRD][:], in_=feat[THIRD])
-        put(h_c, wgs_next[:, S:], FIRST, *CUTS[2])
-        for c in range(HALVES):
-            round_page(nc.scalar.copy, FIRST, BANK * c, BANK * (c + 1))
+        def round_on_gpsimd(out, in_):
+            nc.gpsimd.tensor_scalar(out, in_, 1.0, 0.0, ALU.mult, ALU.add)
+
+        round_page(round_on_gpsimd, FIRST, 0, BANK)
+        round_page(nc.scalar.copy, FIRST, BANK, T2)
+        gated[LAST] = at([P, S], F32, "gated_last", page_at[FIRST])
+        weigh(LAST)
         for t in (SECOND, THIRD):
-            put(hs[t], factors[t], t)
+            put(whole[t][:], t)
             for c in range(HALVES):
-                round_page(nc.scalar.copy, t, BANK * c, min(BANK * (c + 1), T2 - (REST if t == THIRD else 0)))
-        put(hs[LAST], factors[LAST], LAST)
+                round_page(nc.scalar.copy, t, BANK * c, BANK * (c + 1))
+        nc.vector.tensor_tensor(page[LAST][:].indirect(idx3[:]), sums[LAST][:], gated[LAST][:], ALU.mult)
 
         def round_last(copy, quarter):
             round_page(copy, LAST, QUARTER * quarter, QUARTER * (quarter + 1))
@@ -327,9 +344,8 @@ def tile_list_auction_slot_scores_kernel(
             )
 
         round_last(nc.scalar.copy, 0)
-        round_page(nc.scalar.copy, THIRD, T2 - REST, T2)
         round_last(nc.scalar.copy, 2)
-        gather_v2(0, 1, page_at[FIRST])
+        gather_v2(0, 1, last_sig_at)
         round_last(nc.vector.tensor_copy, 1)
         round_last(nc.vector.tensor_copy, 3)
         for quarter in (1, 0, 3, 2):

@@ -27,6 +27,7 @@ HALVES = T2 // BANK
 QUARTER = T2 // 4
 FIRST, SECOND, THIRD, LAST = 2, 0, 1, 3
 WG_SHARE = 24
+GPSIMD_COLUMNS = 320
 CUTS = ((0, P), (P, 2 * P), (2 * P, S))
 
 
@@ -313,7 +314,8 @@ def tile_list_auction_slot_scores_kernel(
         def round_on_gpsimd(out, in_):
             nc.gpsimd.tensor_scalar(out, in_, 1.0, 0.0, ALU.mult, ALU.add)
 
-        round_page(round_on_gpsimd, FIRST, 0, BANK)
+        round_page(round_on_gpsimd, FIRST, 0, GPSIMD_COLUMNS)
+        round_page(nc.scalar.copy, FIRST, GPSIMD_COLUMNS, BANK)
         round_page(nc.scalar.copy, FIRST, BANK, T2)
         gated[LAST] = at([P, S], F32, "gated_last", page_at[FIRST])
         weigh(LAST)

from contextlib import ExitStack

import concourse.mybir as mybir
from concourse.masks import make_identity

K, H, T, S, T2, T3, S2, PICKS = 1024, 512, 2048, 512, 1024, 2048, 1024, 512
FLOPS = 2 * (2 * K * H * S + H * S2 * T2)

F32 = mybir.dt.float32
BF16 = mybir.dt.bfloat16
I32 = mybir.dt.int32
U32 = mybir.dt.uint32
U16 = mybir.dt.uint16
U8 = mybir.dt.uint8
FP8X4 = mybir.dt.float8_e4m3fn_x4
FP4X4 = mybir.dt.float4_e2m1fn_x4
ACT = mybir.ActivationFunctionType
ALU = mybir.AluOpType

P = 128
PACK = 4
PASSES = K // (P * PACK)
BANK = 512
BANKS = 8
TILES = S2 // P
HALVES = T2 // BANK
QUARTER = T2 // 4
FIRST, SECOND, THIRD, LAST = 2, 0, 1, 3
WG_SHARE = 24
GPSIMD_COLUMNS = 320
CUTS = ((0, P), (P, 2 * P), (2 * P, S))


def tile_list_auction_slot_scores_kernel(
    tc, tab_words, tab_scales, offs, w4_words, w4_scales, wg, page0, wgs, offs3,
    tab2_words, tab2_scales, offs2, offs4, bid, reserve, out,
):
    nc = tc.nc
    with ExitStack() as ctx:
        keep = ctx.enter_context(tc.tile_pool(name="keep", bufs=1))
        ring = ctx.enter_context(tc.tile_pool(name="ring", bufs=TILES + 1))
        placed = ctx.enter_context(tc.tile_pool(name="placed", bufs=1))
        psum = ctx.enter_context(tc.psum_pool(name="psum", bufs=1))

        def fresh(shape, dtype, name):
            return keep.tile(shape, dtype, name=name, align_bytes=64)

        def slot(shape, dtype, name, tag):
            return keep.tile(shape, dtype, name=name, tag=tag, align_bytes=64)

        def at(shape, dtype, name, offset):
            return placed.tile(shape, dtype, name=name, align_bytes=64, offset=offset)

        def bank(k):
            return psum.tile([P, BANK], F32, name="bank%d" % k, tag="bank%d" % k)

        def words(ap):
            return ap.bitcast(I32)

        def entries(offsets, lo, hi):
            return offsets[:, lo // 16 : hi // 16]

        rounded_at = 0
        first_page_at = rounded_at + 2 * PACK * T2
        last_sig_at = first_page_at + 4 * T2
        products_at = last_sig_at + 4 * S
        page_at = {FIRST: first_page_at, LAST: products_at + 4 * S}

        idx = keep.tile([P, S // 16], U16, name="idx")
        idx2 = keep.tile([P, S2 // 16], U16, name="idx2")
        idx3 = keep.tile([P, S // 16], U16, name="idx3")
        idx4 = keep.tile([P, PICKS // 16], U16, name="idx4")

        tab_rows = slot([P, T], U8, "tab_rows", "tab_rows")
        tab2_rows = slot([P, T3], U8, "tab2_rows", "tab2_rows")
        w4_rows = slot([P, PASSES * H], U8, "w4_rows", "w4_rows")
        v_scale = [fresh([P, S], U8, "v_scale%d" % a) for a in range(PASSES)]
        one = keep.tile([P, 1], F32, name="one")
        no_bias = keep.tile([P, 2], F32, name="no_bias")
        bid_rows = keep.tile([P, P], F32, name="bid_rows")
        identity = keep.tile([P, P], F32, name="identity")
        v2_scale = fresh([P, S2], U8, "v2_scale")
        nc.gpsimd.memset(words(w4_rows[:]), 0)
        nc.gpsimd.memset(words(tab_rows[64:P, :]), 0)
        nc.vector.memset(words(tab_rows[32:64, :]), 0)
        nc.gpsimd.memset(one[:], 1.0)
        nc.vector.memset(words(tab2_rows[:]), 0)
        nc.gpsimd.memset(bid_rows[:], 0.0)
        nc.gpsimd.memset(no_bias[:], 0.0)
        make_identity(nc, identity[:])
        nc.gpsimd.memset(words(v_scale[1][:]), 0)
        nc.vector.memset(words(v2_scale[:]), 0)
        warm_ln = keep.tile([P, 1], F32, name="warm_ln")
        nc.scalar.activation(out=warm_ln[:], in_=one[:], func=ACT.Ln)

        w4_raw = fresh([P, PASSES * 2 * H], U8, "w4_raw")
        wg_raw = [fresh([P, PACK, H], F32, "wg_raw%d" % a) for a in range(PASSES)]
        tab = [slot([P, T], U32, "tab%d" % a, "tab%d" % a) for a in range(PASSES)]
        tab2 = slot([P, T3], U32, "tab2", "tab2")
        page = [
            at([P, T2], F32, "page%d" % t, page_at[t]) if t in page_at else fresh([P, T2], F32, "page%d" % t)
            for t in range(PACK)
        ]
        factors = [fresh([P, S], F32, "wgs%d" % t) for t in range(PACK)]
        reserve_sb = [keep.tile([P, 4, PICKS], F32, name="reserve%d" % u) for u in range(2)]
        page_rows = page0.rearrange("(p t) c -> t p c", t=PACK)
        wgs_rows = wgs.rearrange("(p t) j -> p t j", t=PACK)

        def load_wg(a):
            nc.sync.dma_start(out=wg_raw[a][:], in_=wg[512 * a : 512 * (a + 1), :].rearrange("(p j) c -> p j c", j=PACK))

        def load_words(tile, table, lo, hi):
            nc.sync.dma_start(out=words(tile[:, lo:hi]), in_=words(table.rearrange("p t i -> p (t i)"))[:, lo:hi])

        def load_page(t):
            nc.sync.dma_start(out=page[t][:], in_=page_rows[t])

        def load_wgs(t):
            for q in (0, 2, 1, 3):
                nc.sync.dma_start(out=factors[t][32 * q : 32 * (q + 1)], in_=wgs_rows[:, t, :])

        nc.sync.dma_start(
            out=words(w4_raw[:]).rearrange("p (a n) -> p a n", a=PASSES), in_=words(w4_words).rearrange("a p n -> p a n")
        )
        nc.sync.dma_start(idx[:], offs)
        nc.sync.dma_start(out=words(tab_rows[0:32, :]), in_=words(tab_scales).rearrange("a q n -> (a q) n"))
        for r in range(4):
            nc.sync.dma_start(out=words(w4_rows[r:P:32, :]), in_=words(w4_scales).rearrange("a (q r) n -> r q a n", r=4)[r])
        v_rows = fresh([P, S], U8, "v_rows")
        nc.vector.tensor_copy(v_rows[:], tab_rows[:].indirect(idx[:]))
        w4_codes = fresh([P, PASSES * 2 * H], U8, "w4_codes")
        nc.vector.tensor_copy(
            out=w4_codes[:].bitcast(U16).rearrange("p (a t m i) -> p a m t i", a=PASSES, t=PACK, i=8),
            in_=w4_raw[:].bitcast(U16).rearrange("p (a m i t) -> p a m t i", a=PASSES, t=PACK, i=8),
        )
        nc.vector.tensor_copy(words(v_scale[0][:]), words(v_rows[:]))
        w4_scale = fresh([P, PASSES * H], U8, "w4_scale")
        nc.vector.tensor_copy(
            out=w4_scale[:].rearrange("p (a t m i) -> p a m t i", a=PASSES, t=PACK, i=16),
            in_=w4_rows[:].rearrange("p (a m i t) -> p a m t i", a=PASSES, t=PACK, i=16),
        )

        def carry(a):
            for q in range(1 - a, 4):
                src = 16 * a + 4 * q
                nc.sync.dma_start(out=words(v_scale[a][32 * q : 32 * q + 4, :]), in_=words(v_rows[src : src + 4, :]))

        load_wg(0)
        nc.sync.dma_start(idx2[:], offs2)
        nc.sync.dma_start(out=words(tab2_rows[0:P:8, :]), in_=words(tab2_scales[0]))
        load_words(tab[0], tab_words[0], 0, T)
        nc.sync.dma_start(out=bid_rows[0:TILES, :], in_=bid.rearrange("(i p) -> i p", p=P))
        carry(0)
        load_wg(1)
        carry(1)
        load_words(tab[1], tab_words[1], 0, T)
        nc.sync.dma_start(idx3[:], offs3)
        for t in (FIRST, SECOND):
            load_wgs(t)
            load_page(t)
        load_wgs(THIRD)
        load_wgs(LAST)
        load_page(THIRD)
        load_words(tab2, tab2_words[0], 0, T3 - P)
        load_page(LAST)
        load_words(tab2, tab2_words[0], T3 - P, T3)
        nc.sync.dma_start(idx4[:], offs4)
        for u in range(2):
            nc.sync.dma_start(
                out=reserve_sb[u][:], in_=reserve[512 * u : 512 * (u + 1), :].rearrange("(i p) m -> p i m", p=P)
            )

        v2_rows = slot([P, S2], U8, "v2_rows", "tab_rows")
        nc.vector.tensor_copy(v2_rows[:], tab2_rows[:].indirect(idx2[:]))
        for r in range(4):
            nc.sync.dma_start(out=words(v2_scale[r:P:32, :]), in_=words(v2_rows[8 * r : P : 32, :]))

        def round_wg(copy, rounded, a, m0, m1, t0=0, t1=PACK):
            copy(
                out=rounded[:].rearrange("p (t m j) -> p m t j", m=P, j=PACK)[:, m0:m1, t0:t1],
                in_=wg_raw[a][:].rearrange("p j (m t) -> p m t j", t=PACK)[:, m0:m1, t0:t1],
            )

        def quantise_wg(rounded, a, tag, runs):
            codes = slot([P, H], U32, "wg_codes%d" % a, tag)
            scale = fresh([P, H], U8, "wg_scale%d" % a)
            for t0, t1 in runs:
                cols = slice(P * t0, P * t1)
                nc.vector.quantize_mx(out=codes[:, cols].bitcast(FP8X4), scales=scale[:, cols], in_=rounded[:, H * t0 : H * t1])
            return codes, scale

        def gather_v(a, tag, cuts):
            codes = slot([P, S], U32, "v_codes%d" % a, tag)
            for lo, hi in cuts:
                nc.vector.tensor_copy(codes[:, lo:hi], tab[a][:].indirect(entries(idx, lo, hi)))
            return codes

        wg_early = slot([P, PACK * H], BF16, "wg_early", "wg_early")
        round_wg(nc.scalar.copy, wg_early, 0, 0, P)
        v_codes = [gather_v(0, "tab2_rows", ((0, S),))]
        wg_mx = [quantise_wg(wg_early, 0, "tab0", ((0, PACK),))]

        bid_turned = bank(BANKS - 1)
        nc.tensor.transpose(bid_turned[:, 0:P], bid_rows[:], identity[:])
        ln_bid = fresh([P, TILES], F32, "ln_bid")
        nc.scalar.activation(out=ln_bid[:], in_=bid_turned[:, 0:TILES], func=ACT.Ln, bias=no_bias[:, 0:1])
        nc.scalar.activation(out=no_bias[:, 0:1], in_=one[:], func=ACT.Sigmoid)

        wg_late = slot([P, PACK * H], BF16, "wg_late", "wg_early")
        round_wg(nc.vector.tensor_copy, wg_late, 1, 0, P, 2, PACK)
        round_wg(nc.vector.tensor_copy, wg_late, 1, 0, WG_SHARE, 0, 2)
        round_wg(nc.scalar.copy, wg_late, 1, WG_SHARE, P, 0, 2)
        wg_mx.append(quantise_wg(wg_late, 1, "wg_codes1", ((2, PACK), (0, 2))))
        v_codes.append(gather_v(1, "wg_early", CUTS))

        def first_stage(acc, weights, scales, a, lo, hi, start, stop):
            nc.tensor.matmul_mx(
                out=acc, lhsT=weights, lhsT_scale=scales,
                rhs=v_codes[a][:, lo:hi].bitcast(FP8X4), rhs_scale=v_scale[a][:, lo:hi],
                start=(a == 0) if start is None else start, stop=(a == PASSES - 1) if stop is None else stop,
            )

        def gate_pass(acc, t, a, lo=0, hi=S, start=None, stop=None):
            codes, scale = wg_mx[a]
            cols = slice(P * t, P * (t + 1))
            first_stage(acc, codes[:, cols].bitcast(FP8X4), scale[:, cols], a, lo, hi, start, stop)

        def feat_pass(acc, t, a, lo=0, hi=S, start=None, stop=None):
            c0 = a * H + P * t
            first_stage(acc, w4_codes[:, 2 * c0 : 2 * (c0 + P)].bitcast(FP4X4), w4_scale[:, c0 : c0 + P], a, lo, hi, start, stop)

        sig_at = {THIRD: rounded_at + PACK * T2 - 2 * S, LAST: last_sig_at}
        sigs = [at([P, S], F32, "sig%d" % t, sig_at[t]) if t in sig_at else fresh([P, S], F32, "sig%d" % t) for t in range(PACK)]
        gated = {t: fresh([P, S], F32, "gated%d" % t) for t in (FIRST, SECOND, THIRD)}

        def sigmoid(acc, gates, bias=0.0):
            nc.scalar.activation(out=gates, in_=acc, func=ACT.Sigmoid, bias=bias)

        cut_bank = [bank(u) for u in range(3)]
        gate_cut = [cut_bank[u][:, 0 : hi - lo] for u, (lo, hi) in enumerate(CUTS)]
        feat_cut = [cut_bank[u][:, BANK // 2 : BANK // 2 + hi - lo] for u, (lo, hi) in enumerate(CUTS)]
        feat_cut[0] = bank(6)[:, 0:P]
        gate = {SECOND: bank(3)[:], LAST: bank(5)[:], THIRD: bank(7)[:]}
        feat = {SECOND: bank(4)[:]}
        for u, (lo, hi) in enumerate(CUTS):
            feat_pass(feat_cut[u], FIRST, 0, lo, hi, start=True, stop=False)
        feat_pass(feat[SECOND], SECOND, 0)
        for u, (lo, hi) in enumerate(CUTS):
            gate_pass(gate_cut[u], FIRST, 0, lo, hi, start=(u == 0), stop=False)
        for t in (SECOND, THIRD, LAST):
            gate_pass(gate[t], t, 0)
        for u, (lo, hi) in enumerate(CUTS):
            gate_pass(gate_cut[u], FIRST, 1, lo, hi, start=False, stop=(u == 0))
            feat_pass(feat_cut[u], FIRST, 1, lo, hi, start=False, stop=True)
            sigmoid(gate_cut[u], sigs[FIRST][:, lo:hi])
        long_run = slice(*CUTS[2])
        nc.gpsimd.tensor_tensor(gated[FIRST][:, long_run], sigs[FIRST][:, long_run], factors[FIRST][:, long_run], ALU.mult)

        sums, whole = {}, {}

        def bring(t):
            sums[t] = fresh([P, S], F32, "sums%d" % t)
            nc.scalar.copy(out=sums[t][:], in_=feat[t])

        def weigh(t):
            nc.gpsimd.tensor_tensor(gated[t][:], sigs[t][:], factors[t][:], ALU.mult)

        def join(t):
            whole[t] = fresh([P, S], F32, "whole%d" % t)
            nc.gpsimd.tensor_tensor(whole[t][:], sums[t][:], gated[t][:], ALU.mult)

        def put(values, t, lo=0, hi=S):
            nc.vector.tensor_copy(page[t][:].indirect(entries(idx3, lo, hi)), values)

        gate_pass(gate[SECOND], SECOND, 1)
        sigmoid(gate[SECOND], sigs[SECOND][:])
        feat_pass(feat[SECOND], SECOND, 1)
        bring(SECOND)
        weigh(SECOND)
        join(SECOND)
        gate_pass(gate[THIRD], THIRD, 1)
        sigmoid(gate[THIRD], sigs[THIRD][:])
        gate_pass(gate[LAST], LAST, 1)
        sigmoid(gate[LAST], sigs[LAST][:], no_bias[:, 1:2])

        short = [at([P, P], F32, "short0", products_at), fresh([P, P], F32, "short1")]
        for u in range(2):
            run = slice(*CUTS[u])
            nc.vector.tensor_tensor(gated[FIRST][:, run], feat_cut[u], factors[FIRST][:, run], ALU.mult)
        for u in range(2):
            run = slice(*CUTS[u])
            nc.vector.tensor_tensor(short[u][:], gated[FIRST][:, run], sigs[FIRST][:, run], ALU.mult)
        for t, k in ((THIRD, 0), (LAST, 6)):
            feat[t] = bank(k)[:]
            for a in range(PASSES):
                feat_pass(feat[t], t, a)
            bring(t)
        nc.scalar.activation(out=no_bias[:, 1:2], in_=one[:], func=ACT.Exp)
        weigh(THIRD)
        join(THIRD)

        put(short[0][:], FIRST, *CUTS[0])
        whole[FIRST] = at([P, 2 * P], F32, "whole_long", products_at)
        nc.vector.tensor_tensor(whole[FIRST][:], feat_cut[2], gated[FIRST][:, long_run], ALU.mult)
        put(short[1][:], FIRST, *CUTS[1])
        put(whole[FIRST][:], FIRST, *CUTS[2])

        rounded = [at([P, PACK * BANK], BF16, "rounded%d" % c, rounded_at + 2 * PACK * BANK * c) for c in range(HALVES)]

        def round_page(copy, t, lo, hi):
            start = PACK * (lo % BANK)
            copy(out=rounded[lo // BANK][:, start + t : start + PACK * (hi - lo) : PACK], in_=page[t][:, lo:hi])

        def round_on_gpsimd(out, in_):
            nc.gpsimd.tensor_scalar(out, in_, 1.0, 0.0, ALU.mult, ALU.add)

        round_page(round_on_gpsimd, FIRST, 0, GPSIMD_COLUMNS)
        round_page(nc.scalar.copy, FIRST, GPSIMD_COLUMNS, BANK)
        round_page(nc.scalar.copy, FIRST, BANK, T2)
        gated[LAST] = at([P, S], F32, "gated_last", page_at[FIRST])
        weigh(LAST)
        for t in (SECOND, THIRD):
            put(whole[t][:], t)
            for c in range(HALVES):
                round_page(nc.scalar.copy, t, BANK * c, BANK * (c + 1))
        nc.vector.tensor_tensor(page[LAST][:].indirect(idx3[:]), sums[LAST][:], gated[LAST][:], ALU.mult)

        def round_last(copy, quarter):
            round_page(copy, LAST, QUARTER * quarter, QUARTER * (quarter + 1))

        page_codes = [fresh([P, BANK], U32, "page_codes%d" % c) for c in range(HALVES)]
        page_scale = [fresh([P, BANK], U8, "page_scale%d" % c) for c in range(HALVES)]
        v2_codes = {}

        def gather_v2(i0, i1, offset):
            codes = at([P, (i1 - i0) * P], U32, "v2_codes%d" % i0, offset)
            nc.vector.tensor_copy(codes[:], tab2[:].indirect(entries(idx2, i0 * P, i1 * P)))
            for i in range(i0, i1):
                v2_codes[i] = codes[:, (i - i0) * P : (i - i0 + 1) * P]

        def quantise_page(quarter):
            c, lo = divmod(QUARTER * quarter, BANK)
            nc.vector.quantize_mx(
                out=page_codes[c][:, lo : lo + QUARTER].bitcast(FP8X4), scales=page_scale[c][:, lo : lo + QUARTER],
                in_=rounded[c][:, PACK * lo : PACK * (lo + QUARTER)],
            )

        round_last(nc.scalar.copy, 0)
        round_last(nc.scalar.copy, 2)
        gather_v2(0, 1, last_sig_at)
        round_last(nc.vector.tensor_copy, 1)
        round_last(nc.vector.tensor_copy, 3)
        for quarter in (1, 0, 3, 2):
            quantise_page(quarter)
        gather_v2(1, 2, page_at[LAST])
        gather_v2(2, 4, page_at[LAST] + T2)
        gather_v2(4, 6, page_at[LAST] + 2 * T2)

        scores, picked = {}, {}

        def parts(i):
            return ((0, PICKS // 2), (PICKS // 2, PICKS)) if i == TILES - 1 else ((0, PICKS),)

        def score(i, c):
            if c == 0:
                scores[i] = slot([P, T2], F32, "e%d" % i, "e%d" % (i % 4))
            acc = bank(4 * c + i % 4)
            for lo, hi in {(0, 0): ((QUARTER, BANK), (0, QUARTER)), (0, 1): ((QUARTER, BANK), (0, QUARTER))}.get((i, c), ((0, BANK),)):
                nc.tensor.matmul_mx(
                    out=acc[:, lo:hi],
                    lhsT=v2_codes[i].bitcast(FP8X4), lhsT_scale=v2_scale[:, i * P : (i + 1) * P],
                    rhs=page_codes[c][:, lo:hi].bitcast(FP8X4), rhs_scale=page_scale[c][:, lo:hi],
                    start=True, stop=True,
                )
            split = {(4, 1): 0, (6, 1): 0}.get((i, c), BANK)
            for empty, lo, hi in ((nc.scalar.copy, 0, split), (nc.vector.tensor_copy, split, BANK)):
                if lo < hi:
                    empty(out=scores[i][:, c * BANK + lo : c * BANK + hi], in_=acc[:, lo:hi])

        def pick(i):
            picked[i] = []
            for lo, hi in parts(i):
                x = at([P, PICKS], F32, "x_first", rounded_at) if i == 0 else ring.tile([P, hi - lo], F32, name="x")
                nc.vector.tensor_copy(x[:], scores[i][:].indirect(entries(idx4, lo, hi)))
                picked[i].append(x)

        def finish(i):
            engine = nc.vector if i >= TILES - 2 else nc.gpsimd
            for x, (lo, hi) in zip(picked[i], parts(i)):
                ex = ring.tile([P, hi - lo], F32, name="ex")
                nc.scalar.activation(out=ex[:], in_=x[:], func=ACT.Exp, bias=ln_bid[:, i : i + 1])
                if i == TILES - 2:
                    res = slot([P, hi - lo], F32, "res_late", "e3")
                else:
                    res = ring.tile([P, hi - lo], F32, name="res")
                width = PICKS // 2 if i >= TILES - 2 else PICKS
                for n in range(0, hi - lo, width):
                    cols = slice(lo + n, lo + n + width)
                    engine.tensor_tensor(res[:, n : n + width], ex[:, n : n + width], reserve_sb[i // 4][:, i % 4, cols], ALU.subtract)
                    nc.sync.dma_start(out=out[i * P : (i + 1) * P, cols], in_=res[:, n : n + width])

        for i in range(3):
            for c in range(HALVES):
                score(i, c)
        pick(0)
        for i in range(TILES):
            if i + 1 < TILES:
                pick(i + 1)
            finish(i)
            if i == 0:
                gather_v2(6, TILES, rounded_at)
            if i + 3 < TILES:
                for c in range(HALVES):
                    score(i + 3, c)
